import numpy as np
import ml_dtypes


def mxq(x, axis, fmt="e4m3"):
    dtype, down = {"e4m3": (ml_dtypes.float8_e4m3fn, 7), "e5m2": (ml_dtypes.float8_e5m2, 14)}[fmt]
    v = np.moveaxis(np.asarray(x, np.float32).astype(ml_dtypes.bfloat16).astype(np.float64), axis, -1)
    blocks = v.reshape(v.shape[:-1] + (-1, 32))
    amax = np.abs(blocks).max(-1, keepdims=True)
    byte = np.maximum(np.where(amax > 0, np.frexp(amax)[1] - 1 + 127, 0) - down, 1)
    scale = np.exp2(byte - 127.0)
    codes = (blocks / scale).astype(np.float32).astype(dtype).astype(np.float64)
    return np.moveaxis((codes * scale).reshape(v.shape), -1, axis)


WIDE = False


def mx_kscale(k):
    if not WIDE:
        return np.ones(k)
    levels = np.array([10, -10, 5, -5, 0])
    if k % 512:
        return np.exp2(np.random.permutation(np.resize(levels, k // 32))).repeat(32)
    a = np.empty((k // 512, 16))
    for p in range(k // 512):
        a[p, :8] = np.random.permutation(np.resize(levels, 8))
        for g in range(8):
            far = levels[np.abs(levels - a[p, g]) >= 10]
            a[p, g + 8] = far[np.random.randint(len(far))]
    return np.exp2(a.ravel()).repeat(32)


def f64(x):
    return np.asarray(x).astype(np.float64)


def striped(idx):
    return np.tile(idx.reshape(-1, 16).T, (8, 1)).astype(np.uint16)


def unstriped(offs):
    return offs[:16].T.reshape(-1).astype(np.int64)


E2M1 = np.array([0.0, 0.5, 1.0, 1.5, 2.0, 3.0, 4.0, 6.0, -0.0, -0.5, -1.0, -1.5, -2.0, -3.0, -4.0, -6.0])


def pack_weight(w, fmt):
    k, n = w.shape
    w = f64(np.asarray(w, np.float32).astype(ml_dtypes.bfloat16)).reshape(k // 32, 32, n)
    amax = np.abs(w).max(1)
    if fmt == "e4m3":
        byte = np.frexp(amax)[1] - 1 + 127 - 7
    else:
        mant, ex = np.frexp(amax / 6.0)
        byte = np.where(mant > 0.5, ex, ex - 1) + 127
    byte = np.clip(np.where(amax > 0, byte, 1), 1, 254)
    scaled = (w * np.exp2(127.0 - byte)[:, None, :]).reshape(k, n).astype(np.float32)
    by_word = np.ascontiguousarray(scaled.reshape(k // 512, 128, 4, n).transpose(0, 1, 3, 2))
    if fmt == "e4m3":
        words = by_word.astype(ml_dtypes.float8_e4m3fn).view(np.uint8)
    else:
        c = by_word.astype(ml_dtypes.float4_e2m1fn).view(np.uint8) & 0xF
        words = (c[..., 0::2] | (c[..., 1::2] << 4)).reshape(k // 512, 128, 2 * n)
    return np.ascontiguousarray(words), np.ascontiguousarray(byte.astype(np.uint8).reshape(k // 512, 16, n))


def unpack_weight(words, scales, fmt):
    g, _, n = scales.shape
    words = np.ascontiguousarray(words).reshape(g, 128, n, -1)
    if fmt == "e4m3":
        vals = words.view(ml_dtypes.float8_e4m3fn).astype(np.float64)
    else:
        nib = np.empty((g, 128, n, 4), np.uint8)
        nib[..., 0::2] = words & 0xF
        nib[..., 1::2] = words >> 4
        vals = E2M1[nib]
    vals = vals * np.repeat(np.exp2(scales.astype(np.float64) - 127.0), 8, axis=1)[..., None]
    return vals.transpose(0, 1, 3, 2).reshape(g * 512, n)


def gelu(v):
    return 0.5 * v * (1.0 + np.tanh(np.sqrt(2.0 / np.pi) * (v + 0.044715 * v**3)))


K, H, N, T, S, T2 = 512, 1024, 512, 2048, 1024, 2048


def setup_inputs():
    n = np.random.standard_normal
    s = mx_kscale(K)[:, None]
    u = mx_kscale(H)[:, None]
    tab_words, tab_scales = pack_weight(n((K, T)) * s, "e4m3")
    w4_words, w4_scales = pack_weight(n((K, H)) / np.sqrt(K) / s, "e2m1")
    w8_words, w8_scales = pack_weight(n((H, N)) / np.sqrt(H) / u, "e4m3")
    return {
        "tab_words": tab_words, "tab_scales": tab_scales,
        "offs": striped(np.random.permutation(T)[:S]),
        "offs2": striped(np.random.permutation(T2)[:S]),
        "offs3": striped(np.random.permutation(T2)[:S]),
        "w1": (n((K, H)) / np.sqrt(K) / s).astype(np.float32),
        "w4_words": w4_words, "w4_scales": w4_scales,
        "wg1": np.exp(0.3 * n((128, S))).astype(np.float32),
        "wg2": np.exp(0.3 * n((128, S))).astype(np.float32),
        "plan": (n((H, T2)) * u).astype(np.float32),
        "w8_words": w8_words, "w8_scales": w8_scales,
    }


def reference(tab_words, tab_scales, offs, offs2, offs3, w1, w4_words, w4_scales, wg1, wg2, plan, w8_words, w8_scales):
    v = unpack_weight(tab_words, tab_scales, "e4m3")[:, unstriped(offs)]
    h1 = mxq(f64(w1), 0, "e4m3").T @ v
    h2 = unpack_weight(w4_words, w4_scales, "e2m1").T @ v
    pageA = np.zeros((H, T2))
    pageA[:, unstriped(offs2)] = np.tile(f64(wg1), (H // 128, 1)) * h1
    pageB = np.zeros((H, T2))
    pageB[:, unstriped(offs3)] = np.tile(f64(wg2), (H // 128, 1)) * h2
    z = f64(plan) / (1.0 + np.square(pageA - pageB))
    return unpack_weight(w8_words, w8_scales, "e4m3").T @ mxq(z, 0, "e4m3")

@@ -1,0 +1,273 @@
+from contextlib import ExitStack
+
+import concourse.mybir as mybir
+from concourse.masks import make_identity
+
+K, H, N, T, S, T2 = 512, 1024, 512, 2048, 1024, 2048
+FLOPS = 2 * (2 * K * H * S + H * N * T2)
+
+F32 = mybir.dt.float32
+BF16 = mybir.dt.bfloat16
+I32 = mybir.dt.int32
+U32 = mybir.dt.uint32
+U16 = mybir.dt.uint16
+U8 = mybir.dt.uint8
+FP8X4 = mybir.dt.float8_e4m3fn_x4
+FP4X4 = mybir.dt.float4_e2m1fn_x4
+ACT = mybir.ActivationFunctionType
+MULT = mybir.AluOpType.mult
+ADD = mybir.AluOpType.add
+
+P = 128
+BANK = 512
+SLICES = H // P
+CHUNKS = T2 // BANK
+BLOCKS = BANK // P
+W1_COLS = 256
+ROOT = 75.0 / 64.0
+
+
+def tile_list_trap_bench_release_kernel(
+    tc, tab_words, tab_scales, offs, offs2, offs3, w1, w4_words, w4_scales, wg1, wg2, plan, w8_words, w8_scales, out
+):
+    nc = tc.nc
+    with ExitStack() as ctx:
+        keep = ctx.enter_context(tc.tile_pool(name="keep", bufs=1))
+        ring = ctx.enter_context(tc.tile_pool(name="ring", bufs=2))
+        plans = ctx.enter_context(tc.tile_pool(name="plans", bufs=3))
+        stores = ctx.enter_context(tc.tile_pool(name="stores", bufs=8))
+        psum = ctx.enter_context(tc.psum_pool(name="psum", bufs=1))
+
+        banks = [psum.tile([P, BANK], F32, name=f"bank{b}") for b in range(8)]
+
+        list_tab = keep.tile([P, S // 16], U16, name="list_tab")
+        list_a = keep.tile([P, S // 16], U16, name="list_a")
+        list_b = keep.tile([P, S // 16], U16, name="list_b")
+        tab_w = keep.tile([P, T], I32, name="tab_w", align_bytes=64)
+        tab_s = keep.tile([P, T], U8, name="tab_s", align_bytes=64)
+        v_w = keep.tile([P, S], U32, name="v_w", align_bytes=64)
+        v_s = keep.tile([P, S], U8, name="v_s", align_bytes=64)
+        w1_w = keep.tile([P, H], U32, name="w1_w", align_bytes=64)
+        w1_s = keep.tile([P, H], U8, name="w1_s", align_bytes=64)
+        w4_w = keep.tile([P, 2 * H], U8, name="w4_w", align_bytes=64)
+        w4_s = keep.tile([P, H], U8, name="w4_s", align_bytes=64)
+        w8_w = keep.tile([P, 2, N], I32, name="w8_w", align_bytes=64)
+        w8_s = keep.tile([P, 2, N], U8, name="w8_s", align_bytes=64)
+        gain_a = keep.tile([P, S], F32, name="gain_a")
+        gain_b = keep.tile([P, S], F32, name="gain_b")
+        ident = keep.tile([P, P], F32, name="ident")
+        page_a = [keep.tile([P, T2], F32, name=f"page_a{i}") for i in range(2)]
+        page_b = [keep.tile([P, T2], F32, name=f"page_b{i}") for i in range(2)]
+        work = [keep.tile([P, T2], F32, name=f"work{i}") for i in range(2)]
+        z_t = [[keep.tile([P, 2, BLOCKS, 2 * P], BF16, name=f"z_t{a}{c}") for c in range(CHUNKS)] for a in range(2)]
+        z_w = [[keep.tile([P, BANK], U32, name=f"z_w{a}{c}", align_bytes=64) for c in range(CHUNKS)] for a in range(2)]
+        z_s = [[keep.tile([P, BANK], U8, name=f"z_s{a}{c}", align_bytes=64) for c in range(CHUNKS)] for a in range(2)]
+
+        nc.gpsimd.memset(tab_s[:].bitcast(I32), 0)
+        nc.gpsimd.memset(w4_s[:].bitcast(I32), 0)
+        nc.gpsimd.memset(w8_s[:].rearrange("p a n -> p (a n)").bitcast(I32), 0)
+        for page in (page_b[0], page_a[0], page_b[1]):
+            nc.vector.memset(page[:], 0.0)
+
+        nc.sync.dma_start(list_tab[:], offs)
+        nc.sync.dma_start(list_b[:], offs3)
+        nc.sync.dma_start(list_a[:], offs2)
+        for q in range(4):
+            nc.sync.dma_start(tab_s[32 * q : 32 * q + 4, :].bitcast(I32), tab_scales[0, 4 * q : 4 * q + 4, :].bitcast(I32))
+        table_words = tab_words[0].rearrange("p n t -> p (n t)").bitcast(I32)
+        for c in range(4):
+            nc.sync.dma_start(tab_w[:, c * 512 : (c + 1) * 512], table_words[:, c * 512 : (c + 1) * 512])
+        for q in range(4):
+            nc.sync.dma_start(w4_s[32 * q : 32 * q + 4, :].bitcast(I32), w4_scales[0, 4 * q : 4 * q + 4, :].bitcast(I32))
+        nc.sync.dma_start(w4_w[:].bitcast(I32), w4_words[0].bitcast(I32))
+        nc.sync.dma_start(gain_b[:], wg2)
+        make_identity(nc, ident[:])
+        nc.gpsimd.memset(page_a[1][:], 0.0)
+
+        halves = [(slice(h * BANK, (h + 1) * BANK), list_tab[:, h * 32 : (h + 1) * 32]) for h in range(2)]
+        for cols, entries in halves:
+            nc.vector.tensor_copy(v_w[:, cols], tab_w[:].bitcast(U32).indirect(entries))
+        for cols, entries in halves:
+            nc.vector.tensor_copy(v_s[:, cols], tab_s[:].indirect(entries))
+
+        def quantise_w1(g):
+            cols = slice(g * W1_COLS, (g + 1) * W1_COLS)
+            raw = ring.tile([P, 4, W1_COLS], F32, name="w1_raw")
+            nc.sync.dma_start(raw[:], w1[:, cols].rearrange("(p t) c -> p t c", t=4))
+            grouped = ring.tile([P, W1_COLS, 4], BF16, name="w1_grouped", align_bytes=64)
+            nc.scalar.copy(
+                grouped[:].rearrange("p (c i) t -> p c t i", i=4),
+                raw[:].rearrange("p t (c i) -> p c t i", i=4),
+            )
+            nc.vector.quantize_mx(
+                out=w1_w[:, cols].bitcast(FP8X4), scales=w1_s[:, cols], in_=grouped[:].rearrange("p c t -> p (c t)")
+            )
+
+        def features_b(s):
+            for half in range(2):
+                cols = slice(half * BANK, (half + 1) * BANK)
+                nc.tensor.matmul_mx(
+                    out=banks[half][:],
+                    lhsT=w4_w[:, 2 * P * s : 2 * P * (s + 1)].bitcast(FP4X4),
+                    lhsT_scale=w4_s[:, P * s : P * (s + 1)],
+                    rhs=v_w[:, cols].bitcast(FP8X4),
+                    rhs_scale=v_s[:, cols],
+                    start=True,
+                    stop=True,
+                )
+                nc.scalar.activation(work[s % 2][:, cols], banks[half][:], ACT.Copy, scale=-1.0)
+
+        def features_a(s):
+            for half in range(2):
+                cols = slice(half * BANK, (half + 1) * BANK)
+                nc.tensor.matmul_mx(
+                    out=banks[half][:],
+                    lhsT=w1_w[:, P * s : P * (s + 1)].bitcast(FP8X4),
+                    lhsT_scale=w1_s[:, P * s : P * (s + 1)],
+                    rhs=v_w[:, cols].bitcast(FP8X4),
+                    rhs_scale=v_s[:, cols],
+                    start=True,
+                    stop=True,
+                )
+                nc.scalar.copy(work[s % 2][:, S + half * BANK : S + (half + 1) * BANK], banks[half][:])
+
+        def scatter_b(s, pieces):
+            width = S // pieces
+            for i in range(pieces):
+                cols = slice(i * width, (i + 1) * width)
+                nc.vector.tensor_tensor(
+                    page_b[s % 2][:].indirect(list_b[:, i * width // 16 : (i + 1) * width // 16]),
+                    work[s % 2][:, cols],
+                    gain_b[:, cols],
+                    MULT,
+                )
+
+        def scatter_a(s):
+            nc.vector.tensor_tensor(page_a[s % 2][:].indirect(list_a[:]), work[s % 2][:, S : 2 * S], gain_a[:], MULT)
+
+        def pair_view(ap):
+            return ap.rearrange("m (b p u e) -> m u b p e", b=BLOCKS, u=2, e=2)
+
+        def damping(s, held, groups):
+            rows = plans.tile([P, T2], F32, name="plan_rows")
+            nc.sync.dma_start(rows[:], plan[P * s : P * (s + 1), :])
+            for page in (page_b, page_a):
+                for c in range(CHUNKS):
+                    for b in range(BLOCKS):
+                        m0 = c * BANK + b * P
+                        nc.tensor.matmul(
+                            held[c][:, b * P : (b + 1) * P],
+                            lhsT=page[s % 2][:, m0 : m0 + P],
+                            rhs=ident[:],
+                            is_transpose=True,
+                            start=(page is page_b and b == 0),
+                            stop=(page is page_a and b == BLOCKS - 1),
+                        )
+            parts = [work[s % 2][:, c * BANK : (c + 1) * BANK] for c in range(CHUNKS)]
+            for group in groups:
+                for c in group:
+                    nc.scalar.activation(
+                        parts[c].rearrange("m (u w e) -> m u w e", u=2, e=2),
+                        held[c][:].rearrange("m (w u e) -> m u w e", u=2, e=2),
+                        ACT.Square,
+                    )
+                    for b in range(BLOCKS):
+                        m0 = c * BANK + b * P
+                        nc.tensor.transpose(held[c][:, b * P : (b + 1) * P], rows[:, m0 : m0 + P], ident[:])
+                for c in group:
+                    nc.scalar.activation(parts[c], parts[c], ACT.Abs_reciprocal_sqrt, bias=ROOT * ROOT, scale=ROOT * ROOT)
+                for c in group:
+                    nc.scalar.activation(parts[c], parts[c], ACT.Square, scale=ROOT)
+                if len(group) == 1:
+                    damp_plan(s, held, group[0])
+                    finish(group[0], held)
+
+        def damp_plan(s, held, c):
+            a, q = divmod(s, 4)
+            nc.vector.tensor_tensor(
+                z_t[a][c][:, :, :, 64 * q : 64 * (q + 1)].rearrange("m u b (p e) -> m u b p e", e=2),
+                pair_view(held[c][:]),
+                work[s % 2][:, c * BANK : (c + 1) * BANK].rearrange("m (u b p e) -> m u b p e", u=2, b=BLOCKS, e=2),
+                MULT,
+            )
+
+        def quantise_z(a, c, pair):
+            grouped = ring.tile([P, BANK, 4], BF16, name="z_grouped", align_bytes=64)
+            words = z_t[a][c][:].rearrange("m u b w -> m (u b w)").bitcast(F32)
+            grouped_words = grouped[:].rearrange("p m t -> p (m t)").bitcast(F32)
+            for half in range(2):
+                bank = pair[half]
+                for u in range(2):
+                    for j in range(2):
+                        w0 = (u * BLOCKS + 2 * half + j) * P
+                        nc.tensor.transpose(bank[:, (2 * u + j) * P : (2 * u + j + 1) * P], words[:, w0 : w0 + P], ident[:])
+                nc.scalar.copy(
+                    grouped_words[:, half * BANK : (half + 1) * BANK].rearrange("p (m u) -> p m u", u=2),
+                    bank[:].rearrange("p (u m) -> p m u", u=2),
+                )
+            nc.vector.quantize_mx(
+                out=z_w[a][c][:].bitcast(FP8X4), scales=z_s[a][c][:], in_=grouped[:].rearrange("p m t -> p (m t)")
+            )
+
+        def product_pass(bank, a, c, n, start, stop):
+            nc.tensor.matmul_mx(
+                out=bank[:],
+                lhsT=w8_w[:, a, n * P : (n + 1) * P].bitcast(FP8X4),
+                lhsT_scale=w8_s[:, a, n * P : (n + 1) * P],
+                rhs=z_w[a][c][:].bitcast(FP8X4),
+                rhs_scale=z_s[a][c][:],
+                start=start,
+                stop=stop,
+            )
+
+        def finish(c, held):
+            quantise_z(1, c, banks[2:4])
+            cols = slice(c * BANK, (c + 1) * BANK)
+            free = banks[4:6] + held[: c + 1]
+            on_vector = 2 if c == CHUNKS - 1 else 3
+            for n in range(N // P):
+                bank = free[(4 * c + n) % len(free)]
+                product_pass(bank, 0, c, n, True, False)
+                product_pass(bank, 1, c, n, False, True)
+                staged = stores.tile([P, BANK], F32, name="staged")
+                if n < on_vector:
+                    nc.vector.tensor_copy(staged[:], bank[:])
+                else:
+                    nc.scalar.copy(staged[:], bank[:])
+                nc.sync.dma_start(out[n * P : (n + 1) * P, cols], staged[:])
+
+        features_b(0)
+        scatter_b(0, 2)
+        quantise_w1(0)
+        nc.sync.dma_start(gain_a[:], wg1)
+        features_a(0)
+        scatter_a(0)
+        features_b(1)
+        features_a(1)
+        scatter_b(1, 1)
+        scatter_a(1)
+        for g in range(1, H // W1_COLS):
+            quantise_w1(g)
+        nc.sync.dma_start(w8_w[:], w8_words.rearrange("a p n t -> p a (n t)").bitcast(I32))
+        for q in range(4):
+            nc.sync.dma_start(
+                w8_s[32 * q : 32 * q + 4, :, :].bitcast(I32),
+                w8_scales[:, 4 * q : 4 * q + 4, :].rearrange("a r n -> r a n").bitcast(I32),
+            )
+
+        steady = banks[2:6]
+        for s in range(SLICES - 1):
+            damping(s, steady, [range(CHUNKS)])
+            for c in range(CHUNKS):
+                damp_plan(s, steady, c)
+            if s + 2 < SLICES:
+                features_b(s + 2)
+                features_a(s + 2)
+                scatter_b(s + 2, 1)
+                scatter_a(s + 2)
+            if s == 3:
+                quantise_z(0, 0, steady[0:2])
+            if 3 <= s <= 5:
+                quantise_z(0, s - 2, steady[2:4])
+
+        damping(SLICES - 1, banks[0:2] + banks[6:8], [[c] for c in range(CHUNKS)])

@@ -23,8 +23,23 @@ BANK = 512
 SLICES = H // P
 CHUNKS = T2 // BANK
 BLOCKS = BANK // P
-W1_COLS = 256
+W1_PIECES = (0, 128, 256, 512, 1024)
+EDGES = (0, 256, 512, 1024, 1536, 2048)
+DQ, DP = 1, 3
+UNITS = len(EDGES) - 1
 ROOT = 75.0 / 64.0
+
+
+def MENG(nc, i):
+    return nc.vector
+
+
+def WCOPY(nc, i):
+    return nc.vector.tensor_copy if i < 4 else nc.scalar.copy
+
+
+def OCOPY(nc, i, g):
+    return nc.vector.tensor_copy if g == 0 else nc.scalar.copy
 
 
 def tile_list_trap_bench_release_kernel(
@@ -33,8 +48,8 @@ def tile_list_trap_bench_release_kernel(
     nc = tc.nc
     with ExitStack() as ctx:
         keep = ctx.enter_context(tc.tile_pool(name="keep", bufs=1))
-        ring = ctx.enter_context(tc.tile_pool(name="ring", bufs=2))
-        plans = ctx.enter_context(tc.tile_pool(name="plans", bufs=3))
+        plans = ctx.enter_context(tc.tile_pool(name="plans", bufs=2))
+        groups = ctx.enter_context(tc.tile_pool(name="groups", bufs=2))
         stores = ctx.enter_context(tc.tile_pool(name="stores", bufs=8))
         psum = ctx.enter_context(tc.psum_pool(name="psum", bufs=1))
 
@@ -48,7 +63,6 @@ def tile_list_trap_bench_release_kernel(
         v_w = keep.tile([P, S], U32, name="v_w", align_bytes=64)
         v_s = keep.tile([P, S], U8, name="v_s", align_bytes=64)
         w1_w = keep.tile([P, H], U32, name="w1_w", align_bytes=64)
-        w1_s = keep.tile([P, H], U8, name="w1_s", align_bytes=64)
         w4_w = keep.tile([P, 2 * H], U8, name="w4_w", align_bytes=64)
         w4_s = keep.tile([P, H], U8, name="w4_s", align_bytes=64)
         w8_w = keep.tile([P, 2, N], I32, name="w8_w", align_bytes=64)
@@ -58,43 +72,42 @@ def tile_list_trap_bench_release_kernel(
         ident = keep.tile([P, P], F32, name="ident")
         page_a = [keep.tile([P, T2], F32, name=f"page_a{i}") for i in range(2)]
         page_b = [keep.tile([P, T2], F32, name=f"page_b{i}") for i in range(2)]
-        work = [keep.tile([P, T2], F32, name=f"work{i}") for i in range(2)]
-        z_t = [[keep.tile([P, 2, BLOCKS, 2 * P], BF16, name=f"z_t{a}{c}") for c in range(CHUNKS)] for a in range(2)]
-        z_w = [[keep.tile([P, BANK], U32, name=f"z_w{a}{c}", align_bytes=64) for c in range(CHUNKS)] for a in range(2)]
-        z_s = [[keep.tile([P, BANK], U8, name=f"z_s{a}{c}", align_bytes=64) for c in range(CHUNKS)] for a in range(2)]
+        work = [keep.tile([P, T2], F32, name=f"work{i}") for i in range(3)]
+        turned = [keep.tile([P, T2], F32, name=f"turned{i}") for i in range(2)]
+        z_tiles = [keep.tile([P, 2, BLOCKS, 2 * P], BF16, name=f"z_t{i}") for i in range(CHUNKS + 2)]
+        z_t = [z_tiles[0:4], z_tiles[0:2] + z_tiles[4:6]]
+        z_w = [keep.tile([P, T2], U32, name=f"z_w{a}", align_bytes=64) for a in range(2)]
+        z_s = [keep.tile([P, T2], U8, name=f"z_s{a}", align_bytes=64) for a in range(2)]
+        outer = banks[0:2] + banks[6:8]
+        inner = banks[2:6]
 
         nc.gpsimd.memset(tab_s[:].bitcast(I32), 0)
         nc.gpsimd.memset(w4_s[:].bitcast(I32), 0)
+        for page in (page_a[0], page_b[0]):
+            nc.vector.memset(page[:].bitcast(I32), 0)
+        make_identity(nc, ident[:])
         nc.gpsimd.memset(w8_s[:].rearrange("p a n -> p (a n)").bitcast(I32), 0)
-        for page in (page_b[0], page_a[0], page_b[1]):
-            nc.vector.memset(page[:], 0.0)
+        for page in (page_a[1], page_b[1]):
+            nc.gpsimd.memset(page[:], 0.0)
 
-        nc.sync.dma_start(list_tab[:], offs)
-        nc.sync.dma_start(list_b[:], offs3)
-        nc.sync.dma_start(list_a[:], offs2)
+        for tile, entries in ((list_tab, offs), (list_a, offs2), (list_b, offs3)):
+            nc.sync.dma_start(tile[:], entries)
         for q in range(4):
             nc.sync.dma_start(tab_s[32 * q : 32 * q + 4, :].bitcast(I32), tab_scales[0, 4 * q : 4 * q + 4, :].bitcast(I32))
-        table_words = tab_words[0].rearrange("p n t -> p (n t)").bitcast(I32)
-        for c in range(4):
-            nc.sync.dma_start(tab_w[:, c * 512 : (c + 1) * 512], table_words[:, c * 512 : (c + 1) * 512])
-        for q in range(4):
-            nc.sync.dma_start(w4_s[32 * q : 32 * q + 4, :].bitcast(I32), w4_scales[0, 4 * q : 4 * q + 4, :].bitcast(I32))
-        nc.sync.dma_start(w4_w[:].bitcast(I32), w4_words[0].bitcast(I32))
-        nc.sync.dma_start(gain_b[:], wg2)
-        make_identity(nc, ident[:])
-        nc.gpsimd.memset(page_a[1][:], 0.0)
-
-        halves = [(slice(h * BANK, (h + 1) * BANK), list_tab[:, h * 32 : (h + 1) * 32]) for h in range(2)]
-        for cols, entries in halves:
+        def gather(half):
+            cols = slice(half * BANK, (half + 1) * BANK)
+            entries = list_tab[:, half * 32 : (half + 1) * 32]
             nc.vector.tensor_copy(v_w[:, cols], tab_w[:].bitcast(U32).indirect(entries))
-        for cols, entries in halves:
             nc.vector.tensor_copy(v_s[:, cols], tab_s[:].indirect(entries))
 
+        w1_s = keep.tile([P, H], U8, name="w1_s", align_bytes=64)
+
         def quantise_w1(g):
-            cols = slice(g * W1_COLS, (g + 1) * W1_COLS)
-            raw = ring.tile([P, 4, W1_COLS], F32, name="w1_raw")
+            cols = slice(W1_PIECES[g], W1_PIECES[g + 1])
+            width = W1_PIECES[g + 1] - W1_PIECES[g]
+            raw = keep.tile([P, 4, width], F32, name=f"w1_raw{g}")
             nc.sync.dma_start(raw[:], w1[:, cols].rearrange("(p t) c -> p t c", t=4))
-            grouped = ring.tile([P, W1_COLS, 4], BF16, name="w1_grouped", align_bytes=64)
+            grouped = keep.tile([P, width, 4], BF16, name=f"w1_grouped{g}", align_bytes=64)
             nc.scalar.copy(
                 grouped[:].rearrange("p (c i) t -> p c t i", i=4),
                 raw[:].rearrange("p t (c i) -> p c t i", i=4),
@@ -103,56 +116,54 @@ def tile_list_trap_bench_release_kernel(
                 out=w1_w[:, cols].bitcast(FP8X4), scales=w1_s[:, cols], in_=grouped[:].rearrange("p c t -> p (c t)")
             )
 
-        def features_b(s):
-            for half in range(2):
-                cols = slice(half * BANK, (half + 1) * BANK)
-                nc.tensor.matmul_mx(
-                    out=banks[half][:],
-                    lhsT=w4_w[:, 2 * P * s : 2 * P * (s + 1)].bitcast(FP4X4),
-                    lhsT_scale=w4_s[:, P * s : P * (s + 1)],
-                    rhs=v_w[:, cols].bitcast(FP8X4),
-                    rhs_scale=v_s[:, cols],
-                    start=True,
-                    stop=True,
-                )
-                nc.scalar.activation(work[s % 2][:, cols], banks[half][:], ACT.Copy, scale=-1.0)
+        def piece(s, j):
+            return work[s % 3][:, j * BANK : (j + 1) * BANK]
 
-        def features_a(s):
-            for half in range(2):
-                cols = slice(half * BANK, (half + 1) * BANK)
-                nc.tensor.matmul_mx(
-                    out=banks[half][:],
-                    lhsT=w1_w[:, P * s : P * (s + 1)].bitcast(FP8X4),
-                    lhsT_scale=w1_s[:, P * s : P * (s + 1)],
-                    rhs=v_w[:, cols].bitcast(FP8X4),
-                    rhs_scale=v_s[:, cols],
-                    start=True,
-                    stop=True,
-                )
-                nc.scalar.copy(work[s % 2][:, S + half * BANK : S + (half + 1) * BANK], banks[half][:])
+        def features(s, j, bank):
+            half = j % 2
+            cols = slice(half * BANK, (half + 1) * BANK)
+            if j >= 2:
+                codes, scales, gain, sign = w4_w[:, 2 * P * s : 2 * P * (s + 1)].bitcast(FP4X4), w4_s, gain_b, -1.0
+            else:
+                codes, scales, gain, sign = w1_w[:, P * s : P * (s + 1)].bitcast(FP8X4), w1_s, gain_a, 1.0
+            nc.tensor.matmul_mx(
+                out=bank[:],
+                lhsT=codes,
+                lhsT_scale=scales[:, P * s : P * (s + 1)],
+                rhs=v_w[:, cols].bitcast(FP8X4),
+                rhs_scale=v_s[:, cols],
+                start=True,
+                stop=True,
+            )
+            if (s, j) == (0, 0):
+                nc.vector.tensor_tensor(piece(s, j), bank[:], gain[:, cols], MULT)
+            else:
+                nc.scalar.activation(piece(s, j), bank[:], ACT.Copy, scale=sign)
+                nc.gpsimd.tensor_tensor(piece(s, j), piece(s, j), gain[:, cols], MULT)
 
-        def scatter_b(s, pieces):
-            width = S // pieces
-            for i in range(pieces):
-                cols = slice(i * width, (i + 1) * width)
-                nc.vector.tensor_tensor(
-                    page_b[s % 2][:].indirect(list_b[:, i * width // 16 : (i + 1) * width // 16]),
-                    work[s % 2][:, cols],
-                    gain_b[:, cols],
-                    MULT,
-                )
+        def place_half(s, j):
+            page, entries = (page_a, list_a) if j < 2 else (page_b, list_b)
+            half = j % 2
+            nc.vector.tensor_copy(page[s % 2][:].indirect(entries[:, 32 * half : 32 * (half + 1)]), piece(s, j))
 
-        def scatter_a(s):
-            nc.vector.tensor_tensor(page_a[s % 2][:].indirect(list_a[:]), work[s % 2][:, S : 2 * S], gain_a[:], MULT)
+        def scatter(s):
+            nc.vector.tensor_copy(page_a[s % 2][:].indirect(list_a[:]), work[s % 3][:, 0:S])
+            nc.vector.tensor_copy(page_b[s % 2][:].indirect(list_b[:]), work[s % 3][:, S : 2 * S])
 
-        def pair_view(ap):
-            return ap.rearrange("m (b p u e) -> m u b p e", b=BLOCKS, u=2, e=2)
-
-        def damping(s, held, groups):
+        def load_plan(s):
             rows = plans.tile([P, T2], F32, name="plan_rows")
             nc.sync.dma_start(rows[:], plan[P * s : P * (s + 1), :])
-            for page in (page_b, page_a):
-                for c in range(CHUNKS):
+            return rows
+
+        def turn_plan(s, rows, c, bank):
+            for b in range(BLOCKS):
+                m0 = c * BANK + b * P
+                nc.tensor.transpose(bank[:, b * P : (b + 1) * P], rows[:, m0 : m0 + P], ident[:])
+            nc.scalar.copy(*by_pairs(turned[s % 2][:, c * BANK : (c + 1) * BANK], bank))
+
+        def difference(s, held):
+            for c in range(CHUNKS):
+                for page in (page_a, page_b):
                     for b in range(BLOCKS):
                         m0 = c * BANK + b * P
                         nc.tensor.matmul(
@@ -160,94 +171,144 @@ def tile_list_trap_bench_release_kernel(
                             lhsT=page[s % 2][:, m0 : m0 + P],
                             rhs=ident[:],
                             is_transpose=True,
-                            start=(page is page_b and b == 0),
-                            stop=(page is page_a and b == BLOCKS - 1),
+                            start=(page is page_a and b == 0),
+                            stop=(page is page_b and b == BLOCKS - 1),
                         )
-            parts = [work[s % 2][:, c * BANK : (c + 1) * BANK] for c in range(CHUNKS)]
-            for group in groups:
-                for c in group:
-                    nc.scalar.activation(
-                        parts[c].rearrange("m (u w e) -> m u w e", u=2, e=2),
-                        held[c][:].rearrange("m (w u e) -> m u w e", u=2, e=2),
-                        ACT.Square,
-                    )
-                    for b in range(BLOCKS):
-                        m0 = c * BANK + b * P
-                        nc.tensor.transpose(held[c][:, b * P : (b + 1) * P], rows[:, m0 : m0 + P], ident[:])
-                for c in group:
-                    nc.scalar.activation(parts[c], parts[c], ACT.Abs_reciprocal_sqrt, bias=ROOT * ROOT, scale=ROOT * ROOT)
-                for c in group:
-                    nc.scalar.activation(parts[c], parts[c], ACT.Square, scale=ROOT)
-                if len(group) == 1:
-                    damp_plan(s, held, group[0])
-                    finish(group[0], held)
 
-        def damp_plan(s, held, c):
+        def by_pairs(out_ap, bank):
+            return out_ap.rearrange("m (u w e) -> m u w e", u=2, e=2), bank[:].rearrange("m (w u e) -> m u w e", u=2, e=2)
+
+        def square(s, c, bank):
+            nc.scalar.activation(*by_pairs(piece(s, c), bank), ACT.Square)
+
+        def damping(s, chunks):
+            for c in chunks:
+                nc.scalar.activation(piece(s, c), piece(s, c), ACT.Abs_reciprocal_sqrt, bias=ROOT * ROOT, scale=ROOT * ROOT)
+            for c in chunks:
+                nc.scalar.activation(piece(s, c), piece(s, c), ACT.Square, scale=ROOT)
+
+        def in_order(ap):
+            return ap.rearrange("m (g w) -> m g w", w=64)
+
+        def damp_plan(s, c, engine):
             a, q = divmod(s, 4)
-            nc.vector.tensor_tensor(
-                z_t[a][c][:, :, :, 64 * q : 64 * (q + 1)].rearrange("m u b (p e) -> m u b p e", e=2),
-                pair_view(held[c][:]),
-                work[s % 2][:, c * BANK : (c + 1) * BANK].rearrange("m (u b p e) -> m u b p e", u=2, b=BLOCKS, e=2),
+            engine.tensor_tensor(
+                z_t[a][c][:, :, :, 64 * q : 64 * (q + 1)].rearrange("m u b w -> m (u b) w"),
+                in_order(turned[s % 2][:, c * BANK : (c + 1) * BANK]),
+                in_order(piece(s, c)),
                 MULT,
             )
 
-        def quantise_z(a, c, pair):
-            grouped = ring.tile([P, BANK, 4], BF16, name="z_grouped", align_bytes=64)
-            words = z_t[a][c][:].rearrange("m u b w -> m (u b w)").bitcast(F32)
+        def quantise_z(a, first, count, free, copy):
+            grouped = groups.tile([P, count * BANK, 4], BF16, name="z_grouped", align_bytes=64)
             grouped_words = grouped[:].rearrange("p m t -> p (m t)").bitcast(F32)
-            for half in range(2):
-                bank = pair[half]
+            for i in range(2 * count):
+                words = z_t[a][first + i // 2][:].rearrange("m u b w -> m (u b w)").bitcast(F32)
                 for u in range(2):
                     for j in range(2):
-                        w0 = (u * BLOCKS + 2 * half + j) * P
+                        w0 = (u * BLOCKS + 2 * (i % 2) + j) * P
+                        nc.tensor.transpose(free[i][:, (2 * u + j) * P : (2 * u + j + 1) * P], words[:, w0 : w0 + P], ident[:])
+                copy(
+                    grouped_words[:, i * BANK : (i + 1) * BANK].rearrange("p (m u) -> p m u", u=2),
+                    free[i][:].rearrange("p (u m) -> p m u", u=2),
+                )
+            cols = slice(first * BANK, (first + count) * BANK)
+            nc.vector.quantize_mx(
+                out=z_w[a][:, cols].bitcast(FP8X4), scales=z_s[a][:, cols], in_=grouped[:].rearrange("p m t -> p (m t)")
+            )
+
+        def last_damping(i, bank):
+            cols = slice(EDGES[i], EDGES[i + 1])
+            c, first = divmod(EDGES[i] // P, BLOCKS)
+            blocks = (EDGES[i + 1] - EDGES[i]) // P
+            total = turned[0][:, cols]
+            nc.vector.tensor_tensor(total, page_a[last % 2][:, cols], page_b[last % 2][:, cols], ADD)
+            for b in range(blocks):
+                nc.tensor.transpose(bank[:, b * P : (b + 1) * P], total[:, b * P : (b + 1) * P], ident[:])
+            values = work[last % 3][:, cols]
+            nc.scalar.activation(
+                values.rearrange("m (u w e) -> m u w e", u=2, e=2),
+                bank[:, 0 : blocks * P].rearrange("m (w u e) -> m u w e", u=2, e=2),
+                ACT.Square,
+            )
+            nc.scalar.activation(values, values, ACT.Abs_reciprocal_sqrt, bias=ROOT * ROOT, scale=ROOT * ROOT)
+            nc.scalar.activation(values, values, ACT.Square, scale=ROOT)
+            plan_part = turned[last % 2][:, c * BANK : (c + 1) * BANK].rearrange("m (u b w) -> m u b w", u=2, w=64)
+            MENG(nc, i).tensor_tensor(
+                z_t[1][c][:, :, first : first + blocks, 192:256],
+                plan_part[:, :, first : first + blocks, :],
+                values.rearrange("m (u b w) -> m u b w", u=2, w=64),
+                MULT,
+            )
+
+        def last_quantise(i, free):
+            cols = slice(EDGES[i], EDGES[i + 1])
+            c, first = divmod(EDGES[i] // P, BLOCKS)
+            blocks = (EDGES[i + 1] - EDGES[i]) // P
+            grouped = groups.tile([P, blocks * P, 4], BF16, name="z_grouped", align_bytes=64)
+            grouped_words = grouped[:].rearrange("p m t -> p (m t)").bitcast(F32)
+            words = z_t[1][c][:].rearrange("m u b w -> m (u b w)").bitcast(F32)
+            for h in range(blocks // 2):
+                k = EDGES[i] // 256 + h
+                bank = free[k % 2]
+                for u in range(2):
+                    for j in range(2):
+                        w0 = (u * BLOCKS + first + 2 * h + j) * P
                         nc.tensor.transpose(bank[:, (2 * u + j) * P : (2 * u + j + 1) * P], words[:, w0 : w0 + P], ident[:])
-                nc.scalar.copy(
-                    grouped_words[:, half * BANK : (half + 1) * BANK].rearrange("p (m u) -> p m u", u=2),
+                WCOPY(nc, k)(
+                    grouped_words[:, h * BANK : (h + 1) * BANK].rearrange("p (m u) -> p m u", u=2),
                     bank[:].rearrange("p (u m) -> p m u", u=2),
                 )
             nc.vector.quantize_mx(
-                out=z_w[a][c][:].bitcast(FP8X4), scales=z_s[a][c][:], in_=grouped[:].rearrange("p m t -> p (m t)")
+                out=z_w[1][:, cols].bitcast(FP8X4), scales=z_s[1][:, cols], in_=grouped[:].rearrange("p m t -> p (m t)")
             )
 
-        def product_pass(bank, a, c, n, start, stop):
-            nc.tensor.matmul_mx(
-                out=bank[:],
-                lhsT=w8_w[:, a, n * P : (n + 1) * P].bitcast(FP8X4),
-                lhsT_scale=w8_s[:, a, n * P : (n + 1) * P],
-                rhs=z_w[a][c][:].bitcast(FP8X4),
-                rhs_scale=z_s[a][c][:],
-                start=start,
-                stop=stop,
-            )
+        def products(i, free):
+            cols = slice(EDGES[i], EDGES[i + 1])
+            width = EDGES[i + 1] - EDGES[i]
+            tiles = BANK // width
+            for g in range(N // P // tiles):
+                k = EDGES[i] // P + g
+                bank = free[k % 4]
+                for a in range(2):
+                    for j in range(tiles):
+                        n = tiles * g + j
+                        nc.tensor.matmul_mx(
+                            out=bank[:, j * width : (j + 1) * width],
+                            lhsT=w8_w[:, a, n * P : (n + 1) * P].bitcast(FP8X4),
+                            lhsT_scale=w8_s[:, a, n * P : (n + 1) * P],
+                            rhs=z_w[a][:, cols].bitcast(FP8X4),
+                            rhs_scale=z_s[a][:, cols],
+                            start=(a, j) == (0, 0),
+                            stop=(a, j) == (1, tiles - 1),
+                        )
+                staged = stores.tile([P, tiles, width], F32, name="staged")
+                OCOPY(nc, i, k % 2)(staged[:].rearrange("p j m -> p (j m)"), bank[:])
+                rows = slice(tiles * g * P, tiles * (g + 1) * P)
+                nc.sync.dma_start(out[rows, cols].rearrange("(j p) m -> p j m", p=P), staged[:])
 
-        def finish(c, held):
-            quantise_z(1, c, banks[2:4])
-            cols = slice(c * BANK, (c + 1) * BANK)
-            free = banks[4:6] + held[: c + 1]
-            on_vector = 2 if c == CHUNKS - 1 else 3
-            for n in range(N // P):
-                bank = free[(4 * c + n) % len(free)]
-                product_pass(bank, 0, c, n, True, False)
-                product_pass(bank, 1, c, n, False, True)
-                staged = stores.tile([P, BANK], F32, name="staged")
-                if n < on_vector:
-                    nc.vector.tensor_copy(staged[:], bank[:])
-                else:
-                    nc.scalar.copy(staged[:], bank[:])
-                nc.sync.dma_start(out[n * P : (n + 1) * P, cols], staged[:])
-
-        features_b(0)
-        scatter_b(0, 2)
+        last = SLICES - 1
         quantise_w1(0)
-        nc.sync.dma_start(gain_a[:], wg1)
-        features_a(0)
-        scatter_a(0)
-        features_b(1)
-        features_a(1)
-        scatter_b(1, 1)
-        scatter_a(1)
-        for g in range(1, H // W1_COLS):
+        table_words = tab_words[0].rearrange("p n t -> p (n t)").bitcast(I32)
+        for half in range(2):
+            cols = slice(half * (T // 2), (half + 1) * (T // 2))
+            nc.sync.dma_start(tab_w[:, cols], table_words[:, cols])
+        gather(0)
+        gather(1)
+        for half in range(2):
+            nc.sync.dma_start(gain_a[:, half * BANK : (half + 1) * BANK], wg1[:, half * BANK : (half + 1) * BANK])
+        nc.sync.dma_start(w4_w[:].bitcast(I32), w4_words[0].bitcast(I32))
+        for q in range(4):
+            nc.sync.dma_start(w4_s[32 * q : 32 * q + 4, :].bitcast(I32), w4_scales[0, 4 * q : 4 * q + 4, :].bitcast(I32))
+        nc.sync.dma_start(gain_b[:], wg2)
+        for j in range(4):
+            features(0, j, inner[j])
+            place_half(0, j)
+        for g in range(1, len(W1_PIECES) - 1):
             quantise_w1(g)
+        for j in range(4):
+            features(1, j, inner[(j + 2) % 4])
+        scatter(1)
         nc.sync.dma_start(w8_w[:], w8_words.rearrange("a p n t -> p a (n t)").bitcast(I32))
         for q in range(4):
             nc.sync.dma_start(
@@ -255,19 +316,31 @@ def tile_list_trap_bench_release_kernel(
                 w8_scales[:, 4 * q : 4 * q + 4, :].rearrange("a r n -> r a n").bitcast(I32),
             )
 
-        steady = banks[2:6]
-        for s in range(SLICES - 1):
-            damping(s, steady, [range(CHUNKS)])
-            for c in range(CHUNKS):
-                damp_plan(s, steady, c)
-            if s + 2 < SLICES:
-                features_b(s + 2)
-                features_a(s + 2)
-                scatter_b(s + 2, 1)
-                scatter_a(s + 2)
-            if s == 3:
-                quantise_z(0, 0, steady[0:2])
-            if 3 <= s <= 5:
-                quantise_z(0, s - 2, steady[2:4])
 
-        damping(SLICES - 1, banks[0:2] + banks[6:8], [[c] for c in range(CHUNKS)])
+        for s in range(SLICES):
+            rows = load_plan(s)
+            for c in range(CHUNKS):
+                turn_plan(s, rows, c, outer[c])
+            if s == last:
+                break
+            difference(s, inner)
+            for c in range(CHUNKS):
+                square(s, c, inner[c])
+            if s in (4, 5):
+                quantise_z(0, 2 * (s - 4), 2, outer, nc.scalar.copy)
+            if s + 2 < SLICES:
+                for j in range(4):
+                    features(s + 2, j, inner[j])
+                scatter(s + 2)
+            damping(s, range(0, 2))
+            damping(s, range(2, 4))
+            for c in range(CHUNKS):
+                damp_plan(s, c, nc.gpsimd)
+
+        for step in range(UNITS + DP):
+            if step < UNITS:
+                last_damping(step, inner[step % 2])
+            if step >= DP:
+                products(step - DP, outer)
+            if DQ <= step < UNITS + DQ:
+                last_quantise(step - DQ, inner[2:4])

@@ -21,25 +21,13 @@ ADD = mybir.AluOpType.add
 P = 128
 BANK = 512
 SLICES = H // P
+LAST = SLICES - 1
 CHUNKS = T2 // BANK
 BLOCKS = BANK // P
-W1_PIECES = (0, 128, 256, 512, 1024)
-EDGES = (0, 256, 512, 1024, 1536, 2048)
-DQ, DP = 1, 3
-UNITS = len(EDGES) - 1
+RUN = P // 2
+LIST_HALF = BANK // 16
+W1_PIECES = ([(0, 128)], [(128, 256), (256, 512)], [(512, 1024)])
 ROOT = 75.0 / 64.0
-
-
-def MENG(nc, i):
-    return nc.vector
-
-
-def WCOPY(nc, i):
-    return nc.vector.tensor_copy if i < 4 else nc.scalar.copy
-
-
-def OCOPY(nc, i, g):
-    return nc.vector.tensor_copy if g == 0 else nc.scalar.copy
 
 
 def tile_list_trap_bench_release_kernel(
@@ -48,12 +36,15 @@ def tile_list_trap_bench_release_kernel(
     nc = tc.nc
     with ExitStack() as ctx:
         keep = ctx.enter_context(tc.tile_pool(name="keep", bufs=1))
-        plans = ctx.enter_context(tc.tile_pool(name="plans", bufs=2))
-        groups = ctx.enter_context(tc.tile_pool(name="groups", bufs=2))
+        loads = ctx.enter_context(tc.tile_pool(name="loads", bufs=2))
+        firsts = ctx.enter_context(tc.tile_pool(name="firsts", bufs=2))
+        seconds = ctx.enter_context(tc.tile_pool(name="seconds", bufs=3))
         stores = ctx.enter_context(tc.tile_pool(name="stores", bufs=8))
         psum = ctx.enter_context(tc.psum_pool(name="psum", bufs=1))
 
         banks = [psum.tile([P, BANK], F32, name=f"bank{b}") for b in range(8)]
+        plan_banks = banks[0:2] + banks[6:8]
+        sum_banks = banks[2:6]
 
         list_tab = keep.tile([P, S // 16], U16, name="list_tab")
         list_a = keep.tile([P, S // 16], U16, name="list_a")
@@ -67,280 +58,250 @@ def tile_list_trap_bench_release_kernel(
         w4_s = keep.tile([P, H], U8, name="w4_s", align_bytes=64)
         w8_w = keep.tile([P, 2, N], I32, name="w8_w", align_bytes=64)
         w8_s = keep.tile([P, 2, N], U8, name="w8_s", align_bytes=64)
-        gain_a = keep.tile([P, S], F32, name="gain_a")
-        gain_b = keep.tile([P, S], F32, name="gain_b")
+        gain = [keep.tile([P, S], F32, name=f"gain{i}") for i in range(2)]
         ident = keep.tile([P, P], F32, name="ident")
-        page_a = [keep.tile([P, T2], F32, name=f"page_a{i}") for i in range(2)]
+        page_a = [keep.tile([P, T2], F32, name=f"page_a{i}", align_bytes=64) for i in range(2)]
         page_b = [keep.tile([P, T2], F32, name=f"page_b{i}") for i in range(2)]
         work = [keep.tile([P, T2], F32, name=f"work{i}") for i in range(3)]
-        turned = [keep.tile([P, T2], F32, name=f"turned{i}") for i in range(2)]
-        z_tiles = [keep.tile([P, 2, BLOCKS, 2 * P], BF16, name=f"z_t{i}") for i in range(CHUNKS + 2)]
-        z_t = [z_tiles[0:4], z_tiles[0:2] + z_tiles[4:6]]
-        z_w = [keep.tile([P, T2], U32, name=f"z_w{a}", align_bytes=64) for a in range(2)]
+        turned = [keep.tile([P, T2], F32, name=f"turned{i}", align_bytes=64) for i in range(2)]
+        z_t = [[keep.tile([P, 2, 2, BLOCKS, 2 * P], BF16, name=f"z_t{a}{h}") for h in range(2)] for a in range(2)]
+        z_w = [[], [keep.tile([P, S], U32, name=f"z_w1{h}", align_bytes=64) for h in range(2)]]
         z_s = [keep.tile([P, T2], U8, name=f"z_s{a}", align_bytes=64) for a in range(2)]
-        outer = banks[0:2] + banks[6:8]
-        inner = banks[2:6]
-
-        nc.gpsimd.memset(tab_s[:].bitcast(I32), 0)
-        nc.gpsimd.memset(w4_s[:].bitcast(I32), 0)
-        for page in (page_a[0], page_b[0]):
-            nc.vector.memset(page[:].bitcast(I32), 0)
-        make_identity(nc, ident[:])
-        nc.gpsimd.memset(w8_s[:].rearrange("p a n -> p (a n)").bitcast(I32), 0)
-        for page in (page_a[1], page_b[1]):
-            nc.gpsimd.memset(page[:], 0.0)
-
-        for tile, entries in ((list_tab, offs), (list_a, offs2), (list_b, offs3)):
-            nc.sync.dma_start(tile[:], entries)
-        for q in range(4):
-            nc.sync.dma_start(tab_s[32 * q : 32 * q + 4, :].bitcast(I32), tab_scales[0, 4 * q : 4 * q + 4, :].bitcast(I32))
-        def gather(half):
-            cols = slice(half * BANK, (half + 1) * BANK)
-            entries = list_tab[:, half * 32 : (half + 1) * 32]
-            nc.vector.tensor_copy(v_w[:, cols], tab_w[:].bitcast(U32).indirect(entries))
-            nc.vector.tensor_copy(v_s[:, cols], tab_s[:].indirect(entries))
-
         w1_s = keep.tile([P, H], U8, name="w1_s", align_bytes=64)
 
-        def quantise_w1(g):
-            cols = slice(W1_PIECES[g], W1_PIECES[g + 1])
-            width = W1_PIECES[g + 1] - W1_PIECES[g]
-            raw = keep.tile([P, 4, width], F32, name=f"w1_raw{g}")
-            nc.sync.dma_start(raw[:], w1[:, cols].rearrange("(p t) c -> p t c", t=4))
-            grouped = keep.tile([P, width, 4], BF16, name=f"w1_grouped{g}", align_bytes=64)
+        def load_plane(plane, rows):
+            for q in range(4):
+                nc.sync.dma_start(plane[32 * q : 32 * q + 4].bitcast(I32), rows[4 * q : 4 * q + 4].bitcast(I32))
+
+        def quantise_w1(pool, ranges):
+            first, end = ranges[0][0], ranges[-1][1]
+            width = end - first
+            raw = pool.tile([P, 4, width], F32, name="rows")
+            nc.sync.dma_start(raw[:], w1[:, first:end].rearrange("(p t) c -> p t c", t=4))
+            grouped = keep.tile([P, width, 4], BF16, name=f"w1_grouped{first}", align_bytes=64)
             nc.scalar.copy(
                 grouped[:].rearrange("p (c i) t -> p c t i", i=4),
                 raw[:].rearrange("p t (c i) -> p c t i", i=4),
             )
-            nc.vector.quantize_mx(
-                out=w1_w[:, cols].bitcast(FP8X4), scales=w1_s[:, cols], in_=grouped[:].rearrange("p c t -> p (c t)")
-            )
+            for start, stop in ranges:
+                nc.vector.quantize_mx(
+                    out=w1_w[:, start:stop].bitcast(FP8X4),
+                    scales=w1_s[:, start:stop],
+                    in_=grouped[:, start - first : stop - first, :].rearrange("p c t -> p (c t)"),
+                )
 
-        def piece(s, j):
-            return work[s % 3][:, j * BANK : (j + 1) * BANK]
+        def columns(i, width=BANK):
+            return slice(i * width, (i + 1) * width)
 
-        def features(s, j, bank):
-            half = j % 2
-            cols = slice(half * BANK, (half + 1) * BANK)
-            if j >= 2:
-                codes, scales, gain, sign = w4_w[:, 2 * P * s : 2 * P * (s + 1)].bitcast(FP4X4), w4_s, gain_b, -1.0
+        def product(s, j, bank):
+            if j < 2:
+                weights, plane = w1_w[:, columns(s, P)].bitcast(FP8X4), w1_s
             else:
-                codes, scales, gain, sign = w1_w[:, P * s : P * (s + 1)].bitcast(FP8X4), w1_s, gain_a, 1.0
+                weights, plane = w4_w[:, columns(s, 2 * P)].bitcast(FP4X4), w4_s
             nc.tensor.matmul_mx(
                 out=bank[:],
-                lhsT=codes,
-                lhsT_scale=scales[:, P * s : P * (s + 1)],
-                rhs=v_w[:, cols].bitcast(FP8X4),
-                rhs_scale=v_s[:, cols],
+                lhsT=weights,
+                lhsT_scale=plane[:, columns(s, P)],
+                rhs=v_w[:, columns(j % 2)].bitcast(FP8X4),
+                rhs_scale=v_s[:, columns(j % 2)],
                 start=True,
                 stop=True,
             )
-            if (s, j) == (0, 0):
-                nc.vector.tensor_tensor(piece(s, j), bank[:], gain[:, cols], MULT)
-            else:
-                nc.scalar.activation(piece(s, j), bank[:], ACT.Copy, scale=sign)
-                nc.gpsimd.tensor_tensor(piece(s, j), piece(s, j), gain[:, cols], MULT)
 
-        def place_half(s, j):
-            page, entries = (page_a, list_a) if j < 2 else (page_b, list_b)
-            half = j % 2
-            nc.vector.tensor_copy(page[s % 2][:].indirect(entries[:, 32 * half : 32 * (half + 1)]), piece(s, j))
+        def features(s, side, pair):
+            for half in range(2):
+                j = 2 * side + half
+                product(s, j, pair[half])
+                nc.scalar.activation(work[s % 3][:, columns(j)], pair[half][:], ACT.Copy, scale=(1.0, -1.0)[side])
+            values = work[s % 3][:, columns(side, S)]
+            nc.gpsimd.tensor_tensor(values, values, gain[side][:], MULT)
 
         def scatter(s):
-            nc.vector.tensor_copy(page_a[s % 2][:].indirect(list_a[:]), work[s % 3][:, 0:S])
-            nc.vector.tensor_copy(page_b[s % 2][:].indirect(list_b[:]), work[s % 3][:, S : 2 * S])
+            nc.vector.tensor_copy(page_a[s % 2][:].indirect(list_a[:]), work[s % 3][:, columns(0, S)])
+            nc.vector.tensor_copy(page_b[s % 2][:].indirect(list_b[:]), work[s % 3][:, columns(1, S)])
 
-        def load_plan(s):
-            rows = plans.tile([P, T2], F32, name="plan_rows")
-            nc.sync.dma_start(rows[:], plan[P * s : P * (s + 1), :])
-            return rows
+        def by_pairs(target, bank):
+            return target.rearrange("m (u w e) -> m u w e", u=2, e=2), bank[:].rearrange("m (w u e) -> m u w e", u=2, e=2)
 
-        def turn_plan(s, rows, c, bank):
+        def turn_chunk(rows, c, bank):
             for b in range(BLOCKS):
-                m0 = c * BANK + b * P
-                nc.tensor.transpose(bank[:, b * P : (b + 1) * P], rows[:, m0 : m0 + P], ident[:])
-            nc.scalar.copy(*by_pairs(turned[s % 2][:, c * BANK : (c + 1) * BANK], bank))
+                nc.tensor.transpose(bank[:, columns(b, P)], rows[:, columns(BLOCKS * c + b, P)], ident[:])
 
-        def difference(s, held):
+        def turn_plan(s, free):
+            rows = loads.tile([P, T2], F32, name="rows")
+            nc.sync.dma_start(rows[:], plan[columns(s, P), :])
+            for c in range(CHUNKS):
+                turn_chunk(rows, c, free[c])
+                nc.scalar.copy(*by_pairs(turned[s % 2][:, columns(c)], free[c]))
+
+        def turn_pages(s):
             for c in range(CHUNKS):
                 for page in (page_a, page_b):
                     for b in range(BLOCKS):
-                        m0 = c * BANK + b * P
                         nc.tensor.matmul(
-                            held[c][:, b * P : (b + 1) * P],
-                            lhsT=page[s % 2][:, m0 : m0 + P],
+                            sum_banks[c][:, columns(b, P)],
+                            lhsT=page[s % 2][:, columns(BLOCKS * c + b, P)],
                             rhs=ident[:],
                             is_transpose=True,
                             start=(page is page_a and b == 0),
                             stop=(page is page_b and b == BLOCKS - 1),
                         )
 
-        def by_pairs(out_ap, bank):
-            return out_ap.rearrange("m (u w e) -> m u w e", u=2, e=2), bank[:].rearrange("m (w u e) -> m u w e", u=2, e=2)
+        def square(target, c):
+            nc.scalar.activation(*by_pairs(target[:, columns(c)], sum_banks[c]), ACT.Square)
 
-        def square(s, c, bank):
-            nc.scalar.activation(*by_pairs(piece(s, c), bank), ACT.Square)
-
-        def damping(s, chunks):
+        def damping(target, chunks):
             for c in chunks:
-                nc.scalar.activation(piece(s, c), piece(s, c), ACT.Abs_reciprocal_sqrt, bias=ROOT * ROOT, scale=ROOT * ROOT)
+                x = target[:, columns(c)]
+                nc.scalar.activation(x, x, ACT.Abs_reciprocal_sqrt, bias=ROOT * ROOT, scale=ROOT * ROOT)
             for c in chunks:
-                nc.scalar.activation(piece(s, c), piece(s, c), ACT.Square, scale=ROOT)
+                x = target[:, columns(c)]
+                nc.scalar.activation(x, x, ACT.Square, scale=ROOT)
 
-        def in_order(ap):
-            return ap.rearrange("m (g w) -> m g w", w=64)
-
-        def damp_plan(s, c, engine):
-            a, q = divmod(s, 4)
+        def damp_plan(engine, s, factors, z_part, cols):
             engine.tensor_tensor(
-                z_t[a][c][:, :, :, 64 * q : 64 * (q + 1)].rearrange("m u b w -> m (u b) w"),
-                in_order(turned[s % 2][:, c * BANK : (c + 1) * BANK]),
-                in_order(piece(s, c)),
+                z_part[:, :, columns(s % 4, RUN)],
+                turned[s % 2][:, cols].rearrange("m (g w) -> m g w", w=RUN),
+                factors[:, cols].rearrange("m (g w) -> m g w", w=RUN),
                 MULT,
             )
 
-        def quantise_z(a, first, count, free, copy):
-            grouped = groups.tile([P, count * BANK, 4], BF16, name="z_grouped", align_bytes=64)
-            grouped_words = grouped[:].rearrange("p m t -> p (m t)").bitcast(F32)
-            for i in range(2 * count):
-                words = z_t[a][first + i // 2][:].rearrange("m u b w -> m (u b w)").bitcast(F32)
+        def turn_back(z_chunk, grouped, pair, copies):
+            words = z_chunk.rearrange("m u b w -> m (u b w)").bitcast(F32)
+            for h in range(2):
                 for u in range(2):
                     for j in range(2):
-                        w0 = (u * BLOCKS + 2 * (i % 2) + j) * P
-                        nc.tensor.transpose(free[i][:, (2 * u + j) * P : (2 * u + j + 1) * P], words[:, w0 : w0 + P], ident[:])
-                copy(
-                    grouped_words[:, i * BANK : (i + 1) * BANK].rearrange("p (m u) -> p m u", u=2),
-                    free[i][:].rearrange("p (u m) -> p m u", u=2),
+                        source = words[:, columns(u * BLOCKS + 2 * h + j, P)]
+                        nc.tensor.transpose(pair[h][:, columns(2 * u + j, P)], source, ident[:])
+                copies[h](
+                    grouped[:, columns(h)].rearrange("p (m u) -> p m u", u=2),
+                    pair[h][:].rearrange("p (u m) -> p m u", u=2),
                 )
-            cols = slice(first * BANK, (first + count) * BANK)
-            nc.vector.quantize_mx(
-                out=z_w[a][:, cols].bitcast(FP8X4), scales=z_s[a][:, cols], in_=grouped[:].rearrange("p m t -> p (m t)")
-            )
 
-        def last_damping(i, bank):
-            cols = slice(EDGES[i], EDGES[i + 1])
-            c, first = divmod(EDGES[i] // P, BLOCKS)
-            blocks = (EDGES[i + 1] - EDGES[i]) // P
-            total = turned[0][:, cols]
-            nc.vector.tensor_tensor(total, page_a[last % 2][:, cols], page_b[last % 2][:, cols], ADD)
-            for b in range(blocks):
-                nc.tensor.transpose(bank[:, b * P : (b + 1) * P], total[:, b * P : (b + 1) * P], ident[:])
-            values = work[last % 3][:, cols]
-            nc.scalar.activation(
-                values.rearrange("m (u w e) -> m u w e", u=2, e=2),
-                bank[:, 0 : blocks * P].rearrange("m (w u e) -> m u w e", u=2, e=2),
-                ACT.Square,
-            )
-            nc.scalar.activation(values, values, ACT.Abs_reciprocal_sqrt, bias=ROOT * ROOT, scale=ROOT * ROOT)
-            nc.scalar.activation(values, values, ACT.Square, scale=ROOT)
-            plan_part = turned[last % 2][:, c * BANK : (c + 1) * BANK].rearrange("m (u b w) -> m u b w", u=2, w=64)
-            MENG(nc, i).tensor_tensor(
-                z_t[1][c][:, :, first : first + blocks, 192:256],
-                plan_part[:, :, first : first + blocks, :],
-                values.rearrange("m (u b w) -> m u b w", u=2, w=64),
-                MULT,
-            )
-
-        def last_quantise(i, free):
-            cols = slice(EDGES[i], EDGES[i + 1])
-            c, first = divmod(EDGES[i] // P, BLOCKS)
-            blocks = (EDGES[i + 1] - EDGES[i]) // P
-            grouped = groups.tile([P, blocks * P, 4], BF16, name="z_grouped", align_bytes=64)
+        def turn_back_first_pass(half, free):
+            grouped = firsts.tile([P, S, 4], BF16, name="first_grouped", align_bytes=64)
             grouped_words = grouped[:].rearrange("p m t -> p (m t)").bitcast(F32)
-            words = z_t[1][c][:].rearrange("m u b w -> m (u b w)").bitcast(F32)
-            for h in range(blocks // 2):
-                k = EDGES[i] // 256 + h
-                bank = free[k % 2]
-                for u in range(2):
-                    for j in range(2):
-                        w0 = (u * BLOCKS + first + 2 * h + j) * P
-                        nc.tensor.transpose(bank[:, (2 * u + j) * P : (2 * u + j + 1) * P], words[:, w0 : w0 + P], ident[:])
-                WCOPY(nc, k)(
-                    grouped_words[:, h * BANK : (h + 1) * BANK].rearrange("p (m u) -> p m u", u=2),
-                    bank[:].rearrange("p (u m) -> p m u", u=2),
-                )
+            for c in range(2):
+                turn_back(z_t[0][half][:, c], grouped_words[:, columns(c, S)], free[columns(c, 2)], [nc.scalar.copy] * 2)
+            return grouped
+
+        def quantise_first_pass(half):
             nc.vector.quantize_mx(
-                out=z_w[1][:, cols].bitcast(FP8X4), scales=z_s[1][:, cols], in_=grouped[:].rearrange("p m t -> p (m t)")
+                out=z_w[0][half][:].bitcast(FP8X4),
+                scales=z_s[0][:, columns(half, S)],
+                in_=first_pass[half][:].rearrange("p m t -> p (m t)"),
             )
 
-        def products(i, free):
-            cols = slice(EDGES[i], EDGES[i + 1])
-            width = EDGES[i + 1] - EDGES[i]
-            tiles = BANK // width
-            for g in range(N // P // tiles):
-                k = EDGES[i] // P + g
-                bank = free[k % 4]
+        def codes(a, c):
+            return z_w[a][c // 2][:, columns(c % 2)].bitcast(FP8X4)
+
+        def quantise_second_pass(c, pair):
+            grouped = seconds.tile([P, BANK, 4], BF16, name="second_grouped", align_bytes=64)
+            flat = grouped[:].rearrange("p m t -> p (m t)")
+            turn_back(z_t[1][c // 2][:, c % 2], flat.bitcast(F32), pair, [nc.scalar.copy, nc.vector.tensor_copy])
+            nc.vector.quantize_mx(out=codes(1, c), scales=z_s[1][:, columns(c)], in_=flat)
+
+        def last_product(c, free):
+            for n in range(N // P):
+                bank = free[(BLOCKS * c + n) % len(free)]
                 for a in range(2):
-                    for j in range(tiles):
-                        n = tiles * g + j
-                        nc.tensor.matmul_mx(
-                            out=bank[:, j * width : (j + 1) * width],
-                            lhsT=w8_w[:, a, n * P : (n + 1) * P].bitcast(FP8X4),
-                            lhsT_scale=w8_s[:, a, n * P : (n + 1) * P],
-                            rhs=z_w[a][:, cols].bitcast(FP8X4),
-                            rhs_scale=z_s[a][:, cols],
-                            start=(a, j) == (0, 0),
-                            stop=(a, j) == (1, tiles - 1),
-                        )
-                staged = stores.tile([P, tiles, width], F32, name="staged")
-                OCOPY(nc, i, k % 2)(staged[:].rearrange("p j m -> p (j m)"), bank[:])
-                rows = slice(tiles * g * P, tiles * (g + 1) * P)
-                nc.sync.dma_start(out[rows, cols].rearrange("(j p) m -> p j m", p=P), staged[:])
+                    nc.tensor.matmul_mx(
+                        out=bank[:],
+                        lhsT=w8_w[:, a, columns(n, P)].bitcast(FP8X4),
+                        lhsT_scale=w8_s[:, a, columns(n, P)],
+                        rhs=codes(a, c),
+                        rhs_scale=z_s[a][:, columns(c)],
+                        start=(a == 0),
+                        stop=(a == 1),
+                    )
+                staged = stores.tile([P, BANK], F32, name="staged")
+                (nc.vector.tensor_copy, nc.scalar.copy)[n % 2](staged[:], bank[:])
+                nc.sync.dma_start(out[columns(n, P), columns(c)], staged[:])
 
-        last = SLICES - 1
-        quantise_w1(0)
+        nc.gpsimd.memset(tab_s[:].bitcast(I32), 0)
+        nc.gpsimd.memset(w4_s[:].bitcast(I32), 0)
+        for page in (page_a[0], page_b[0], page_a[1], page_b[1]):
+            nc.vector.memset(page[:].bitcast(I32), 0)
+        make_identity(nc, ident[:])
+        nc.gpsimd.memset(w8_s[:].rearrange("p a n -> p (a n)").bitcast(I32), 0)
+
+        for tile, entries in ((list_tab, offs), (list_a, offs2), (list_b, offs3)):
+            nc.sync.dma_start(tile[:], entries)
+        load_plane(tab_s, tab_scales[0])
+        quantise_w1(keep, W1_PIECES[0])
         table_words = tab_words[0].rearrange("p n t -> p (n t)").bitcast(I32)
         for half in range(2):
-            cols = slice(half * (T // 2), (half + 1) * (T // 2))
-            nc.sync.dma_start(tab_w[:, cols], table_words[:, cols])
-        gather(0)
-        gather(1)
+            nc.sync.dma_start(tab_w[:, columns(half, T // 2)], table_words[:, columns(half, T // 2)])
         for half in range(2):
-            nc.sync.dma_start(gain_a[:, half * BANK : (half + 1) * BANK], wg1[:, half * BANK : (half + 1) * BANK])
+            entries = list_tab[:, columns(half, LIST_HALF)]
+            nc.vector.tensor_copy(v_w[:, columns(half)], tab_w[:].bitcast(U32).indirect(entries))
+            nc.vector.tensor_copy(v_s[:, columns(half)], tab_s[:].indirect(entries))
+        quantise_w1(loads, W1_PIECES[1])
+        for half in range(2):
+            nc.sync.dma_start(gain[0][:, columns(half)], wg1[:, columns(half)])
         nc.sync.dma_start(w4_w[:].bitcast(I32), w4_words[0].bitcast(I32))
-        for q in range(4):
-            nc.sync.dma_start(w4_s[32 * q : 32 * q + 4, :].bitcast(I32), w4_scales[0, 4 * q : 4 * q + 4, :].bitcast(I32))
-        nc.sync.dma_start(gain_b[:], wg2)
-        for j in range(4):
-            features(0, j, inner[j])
-            place_half(0, j)
-        for g in range(1, len(W1_PIECES) - 1):
-            quantise_w1(g)
-        for j in range(4):
-            features(1, j, inner[(j + 2) % 4])
+        load_plane(w4_s, w4_scales[0])
+        nc.sync.dma_start(gain[1][:], wg2)
+
+        for half in range(2):
+            product(0, half, sum_banks[half])
+            nc.vector.tensor_tensor(work[0][:, columns(half)], sum_banks[half][:], gain[0][:, columns(half)], MULT)
+        features(0, 1, sum_banks[0:2])
+        scatter(0)
+        quantise_w1(loads, W1_PIECES[2])
+        for side in range(2):
+            features(1, side, sum_banks[0:2])
         scatter(1)
         nc.sync.dma_start(w8_w[:], w8_words.rearrange("a p n t -> p a (n t)").bitcast(I32))
-        for q in range(4):
-            nc.sync.dma_start(
-                w8_s[32 * q : 32 * q + 4, :, :].bitcast(I32),
-                w8_scales[:, 4 * q : 4 * q + 4, :].rearrange("a r n -> r a n").bitcast(I32),
-            )
+        load_plane(w8_s, w8_scales.rearrange("a r n -> r a n"))
 
+        def damp_half(engine, s, half):
+            damping(work[s % 3], range(2 * half, 2 * half + 2))
+            z_part = z_t[s // 4][half][:].rearrange("m c u b w -> m (c u b) w")
+            damp_plan(engine, s, work[s % 3], z_part, columns(half, S))
 
-        for s in range(SLICES):
-            rows = load_plan(s)
+        first_pass = []
+        for s in range(LAST - 1):
+            turn_plan(s, plan_banks if s > 0 else sum_banks)
+            turn_pages(s)
             for c in range(CHUNKS):
-                turn_plan(s, rows, c, outer[c])
-            if s == last:
-                break
-            difference(s, inner)
-            for c in range(CHUNKS):
-                square(s, c, inner[c])
-            if s in (4, 5):
-                quantise_z(0, 2 * (s - 4), 2, outer, nc.scalar.copy)
-            if s + 2 < SLICES:
-                for j in range(4):
-                    features(s + 2, j, inner[j])
-                scatter(s + 2)
-            damping(s, range(0, 2))
-            damping(s, range(2, 4))
-            for c in range(CHUNKS):
-                damp_plan(s, c, nc.gpsimd)
+                square(work[s % 3], c)
+            if s + 2 == LAST:
+                first_pass.append(turn_back_first_pass(0, plan_banks))
+            for side in range(2):
+                features(s + 2, side, sum_banks[columns(side, 2)])
+            scatter(s + 2)
+            for half in range(2):
+                damp_half(nc.gpsimd, s, half)
 
-        for step in range(UNITS + DP):
-            if step < UNITS:
-                last_damping(step, inner[step % 2])
-            if step >= DP:
-                products(step - DP, outer)
-            if DQ <= step < UNITS + DQ:
-                last_quantise(step - DQ, inner[2:4])
+        s = LAST - 1
+        turn_plan(s, plan_banks)
+        turn_pages(s)
+        for half, engine in enumerate((nc.gpsimd, nc.vector)):
+            for c in range(2 * half, 2 * half + 2):
+                square(work[s % 3], c)
+            damp_half(engine, s, half)
+        first_pass.append(turn_back_first_pass(1, sum_banks))
+        turn_plan(LAST, plan_banks)
+
+        last_work = work[(LAST + 1) % 3]
+        for c in range(CHUNKS):
+            cols = columns(c)
+            nc.vector.tensor_tensor(last_work[:, cols], page_a[LAST % 2][:, cols], page_b[LAST % 2][:, cols], ADD)
+        z_w[0].append(keep.tile([P, S], U32, name="z_w00", tag=f"page_a{LAST % 2}", align_bytes=64))
+        z_w[0].append(keep.tile([P, S], U32, name="z_w01", tag=f"turned{(LAST - 1) % 2}", align_bytes=64))
+        quantise_first_pass(0)
+        out_banks = plan_banks[2:4] + sum_banks[1:4] + sum_banks[0:1]
+        for step in range(CHUNKS + 3):
+            if step == CHUNKS - 1:
+                quantise_first_pass(1)
+            if step < CHUNKS:
+                turn_chunk(last_work, step, sum_banks[step])
+                square(last_work, step)
+                damping(last_work, [step])
+                z_part = z_t[1][step // 2][:, step % 2].rearrange("m u b w -> m (u b) w")
+                damp_plan(nc.vector, LAST, last_work, z_part, columns(step))
+            if step >= 3:
+                last_product(step - 3, out_banks)
+            if 1 <= step <= CHUNKS:
+                quantise_second_pass(step - 1, plan_banks[0:2])

@@ -135,8 +135,8 @@ def tile_list_trap_bench_release_kernel(
                 nc.scalar.copy(*by_pairs(turned[s % 2][:, columns(c)], free[c]))
 
         def turn_pages(s):
-            for c in range(CHUNKS):
-                for page in (page_a, page_b):
+            for page in (page_a, page_b):
+                for c in range(CHUNKS):
                     for b in range(BLOCKS):
                         nc.tensor.matmul(
                             sum_banks[c][:, columns(b, P)],
@@ -262,10 +262,13 @@ def tile_list_trap_bench_release_kernel(
 
         first_pass = []
         for s in range(LAST - 1):
-            turn_plan(s, plan_banks if s > 0 else sum_banks)
+            if s == 0:
+                turn_plan(s, sum_banks)
             turn_pages(s)
             for c in range(CHUNKS):
                 square(work[s % 3], c)
+            if s > 0:
+                turn_plan(s, plan_banks)
             if s + 2 == LAST:
                 first_pass.append(turn_back_first_pass(0, plan_banks))
             for side in range(2):

@@ -24,9 +24,9 @@ SLICES = H // P
 LAST = SLICES - 1
 CHUNKS = T2 // BANK
 BLOCKS = BANK // P
-RUN = P // 2
 LIST_HALF = BANK // 16
-W1_PIECES = ([(0, 128)], [(128, 256), (256, 512)], [(512, 1024)])
+LAG = 2
+ON_VECTOR = 3
 ROOT = 75.0 / 64.0
 
 
@@ -36,275 +36,307 @@ def tile_list_trap_bench_release_kernel(
     nc = tc.nc
     with ExitStack() as ctx:
         keep = ctx.enter_context(tc.tile_pool(name="keep", bufs=1))
-        loads = ctx.enter_context(tc.tile_pool(name="loads", bufs=2))
-        firsts = ctx.enter_context(tc.tile_pool(name="firsts", bufs=2))
-        seconds = ctx.enter_context(tc.tile_pool(name="seconds", bufs=3))
-        stores = ctx.enter_context(tc.tile_pool(name="stores", bufs=8))
         psum = ctx.enter_context(tc.psum_pool(name="psum", bufs=1))
-
         banks = [psum.tile([P, BANK], F32, name=f"bank{b}") for b in range(8)]
-        plan_banks = banks[0:2] + banks[6:8]
-        sum_banks = banks[2:6]
-
-        list_tab = keep.tile([P, S // 16], U16, name="list_tab")
-        list_a = keep.tile([P, S // 16], U16, name="list_a")
-        list_b = keep.tile([P, S // 16], U16, name="list_b")
-        tab_w = keep.tile([P, T], I32, name="tab_w", align_bytes=64)
-        tab_s = keep.tile([P, T], U8, name="tab_s", align_bytes=64)
-        v_w = keep.tile([P, S], U32, name="v_w", align_bytes=64)
-        v_s = keep.tile([P, S], U8, name="v_s", align_bytes=64)
-        w1_w = keep.tile([P, H], U32, name="w1_w", align_bytes=64)
-        w4_w = keep.tile([P, 2 * H], U8, name="w4_w", align_bytes=64)
-        w4_s = keep.tile([P, H], U8, name="w4_s", align_bytes=64)
-        w8_w = keep.tile([P, 2, N], I32, name="w8_w", align_bytes=64)
-        w8_s = keep.tile([P, 2, N], U8, name="w8_s", align_bytes=64)
-        gain = [keep.tile([P, S], F32, name=f"gain{i}") for i in range(2)]
-        ident = keep.tile([P, P], F32, name="ident")
-        page_a = [keep.tile([P, T2], F32, name=f"page_a{i}", align_bytes=64) for i in range(2)]
-        page_b = [keep.tile([P, T2], F32, name=f"page_b{i}") for i in range(2)]
-        work = [keep.tile([P, T2], F32, name=f"work{i}") for i in range(3)]
-        turned = [keep.tile([P, T2], F32, name=f"turned{i}", align_bytes=64) for i in range(2)]
-        z_t = [[keep.tile([P, 2, 2, BLOCKS, 2 * P], BF16, name=f"z_t{a}{h}") for h in range(2)] for a in range(2)]
-        z_w = [[], [keep.tile([P, S], U32, name=f"z_w1{h}", align_bytes=64) for h in range(2)]]
-        z_s = [keep.tile([P, T2], U8, name=f"z_s{a}", align_bytes=64) for a in range(2)]
-        w1_s = keep.tile([P, H], U8, name="w1_s", align_bytes=64)
-
-        def load_plane(plane, rows):
-            for q in range(4):
-                nc.sync.dma_start(plane[32 * q : 32 * q + 4].bitcast(I32), rows[4 * q : 4 * q + 4].bitcast(I32))
-
-        def quantise_w1(pool, ranges):
-            first, end = ranges[0][0], ranges[-1][1]
-            width = end - first
-            raw = pool.tile([P, 4, width], F32, name="rows")
-            nc.sync.dma_start(raw[:], w1[:, first:end].rearrange("(p t) c -> p t c", t=4))
-            grouped = keep.tile([P, width, 4], BF16, name=f"w1_grouped{first}", align_bytes=64)
-            nc.scalar.copy(
-                grouped[:].rearrange("p (c i) t -> p c t i", i=4),
-                raw[:].rearrange("p t (c i) -> p c t i", i=4),
-            )
-            for start, stop in ranges:
-                nc.vector.quantize_mx(
-                    out=w1_w[:, start:stop].bitcast(FP8X4),
-                    scales=w1_s[:, start:stop],
-                    in_=grouped[:, start - first : stop - first, :].rearrange("p c t -> p (c t)"),
-                )
 
         def columns(i, width=BANK):
             return slice(i * width, (i + 1) * width)
 
-        def product(s, j, bank):
-            if j < 2:
-                weights, plane = w1_w[:, columns(s, P)].bitcast(FP8X4), w1_s
+        def tile(shape, dtype, name, tag=None):
+            return keep.tile(shape, dtype, name=name, tag=tag or name, align_bytes=64)
+
+        list_tab = tile([P, S // 16], U16, "list_tab")
+        list_a = tile([P, S // 16], U16, "list_a")
+        list_b = tile([P, S // 16], U16, "list_b")
+        tab_w = tile([P, T], I32, "tab_w", tag="rows0")
+        tab_s = tile([P, T], U8, "tab_s")
+        v_w = tile([P, S], U32, "v_w")
+        v_s = tile([P, S], U8, "v_s")
+        w1_w = tile([P, H], U32, "w1_w")
+        w1_s = tile([P, H], U8, "w1_s")
+        w4_raw_w = tile([P, 2 * H], U8, "w4_raw_w")
+        w4_raw_s = tile([P, H], U8, "w4_raw_s")
+        w4_dealt = []
+        w8_w = tile([P, 2, N], I32, "w8_w")
+        w8_s = tile([P, 2, N], U8, "w8_s")
+        gain_a = [tile([P, S], F32, f"gain_a{t}") for t in range(4)]
+        gain_b = [tile([P, S], F32, f"gain_b{t}") for t in range(4)]
+        ident = tile([P, P], F32, "ident")
+        works = tile([P, 5 * S], F32, "works")
+        h_b = [works[:, columns(i, S)] for i in range(3)]
+
+        def factor(s, first, count=1):
+            half = h_b[s % 3] if first < 2 else works[:, columns(3 + s % 2, S)]
+            return half[:, (first % 2) * BANK : (first % 2 + count) * BANK]
+
+        first_rows = [tile([P, S], F32, "first_rows0", tag="w4_late_s"), tile([P, S], F32, "first_rows1", tag="w4_late")]
+        h_a = [tile([P, S], F32, f"h_a{i}") for i in range(2)]
+
+        def a_values(s):
+            return h_a[0 if s < 2 else (s + 1) % 2]
+
+        w1_raw = [tile([P, T2], F32, "w1_raw0", tag="rows1")[:], works[:, 2 * S : 4 * S]]
+        w1_first = tile([P, BANK], BF16, "w1_first", tag="page_b1")
+        page_b = [tile([P, T2], F32, "page_b0")]
+        page_a = [tile([P, T2], F32, "page_a0")]
+        squares = [tile([P, BANK], F32, f"squares{i}") for i in range(3)]
+        pairs = [tile([P, 4 * T2], BF16, f"pairs{a}") for a in range(2)]
+        rows = []
+        first_grouped = tile([P, 4 * T2], BF16, "first_grouped")
+        second_grouped = [tile([P, 4 * BANK], BF16, f"second_grouped{i}") for i in range(2)]
+
+        def load_plane(plane, src_rows):
+            for q in range(4):
+                nc.sync.dma_start(plane[32 * q : 32 * q + 4].bitcast(I32), src_rows[4 * q : 4 * q + 4].bitcast(I32))
+
+        def load_gain(target, wg, t, cols=slice(0, S)):
+            dealt = wg.rearrange("(p t) j -> t p j", t=4)[t]
+            for q in range(4):
+                nc.sync.dma_start(target[t][32 * q : 32 * q + 32, cols], dealt[:, cols])
+
+        def clear(page):
+            for c in range(CHUNKS):
+                nc.gpsimd.memset(page[:, columns(c)].bitcast(I32), 0)
+
+        def deal_w4(a, t0, t1, name):
+            count = t1 - t0
+            words = tile([P, count * 2 * P], U8, name)
+            plane = tile([P, count * P], U8, name + "_s")
+            nc.gpsimd.tensor_copy(
+                words[:].rearrange("p (t m e) -> p t m e", m=P, e=2),
+                w4_raw_w[:, columns(a, H)].rearrange("p (m t e) -> p t m e", t=4, e=2)[:, t0:t1],
+            )
+            nc.gpsimd.tensor_copy(
+                plane[:].rearrange("p (t m) -> p t m", m=P),
+                w4_raw_s[:, columns(a)].rearrange("p (m t) -> p t m", t=4)[:, t0:t1],
+            )
+            for t in range(count):
+                w4_dealt.append((words[:, columns(t, 2 * P)], plane[:, columns(t, P)]))
+
+        def load_w1(a):
+            nc.sync.dma_start(w1_raw[a].rearrange("p (j c) -> p j c", j=4), w1[:, columns(a)].rearrange("(p j) c -> p j c", j=4))
+
+        def quantise_w1(a, t0, t1, grouped, cuts):
+            nc.scalar.copy(
+                grouped.rearrange("p (t m j) -> p m j t", m=P, j=4),
+                w1_raw[a].rearrange("p (j m t) -> p m j t", j=4, t=4)[:, :, :, t0:t1],
+            )
+            for start, stop in cuts:
+                cols = slice((4 * a + start) * P, (4 * a + stop) * P)
+                nc.vector.quantize_mx(
+                    out=w1_w[:, cols].bitcast(FP8X4),
+                    scales=w1_s[:, cols],
+                    in_=grouped[:, (start - t0) * BANK : (stop - t0) * BANK],
+                )
+
+        def product(s, side, half, bank):
+            if side == 0:
+                weights, plane = w1_w[:, columns(s, P)].bitcast(FP8X4), w1_s[:, columns(s, P)]
             else:
-                weights, plane = w4_w[:, columns(s, 2 * P)].bitcast(FP4X4), w4_s
+                weights, plane = w4_dealt[s][0].bitcast(FP4X4), w4_dealt[s][1]
             nc.tensor.matmul_mx(
                 out=bank[:],
                 lhsT=weights,
-                lhsT_scale=plane[:, columns(s, P)],
-                rhs=v_w[:, columns(j % 2)].bitcast(FP8X4),
-                rhs_scale=v_s[:, columns(j % 2)],
+                lhsT_scale=plane,
+                rhs=v_w[:, columns(half)].bitcast(FP8X4),
+                rhs_scale=v_s[:, columns(half)],
                 start=True,
                 stop=True,
             )
 
-        def features(s, side, pair):
+        def feature_half(s, side, half, target, bank):
+            product(s, side, half, bank)
+            nc.scalar.activation(target, bank[:], ACT.Copy, scale=(-1.0, 1.0)[side])
+
+        def features(s, side):
+            values = (a_values(s)[:], h_b[s % 3])[side]
             for half in range(2):
-                j = 2 * side + half
-                product(s, j, pair[half])
-                nc.scalar.activation(work[s % 3][:, columns(j)], pair[half][:], ACT.Copy, scale=(1.0, -1.0)[side])
-            values = work[s % 3][:, columns(side, S)]
-            nc.gpsimd.tensor_tensor(values, values, gain[side][:], MULT)
+                feature_half(s, side, half, values[:, columns(half)], banks[half])
+            nc.gpsimd.tensor_tensor(values, values, (gain_a, gain_b)[side][s % 4][:], MULT)
 
-        def scatter(s):
-            nc.vector.tensor_copy(page_a[s % 2][:].indirect(list_a[:]), work[s % 3][:, columns(0, S)])
-            nc.vector.tensor_copy(page_b[s % 2][:].indirect(list_b[:]), work[s % 3][:, columns(1, S)])
+        def scatter_a(s):
+            nc.vector.tensor_copy(page_a[s % 2][:].indirect(list_a[:]), a_values(s)[:])
 
-        def by_pairs(target, bank):
-            return target.rearrange("m (u w e) -> m u w e", u=2, e=2), bank[:].rearrange("m (w u e) -> m u w e", u=2, e=2)
+        def scatter_b(s):
+            nc.vector.tensor_copy(page_b[s % 2][:].indirect(list_b[:]), h_b[s % 3])
 
-        def turn_chunk(rows, c, bank):
+        def load_plan(s):
+            nc.sync.dma_start(rows[s % 2][:], plan.rearrange("(a p t) m -> a t p m", a=2, t=4)[s // 4, s % 4])
+
+        def turn_pages(s, c):
+            bank = banks[((7, 0, 7, 0) if s == LAST - 1 else (7, 0, 1, 0))[c]]
+            for page in (page_b[s % 2], page_a[s % 2]):
+                for b in range(BLOCKS):
+                    nc.tensor.matmul(
+                        bank[:, columns(b, P)],
+                        lhsT=page[:, columns(BLOCKS * c + b, P)],
+                        rhs=ident[:],
+                        is_transpose=True,
+                        start=(page is page_b[s % 2] and b == 0),
+                        stop=(page is page_a[s % 2] and b == BLOCKS - 1),
+                    )
+            nc.scalar.activation(squares[(CHUNKS * s + c) % 3][:], bank[:], ACT.Square)
+
+        def turn_back(s, c):
+            bank = banks[(5 if s == LAST - 1 else 6) + c % 2]
             for b in range(BLOCKS):
-                nc.tensor.transpose(bank[:, columns(b, P)], rows[:, columns(BLOCKS * c + b, P)], ident[:])
+                nc.tensor.transpose(bank[:, columns(b, P)], squares[(CHUNKS * s + c) % 3][:, columns(b, P)], ident[:])
+            nc.scalar.activation(
+                factor(s, c), bank[:], ACT.Abs_reciprocal_sqrt, bias=ROOT * ROOT, scale=ROOT * ROOT
+            )
 
-        def turn_plan(s, free):
-            rows = loads.tile([P, T2], F32, name="rows")
-            nc.sync.dma_start(rows[:], plan[columns(s, P), :])
-            for c in range(CHUNKS):
-                turn_chunk(rows, c, free[c])
-                nc.scalar.copy(*by_pairs(turned[s % 2][:, columns(c)], free[c]))
-
-        def turn_pages(s):
-            for page in (page_a, page_b):
-                for c in range(CHUNKS):
-                    for b in range(BLOCKS):
-                        nc.tensor.matmul(
-                            sum_banks[c][:, columns(b, P)],
-                            lhsT=page[s % 2][:, columns(BLOCKS * c + b, P)],
-                            rhs=ident[:],
-                            is_transpose=True,
-                            start=(page is page_a and b == 0),
-                            stop=(page is page_b and b == BLOCKS - 1),
-                        )
-
-        def square(target, c):
-            nc.scalar.activation(*by_pairs(target[:, columns(c)], sum_banks[c]), ACT.Square)
-
-        def damping(target, chunks):
-            for c in chunks:
-                x = target[:, columns(c)]
-                nc.scalar.activation(x, x, ACT.Abs_reciprocal_sqrt, bias=ROOT * ROOT, scale=ROOT * ROOT)
-            for c in chunks:
-                x = target[:, columns(c)]
-                nc.scalar.activation(x, x, ACT.Square, scale=ROOT)
-
-        def damp_plan(engine, s, factors, z_part, cols):
+        def damp_plan(engine, s, first, count, x):
+            cols = slice(first * BANK, (first + count) * BANK)
+            nc.scalar.activation(x, x, ACT.Square, scale=ROOT)
+            target = pairs[s // 4][:].rearrange("p (c u m e) -> p u e c m", u=2, m=BANK, e=2)
             engine.tensor_tensor(
-                z_part[:, :, columns(s % 4, RUN)],
-                turned[s % 2][:, cols].rearrange("m (g w) -> m g w", w=RUN),
-                factors[:, cols].rearrange("m (g w) -> m g w", w=RUN),
+                target[:, (s % 4) // 2, s % 2, first : first + count],
+                x.rearrange("p (c m) -> p c m", m=BANK),
+                (first_rows[first // 2][:] if s == 0 else rows[s % 2][:, cols]).rearrange("p (c m) -> p c m", m=BANK),
                 MULT,
             )
 
-        def turn_back(z_chunk, grouped, pair, copies):
-            words = z_chunk.rearrange("m u b w -> m (u b w)").bitcast(F32)
-            for h in range(2):
-                for u in range(2):
-                    for j in range(2):
-                        source = words[:, columns(u * BLOCKS + 2 * h + j, P)]
-                        nc.tensor.transpose(pair[h][:, columns(2 * u + j, P)], source, ident[:])
-                copies[h](
-                    grouped[:, columns(h)].rearrange("p (m u) -> p m u", u=2),
-                    pair[h][:].rearrange("p (u m) -> p m u", u=2),
-                )
+        def weave(copy, a, c, target):
+            source = pairs[a][:, columns(c, 4 * BANK)].bitcast(F32)
+            copy(target.bitcast(F32).rearrange("p (m u) -> p m u", u=2), source.rearrange("p (u m) -> p m u", u=2))
 
-        def turn_back_first_pass(half, free):
-            grouped = firsts.tile([P, S, 4], BF16, name="first_grouped", align_bytes=64)
-            grouped_words = grouped[:].rearrange("p m t -> p (m t)").bitcast(F32)
-            for c in range(2):
-                turn_back(z_t[0][half][:, c], grouped_words[:, columns(c, S)], free[columns(c, 2)], [nc.scalar.copy] * 2)
-            return grouped
+        def window(page, entries, half):
+            return page[:].indirect(entries[:, columns(half, LIST_HALF)])
 
-        def quantise_first_pass(half):
+        nc.vector.memset(tab_s[:].bitcast(I32), 0)
+        nc.vector.memset(w4_raw_s[:].bitcast(I32), 0)
+        nc.sync.dma_start(list_tab[:], offs)
+        load_plane(tab_s, tab_scales[0])
+        nc.sync.dma_start(w4_raw_w[:].bitcast(I32), w4_words[0].bitcast(I32))
+        nc.sync.dma_start(tab_w[:], tab_words[0].rearrange("p n t -> p (n t)").bitcast(I32))
+        load_plane(w4_raw_s, w4_scales[0])
+        nc.sync.dma_start(list_b[:], offs3)
+        load_gain(gain_b, wg2, 0, columns(0))
+        load_w1(0)
+        load_gain(gain_b, wg2, 0, columns(1))
+        nc.sync.dma_start(list_a[:], offs2)
+        load_gain(gain_a, wg1, 0, columns(0))
+        load_gain(gain_a, wg1, 0, columns(1))
+        load_w1(1)
+        load_gain(gain_b, wg2, 1)
+        load_gain(gain_a, wg1, 1)
+        page_a.append(tile([P, T2], F32, "page_a1"))
+        for page in (page_b[0], page_a[0], page_a[1]):
+            nc.vector.memset(page[:].bitcast(I32), 0)
+        make_identity(nc, ident[:])
+        nc.gpsimd.memset(w8_s[:].rearrange("p a n -> p (a n)").bitcast(I32), 0)
+        deal_w4(0, 0, 1, "w4_first")
+        deal_w4(0, 1, 4, "w4_next")
+        nc.vector.tensor_copy(v_s[:], tab_s[:].indirect(list_tab[:]))
+        for half in range(2):
+            entries = list_tab[:, columns(half, LIST_HALF)]
+            nc.vector.tensor_copy(v_w[:, columns(half)], tab_w[:].bitcast(U32).indirect(entries))
+
+        for half in range(2):
+            values = h_b[0][:, columns(half)]
+            feature_half(0, 1, half, values, banks[4 + half])
+            nc.vector.tensor_tensor(window(page_b[0], list_b, half), values, gain_b[0][:, columns(half)], MULT)
+            if half == 0:
+                quantise_w1(0, 0, 1, w1_first[:], [(0, 1)])
+        for half in range(2):
+            feature_half(0, 0, half, h_a[0][:, columns(half)], banks[4 + half])
+            nc.vector.tensor_tensor(window(page_a[0], list_a, half), h_a[0][:, columns(half)], gain_a[0][:, columns(half)], MULT)
+        w1_next = tile([P, 3 * BANK], BF16, "w1_next", tag="page_b1")
+        quantise_w1(0, 1, 4, w1_next[:], [(1, 2), (2, 4)])
+        page_b.append(tile([P, T2], F32, "page_b1"))
+        nc.gpsimd.memset(page_b[1][:].bitcast(I32), 0)
+        quantise_w1(1, 0, 4, h_b[1].bitcast(BF16), [(0, 4)])
+
+        product(1, 1, 0, banks[7])
+        nc.vector.tensor_tensor(h_b[1][:, columns(0)], banks[7][:], gain_b[1][:, columns(0)], MULT)
+        nc.vector.tensor_copy(window(page_b[1], list_b, 0), h_b[1][:, columns(0)])
+        values = h_b[1][:, columns(1)]
+        feature_half(1, 1, 1, values, banks[0])
+        nc.gpsimd.tensor_tensor(values, values, gain_b[1][:, columns(1)], MULT)
+        nc.vector.tensor_copy(window(page_b[1], list_b, 1), values)
+        for half in range(2):
+            values = h_a[0][:, columns(half)]
+            feature_half(1, 0, half, values, banks[(7, 0)[half]])
+            nc.gpsimd.tensor_tensor(values, values, gain_a[1][:, columns(half)], MULT)
+            nc.vector.tensor_copy(window(page_a[1], list_a, half), values)
+        rows.extend(tile([P, T2], F32, f"rows{i}") for i in range(2))
+        load_gain(gain_b, wg2, 2)
+        load_gain(gain_a, wg1, 2)
+        for half in range(2):
+            nc.sync.dma_start(first_rows[half][:], plan.rearrange("(p t) m -> t p m", t=4)[0, 0:P, columns(half, S)])
+        load_gain(gain_b, wg2, 3)
+        load_gain(gain_a, wg1, 3)
+
+        for s in range(LAST):
+            load_plan(s + 1)
+            if s == 1:
+                nc.sync.dma_start(w8_w[:], w8_words.rearrange("a p n t -> p a (n t)").bitcast(I32))
+                load_plane(w8_s, w8_scales.rearrange("a r n -> r a n"))
+            ahead = s + 2 <= LAST
+            if ahead:
+                features(s + 2, 1)
+                features(s + 2, 0)
+            for c in range(CHUNKS + 1):
+                if c < CHUNKS:
+                    turn_pages(s, c)
+                if c >= 1:
+                    turn_back(s, c - 1)
+                if c in (2, 4):
+                    damp_plan(nc.gpsimd, s, c - 2, 2, factor(s, c - 2, 2))
+            if ahead:
+                scatter_b(s + 2)
+                scatter_a(s + 2)
+            if s == 0:
+                deal_w4(1, 0, 4, "w4_late")
+            for c in {4: (0,), 5: (1,), 6: (2, 3)}.get(s, ()):
+                weave(nc.scalar.copy, 0, c, first_grouped[:, columns(c, 4 * BANK)])
+
+        z_w = [tile([P, T2], U32, "z_w0", tag="rows0"), tile([P, T2], U32, "z_w1", tag="page_b0")]
+        z_s = [tile([P, T2], U8, "z_s0", tag="h_a0"), tile([P, T2], U8, "z_s1")]
+
+        def first_codes(half):
             nc.vector.quantize_mx(
-                out=z_w[0][half][:].bitcast(FP8X4),
+                out=z_w[0][:, columns(half, S)].bitcast(FP8X4),
                 scales=z_s[0][:, columns(half, S)],
-                in_=first_pass[half][:].rearrange("p m t -> p (m t)"),
+                in_=first_grouped[:, columns(half, 4 * S)],
             )
 
-        def codes(a, c):
-            return z_w[a][c // 2][:, columns(c % 2)].bitcast(FP8X4)
-
-        def quantise_second_pass(c, pair):
-            grouped = seconds.tile([P, BANK, 4], BF16, name="second_grouped", align_bytes=64)
-            flat = grouped[:].rearrange("p m t -> p (m t)")
-            turn_back(z_t[1][c // 2][:, c % 2], flat.bitcast(F32), pair, [nc.scalar.copy, nc.vector.tensor_copy])
-            nc.vector.quantize_mx(out=codes(1, c), scales=z_s[1][:, columns(c)], in_=flat)
-
-        def last_product(c, free):
+        def last_product(c):
             for n in range(N // P):
-                bank = free[(BLOCKS * c + n) % len(free)]
+                bank = banks[(BLOCKS * c + n) % 8]
                 for a in range(2):
                     nc.tensor.matmul_mx(
                         out=bank[:],
                         lhsT=w8_w[:, a, columns(n, P)].bitcast(FP8X4),
                         lhsT_scale=w8_s[:, a, columns(n, P)],
-                        rhs=codes(a, c),
+                        rhs=z_w[a][:, columns(c)].bitcast(FP8X4),
                         rhs_scale=z_s[a][:, columns(c)],
                         start=(a == 0),
                         stop=(a == 1),
                     )
-                staged = stores.tile([P, BANK], F32, name="staged")
-                (nc.vector.tensor_copy, nc.scalar.copy)[n % 2](staged[:], bank[:])
-                nc.sync.dma_start(out[columns(n, P), columns(c)], staged[:])
+                staged = (gain_a + gain_b)[(BLOCKS * c + n) // 2][:, columns(n % 2)]
+                (nc.vector.tensor_copy if (n % 2 == 1 and 2 * c + n // 2 >= 8 - ON_VECTOR) else nc.scalar.copy)(staged, bank[:])
+                nc.sync.dma_start(out[columns(n, P), columns(c)], staged)
 
-        nc.gpsimd.memset(tab_s[:].bitcast(I32), 0)
-        nc.gpsimd.memset(w4_s[:].bitcast(I32), 0)
-        for page in (page_a[0], page_b[0], page_a[1], page_b[1]):
-            nc.vector.memset(page[:].bitcast(I32), 0)
-        make_identity(nc, ident[:])
-        nc.gpsimd.memset(w8_s[:].rearrange("p a n -> p (a n)").bitcast(I32), 0)
+        def last_factors(c):
+            x = factor(LAST - 1, c)
+            nc.vector.tensor_tensor(x, page_a[LAST % 2][:, columns(c)], page_b[LAST % 2][:, columns(c)], ADD)
+            nc.scalar.activation(x, x, ACT.Square)
+            nc.scalar.activation(x, x, ACT.Abs_reciprocal_sqrt, bias=ROOT * ROOT, scale=ROOT * ROOT)
 
-        for tile, entries in ((list_tab, offs), (list_a, offs2), (list_b, offs3)):
-            nc.sync.dma_start(tile[:], entries)
-        load_plane(tab_s, tab_scales[0])
-        quantise_w1(keep, W1_PIECES[0])
-        table_words = tab_words[0].rearrange("p n t -> p (n t)").bitcast(I32)
-        for half in range(2):
-            nc.sync.dma_start(tab_w[:, columns(half, T // 2)], table_words[:, columns(half, T // 2)])
-        for half in range(2):
-            entries = list_tab[:, columns(half, LIST_HALF)]
-            nc.vector.tensor_copy(v_w[:, columns(half)], tab_w[:].bitcast(U32).indirect(entries))
-            nc.vector.tensor_copy(v_s[:, columns(half)], tab_s[:].indirect(entries))
-        quantise_w1(loads, W1_PIECES[1])
-        for half in range(2):
-            nc.sync.dma_start(gain[0][:, columns(half)], wg1[:, columns(half)])
-        nc.sync.dma_start(w4_w[:].bitcast(I32), w4_words[0].bitcast(I32))
-        load_plane(w4_s, w4_scales[0])
-        nc.sync.dma_start(gain[1][:], wg2)
+        def second_codes(c):
+            damp_plan(nc.vector, LAST, c, 1, factor(LAST - 1, c))
+            weave(nc.vector.tensor_copy, 1, c, second_grouped[c % 2][:])
+            nc.vector.quantize_mx(
+                out=z_w[1][:, columns(c)].bitcast(FP8X4), scales=z_s[1][:, columns(c)], in_=second_grouped[c % 2][:]
+            )
 
-        for half in range(2):
-            product(0, half, sum_banks[half])
-            nc.vector.tensor_tensor(work[0][:, columns(half)], sum_banks[half][:], gain[0][:, columns(half)], MULT)
-        features(0, 1, sum_banks[0:2])
-        scatter(0)
-        quantise_w1(loads, W1_PIECES[2])
-        for side in range(2):
-            features(1, side, sum_banks[0:2])
-        scatter(1)
-        nc.sync.dma_start(w8_w[:], w8_words.rearrange("a p n t -> p a (n t)").bitcast(I32))
-        load_plane(w8_s, w8_scales.rearrange("a r n -> r a n"))
-
-        def damp_half(engine, s, half):
-            damping(work[s % 3], range(2 * half, 2 * half + 2))
-            z_part = z_t[s // 4][half][:].rearrange("m c u b w -> m (c u b) w")
-            damp_plan(engine, s, work[s % 3], z_part, columns(half, S))
-
-        first_pass = []
-        for s in range(LAST - 1):
-            if s == 0:
-                turn_plan(s, sum_banks)
-            turn_pages(s)
-            for c in range(CHUNKS):
-                square(work[s % 3], c)
-            if s > 0:
-                turn_plan(s, plan_banks)
-            if s + 2 == LAST:
-                first_pass.append(turn_back_first_pass(0, plan_banks))
-            for side in range(2):
-                features(s + 2, side, sum_banks[columns(side, 2)])
-            scatter(s + 2)
-            for half in range(2):
-                damp_half(nc.gpsimd, s, half)
-
-        s = LAST - 1
-        turn_plan(s, plan_banks)
-        turn_pages(s)
-        for half, engine in enumerate((nc.gpsimd, nc.vector)):
-            for c in range(2 * half, 2 * half + 2):
-                square(work[s % 3], c)
-            damp_half(engine, s, half)
-        first_pass.append(turn_back_first_pass(1, sum_banks))
-        turn_plan(LAST, plan_banks)
-
-        last_work = work[(LAST + 1) % 3]
-        for c in range(CHUNKS):
-            cols = columns(c)
-            nc.vector.tensor_tensor(last_work[:, cols], page_a[LAST % 2][:, cols], page_b[LAST % 2][:, cols], ADD)
-        z_w[0].append(keep.tile([P, S], U32, name="z_w00", tag=f"page_a{LAST % 2}", align_bytes=64))
-        z_w[0].append(keep.tile([P, S], U32, name="z_w01", tag=f"turned{(LAST - 1) % 2}", align_bytes=64))
-        quantise_first_pass(0)
-        out_banks = plan_banks[2:4] + sum_banks[1:4] + sum_banks[0:1]
-        for step in range(CHUNKS + 3):
-            if step == CHUNKS - 1:
-                quantise_first_pass(1)
+        for step in range(CHUNKS + LAG + 1):
             if step < CHUNKS:
-                turn_chunk(last_work, step, sum_banks[step])
-                square(last_work, step)
-                damping(last_work, [step])
-                z_part = z_t[1][step // 2][:, step % 2].rearrange("m u b w -> m (u b) w")
-                damp_plan(nc.vector, LAST, last_work, z_part, columns(step))
-            if step >= 3:
-                last_product(step - 3, out_banks)
+                last_factors(step)
             if 1 <= step <= CHUNKS:
-                quantise_second_pass(step - 1, plan_banks[0:2])
+                second_codes(step - 1)
+            if step in (1, 3):
+                first_codes(step // 2)
+            if step > LAG:
+                last_product(step - LAG - 1)

@@ -25,8 +25,7 @@ LAST = SLICES - 1
 CHUNKS = T2 // BANK
 BLOCKS = BANK // P
 LIST_HALF = BANK // 16
-LAG = 2
-ON_VECTOR = 3
+ON_VECTOR = (11, 13, 15)
 ROOT = 75.0 / 64.0
 
 
@@ -62,14 +61,14 @@ def tile_list_trap_bench_release_kernel(
         gain_a = [tile([P, S], F32, f"gain_a{t}") for t in range(4)]
         gain_b = [tile([P, S], F32, f"gain_b{t}") for t in range(4)]
         ident = tile([P, P], F32, "ident")
-        works = tile([P, 5 * S], F32, "works")
+        works = tile([P, 4 * S], F32, "works")
+        late = {}
         h_b = [works[:, columns(i, S)] for i in range(3)]
 
         def factor(s, first, count=1):
-            half = h_b[s % 3] if first < 2 else works[:, columns(3 + s % 2, S)]
+            half = h_b[s % 3] if first < 2 else late[s]
             return half[:, (first % 2) * BANK : (first % 2 + count) * BANK]
 
-        first_rows = [tile([P, S], F32, "first_rows0", tag="w4_late_s"), tile([P, S], F32, "first_rows1", tag="w4_late")]
         h_a = [tile([P, S], F32, f"h_a{i}") for i in range(2)]
 
         def a_values(s):
@@ -94,20 +93,22 @@ def tile_list_trap_bench_release_kernel(
             for q in range(4):
                 nc.sync.dma_start(target[t][32 * q : 32 * q + 32, cols], dealt[:, cols])
 
+        def load_gain_once(target, wg, t):
+            nc.sync.dma_start(target[t][:], wg.rearrange("(p t) j -> t p j", t=4)[t].partition_broadcast(4))
+
         def clear(page):
             for c in range(CHUNKS):
                 nc.gpsimd.memset(page[:, columns(c)].bitcast(I32), 0)
 
-        def deal_w4(a, t0, t1, name):
-            count = t1 - t0
-            words = tile([P, count * 2 * P], U8, name)
-            plane = tile([P, count * P], U8, name + "_s")
+        def deal_w4(s, spent):
+            a, t0, t1, count = s // 4, s % 4, s % 4 + 1, 1
+            words, plane = spent[:, 0 : 2 * P], spent[:, 2 * P : 3 * P]
             nc.gpsimd.tensor_copy(
-                words[:].rearrange("p (t m e) -> p t m e", m=P, e=2),
+                words.rearrange("p (t m e) -> p t m e", m=P, e=2),
                 w4_raw_w[:, columns(a, H)].rearrange("p (m t e) -> p t m e", t=4, e=2)[:, t0:t1],
             )
             nc.gpsimd.tensor_copy(
-                plane[:].rearrange("p (t m) -> p t m", m=P),
+                plane.rearrange("p (t m) -> p t m", m=P),
                 w4_raw_s[:, columns(a)].rearrange("p (m t) -> p t m", t=4)[:, t0:t1],
             )
             for t in range(count):
@@ -148,11 +149,12 @@ def tile_list_trap_bench_release_kernel(
             product(s, side, half, bank)
             nc.scalar.activation(target, bank[:], ACT.Copy, scale=(-1.0, 1.0)[side])
 
-        def features(s, side):
+        def feature_piece(s, piece):
+            side, half = 1 - piece // 2, piece % 2
             values = (a_values(s)[:], h_b[s % 3])[side]
-            for half in range(2):
-                feature_half(s, side, half, values[:, columns(half)], banks[half])
-            nc.gpsimd.tensor_tensor(values, values, (gain_a, gain_b)[side][s % 4][:], MULT)
+            feature_half(s, side, half, values[:, columns(half)], banks[half])
+            if half == 1:
+                nc.gpsimd.tensor_tensor(values, values, (gain_a, gain_b)[side][s % 4][:], MULT)
 
         def scatter_a(s):
             nc.vector.tensor_copy(page_a[s % 2][:].indirect(list_a[:]), a_values(s)[:])
@@ -164,7 +166,7 @@ def tile_list_trap_bench_release_kernel(
             nc.sync.dma_start(rows[s % 2][:], plan.rearrange("(a p t) m -> a t p m", a=2, t=4)[s // 4, s % 4])
 
         def turn_pages(s, c):
-            bank = banks[((7, 0, 7, 0) if s == LAST - 1 else (7, 0, 1, 0))[c]]
+            bank = banks[c % 2]
             for page in (page_b[s % 2], page_a[s % 2]):
                 for b in range(BLOCKS):
                     nc.tensor.matmul(
@@ -178,27 +180,29 @@ def tile_list_trap_bench_release_kernel(
             nc.scalar.activation(squares[(CHUNKS * s + c) % 3][:], bank[:], ACT.Square)
 
         def turn_back(s, c):
-            bank = banks[(5 if s == LAST - 1 else 6) + c % 2]
+            bank = banks[2 + c % 2]
             for b in range(BLOCKS):
                 nc.tensor.transpose(bank[:, columns(b, P)], squares[(CHUNKS * s + c) % 3][:, columns(b, P)], ident[:])
             nc.scalar.activation(
                 factor(s, c), bank[:], ACT.Abs_reciprocal_sqrt, bias=ROOT * ROOT, scale=ROOT * ROOT
             )
 
+        def finish(x):
+            nc.scalar.activation(x, x, ACT.Square, scale=ROOT)
+
         def damp_plan(engine, s, first, count, x):
             cols = slice(first * BANK, (first + count) * BANK)
-            nc.scalar.activation(x, x, ACT.Square, scale=ROOT)
             target = pairs[s // 4][:].rearrange("p (c u m e) -> p u e c m", u=2, m=BANK, e=2)
             engine.tensor_tensor(
                 target[:, (s % 4) // 2, s % 2, first : first + count],
                 x.rearrange("p (c m) -> p c m", m=BANK),
-                (first_rows[first // 2][:] if s == 0 else rows[s % 2][:, cols]).rearrange("p (c m) -> p c m", m=BANK),
+                rows[s % 2][:, cols].rearrange("p (c m) -> p c m", m=BANK),
                 MULT,
             )
 
-        def weave(copy, a, c, target):
-            source = pairs[a][:, columns(c, 4 * BANK)].bitcast(F32)
-            copy(target.bitcast(F32).rearrange("p (m u) -> p m u", u=2), source.rearrange("p (u m) -> p m u", u=2))
+        def weave(copy, a, c, target, part=slice(0, BANK)):
+            source = pairs[a][:, columns(c, 4 * BANK)].bitcast(F32).rearrange("p (u m) -> p m u", u=2)
+            copy(target.bitcast(F32).rearrange("p (m u) -> p m u", u=2)[:, part], source[:, part])
 
         def window(page, entries, half):
             return page[:].indirect(entries[:, columns(half, LIST_HALF)])
@@ -218,26 +222,27 @@ def tile_list_trap_bench_release_kernel(
         load_gain(gain_a, wg1, 0, columns(0))
         load_gain(gain_a, wg1, 0, columns(1))
         load_w1(1)
-        load_gain(gain_b, wg2, 1)
-        load_gain(gain_a, wg1, 1)
+        load_gain_once(gain_b, wg2, 1)
+        load_gain_once(gain_a, wg1, 1)
         page_a.append(tile([P, T2], F32, "page_a1"))
         for page in (page_b[0], page_a[0], page_a[1]):
             nc.vector.memset(page[:].bitcast(I32), 0)
         make_identity(nc, ident[:])
         nc.gpsimd.memset(w8_s[:].rearrange("p a n -> p (a n)").bitcast(I32), 0)
-        deal_w4(0, 0, 1, "w4_first")
-        deal_w4(0, 1, 4, "w4_next")
+        deal_w4(0, tile([P, 3 * P], U8, "w4_first")[:])
         nc.vector.tensor_copy(v_s[:], tab_s[:].indirect(list_tab[:]))
         for half in range(2):
             entries = list_tab[:, columns(half, LIST_HALF)]
             nc.vector.tensor_copy(v_w[:, columns(half)], tab_w[:].bitcast(U32).indirect(entries))
 
-        for half in range(2):
-            values = h_b[0][:, columns(half)]
-            feature_half(0, 1, half, values, banks[4 + half])
-            nc.vector.tensor_tensor(window(page_b[0], list_b, half), values, gain_b[0][:, columns(half)], MULT)
-            if half == 0:
-                quantise_w1(0, 0, 1, w1_first[:], [(0, 1)])
+        product(0, 1, 0, banks[4])
+        nc.vector.tensor_tensor(h_b[0][:, columns(0)], banks[4][:], gain_b[0][:, columns(0)], MULT)
+        nc.vector.tensor_copy(window(page_b[0], list_b, 0), h_b[0][:, columns(0)])
+        quantise_w1(0, 0, 1, w1_first[:], [(0, 1)])
+        values = h_b[0][:, columns(1)]
+        feature_half(0, 1, 1, values, banks[5])
+        deal_w4(1, tile([P, 3 * P], U8, "w4_second", tag="w4_first")[:])
+        nc.vector.tensor_tensor(window(page_b[0], list_b, 1), values, gain_b[0][:, columns(1)], MULT)
         for half in range(2):
             feature_half(0, 0, half, h_a[0][:, columns(half)], banks[4 + half])
             nc.vector.tensor_tensor(window(page_a[0], list_a, half), h_a[0][:, columns(half)], gain_a[0][:, columns(half)], MULT)
@@ -247,58 +252,66 @@ def tile_list_trap_bench_release_kernel(
         nc.gpsimd.memset(page_b[1][:].bitcast(I32), 0)
         quantise_w1(1, 0, 4, h_b[1].bitcast(BF16), [(0, 4)])
 
-        product(1, 1, 0, banks[7])
-        nc.vector.tensor_tensor(h_b[1][:, columns(0)], banks[7][:], gain_b[1][:, columns(0)], MULT)
+        product(1, 1, 0, banks[0])
+        nc.vector.tensor_tensor(h_b[1][:, columns(0)], banks[0][:], gain_b[1][:, columns(0)], MULT)
         nc.vector.tensor_copy(window(page_b[1], list_b, 0), h_b[1][:, columns(0)])
         values = h_b[1][:, columns(1)]
-        feature_half(1, 1, 1, values, banks[0])
+        feature_half(1, 1, 1, values, banks[1])
         nc.gpsimd.tensor_tensor(values, values, gain_b[1][:, columns(1)], MULT)
         nc.vector.tensor_copy(window(page_b[1], list_b, 1), values)
         for half in range(2):
             values = h_a[0][:, columns(half)]
-            feature_half(1, 0, half, values, banks[(7, 0)[half]])
-            nc.gpsimd.tensor_tensor(values, values, gain_a[1][:, columns(half)], MULT)
+            staged = tile([P, BANK], F32, f"staged{half}")
+            feature_half(1, 0, half, staged[:], banks[half])
+            nc.gpsimd.tensor_tensor(values, staged[:], gain_a[1][:, columns(half)], MULT)
             nc.vector.tensor_copy(window(page_a[1], list_a, half), values)
+            deal_w4(2 + half, tile([P, 3 * P], U8, f"w4_slice{2 + half}", tag=f"staged{half}")[:])
         rows.extend(tile([P, T2], F32, f"rows{i}") for i in range(2))
-        load_gain(gain_b, wg2, 2)
-        load_gain(gain_a, wg1, 2)
-        for half in range(2):
-            nc.sync.dma_start(first_rows[half][:], plan.rearrange("(p t) m -> t p m", t=4)[0, 0:P, columns(half, S)])
-        load_gain(gain_b, wg2, 3)
-        load_gain(gain_a, wg1, 3)
+        load_gain_once(gain_b, wg2, 2)
+        load_plan(0)
+        load_gain_once(gain_a, wg1, 2)
+        load_gain_once(gain_b, wg2, 3)
+        load_plan(1)
+        load_gain_once(gain_a, wg1, 3)
 
+        woven = []
         for s in range(LAST):
-            load_plan(s + 1)
+            if s > 0:
+                load_plan(s + 1)
             if s == 1:
                 nc.sync.dma_start(w8_w[:], w8_words.rearrange("a p n t -> p a (n t)").bitcast(I32))
                 load_plane(w8_s, w8_scales.rearrange("a r n -> r a n"))
             ahead = s + 2 <= LAST
-            if ahead:
-                features(s + 2, 1)
-                features(s + 2, 0)
+            late[s] = tile([P, S], F32, f"late_factors{s}", tag=f"late{s % 2}")
             for c in range(CHUNKS + 1):
                 if c < CHUNKS:
                     turn_pages(s, c)
+                    if s == LAST - 1 or (s >= 4 and c % 2 == 0):
+                        piece = len(woven)
+                        woven.append(piece)
+                        weave(nc.scalar.copy, 0, piece // 2, first_grouped[:, columns(piece // 2, 4 * BANK)], columns(piece % 2, BANK // 2))
                 if c >= 1:
                     turn_back(s, c - 1)
+                    if ahead:
+                        feature_piece(s + 2, c - 1)
                 if c in (2, 4):
+                    finish(factor(s, c - 2, 2))
                     damp_plan(nc.gpsimd, s, c - 2, 2, factor(s, c - 2, 2))
             if ahead:
                 scatter_b(s + 2)
                 scatter_a(s + 2)
-            if s == 0:
-                deal_w4(1, 0, 4, "w4_late")
-            for c in {4: (0,), 5: (1,), 6: (2, 3)}.get(s, ()):
-                weave(nc.scalar.copy, 0, c, first_grouped[:, columns(c, 4 * BANK)])
+            if s < 4:
+                deal_w4(4 + s, tile([P, 3 * P], U8, f"w4_slice{4 + s}", tag=f"late{s % 2}")[:])
+
 
         z_w = [tile([P, T2], U32, "z_w0", tag="rows0"), tile([P, T2], U32, "z_w1", tag="page_b0")]
-        z_s = [tile([P, T2], U8, "z_s0", tag="h_a0"), tile([P, T2], U8, "z_s1")]
+        z_s = [tile([P, T2], U8, "z_s0"), tile([P, T2], U8, "z_s1")]
 
-        def first_codes(half):
+        def first_codes(c):
             nc.vector.quantize_mx(
-                out=z_w[0][:, columns(half, S)].bitcast(FP8X4),
-                scales=z_s[0][:, columns(half, S)],
-                in_=first_grouped[:, columns(half, 4 * S)],
+                out=z_w[0][:, columns(c)].bitcast(FP8X4),
+                scales=z_s[0][:, columns(c)],
+                in_=first_grouped[:, columns(c, 4 * BANK)],
             )
 
         def last_product(c):
@@ -315,28 +328,41 @@ def tile_list_trap_bench_release_kernel(
                         stop=(a == 1),
                     )
                 staged = (gain_a + gain_b)[(BLOCKS * c + n) // 2][:, columns(n % 2)]
-                (nc.vector.tensor_copy if (n % 2 == 1 and 2 * c + n // 2 >= 8 - ON_VECTOR) else nc.scalar.copy)(staged, bank[:])
+                (nc.vector.tensor_copy if BLOCKS * c + n in ON_VECTOR else nc.scalar.copy)(staged, bank[:])
                 nc.sync.dma_start(out[columns(n, P), columns(c)], staged)
 
-        def last_factors(c):
-            x = factor(LAST - 1, c)
+        def last_values(c, count=1):
+            if c < 2:
+                return late[LAST - 1][:, columns(c)]
+            return first_grouped[:, columns(c - 2, 4 * BANK)].bitcast(F32)[:, 0:BANK]
+
+        def last_factors(c, count=1):
+            x = last_values(c)
             nc.vector.tensor_tensor(x, page_a[LAST % 2][:, columns(c)], page_b[LAST % 2][:, columns(c)], ADD)
             nc.scalar.activation(x, x, ACT.Square)
             nc.scalar.activation(x, x, ACT.Abs_reciprocal_sqrt, bias=ROOT * ROOT, scale=ROOT * ROOT)
+            finish(x)
 
         def second_codes(c):
-            damp_plan(nc.vector, LAST, c, 1, factor(LAST - 1, c))
+            damp_plan(nc.vector, LAST, c, 1, last_values(c))
             weave(nc.vector.tensor_copy, 1, c, second_grouped[c % 2][:])
             nc.vector.quantize_mx(
                 out=z_w[1][:, columns(c)].bitcast(FP8X4), scales=z_s[1][:, columns(c)], in_=second_grouped[c % 2][:]
             )
 
-        for step in range(CHUNKS + LAG + 1):
-            if step < CHUNKS:
-                last_factors(step)
-            if 1 <= step <= CHUNKS:
-                second_codes(step - 1)
-            if step in (1, 3):
-                first_codes(step // 2)
-            if step > LAG:
-                last_product(step - LAG - 1)
+        last_factors(0)
+        first_codes(0)
+        last_factors(1)
+        first_codes(1)
+        second_codes(0)
+        last_factors(2)
+        second_codes(1)
+        last_factors(3)
+        second_codes(2)
+        first_codes(2)
+        second_codes(3)
+        first_codes(3)
+        last_product(0)
+        last_product(1)
+        last_product(2)
+        last_product(3)

@@ -61,9 +61,9 @@ def tile_list_trap_bench_release_kernel(
         gain_a = [tile([P, S], F32, f"gain_a{t}") for t in range(4)]
         gain_b = [tile([P, S], F32, f"gain_b{t}") for t in range(4)]
         ident = tile([P, P], F32, "ident")
-        works = tile([P, 4 * S], F32, "works")
+        works = tile([P, 5 * S], F32, "works")
         late = {}
-        h_b = [works[:, columns(i, S)] for i in range(3)]
+        h_b = [works[:, columns(i, S)] for i in (0, 1, 3)]
 
         def factor(s, first, count=1):
             half = h_b[s % 3] if first < 2 else late[s]
@@ -72,9 +72,9 @@ def tile_list_trap_bench_release_kernel(
         h_a = [tile([P, S], F32, f"h_a{i}") for i in range(2)]
 
         def a_values(s):
-            return h_a[0 if s < 2 else (s + 1) % 2]
+            return works[:, columns(2, S)] if s == 1 else h_a[s % 2][:]
 
-        w1_raw = [tile([P, T2], F32, "w1_raw0", tag="rows1")[:], works[:, 2 * S : 4 * S]]
+        w1_raw = [tile([P, T2], F32, "w1_raw0", tag="rows1")[:], works[:, 3 * S : 5 * S]]
         w1_first = tile([P, BANK], BF16, "w1_first", tag="page_b1")
         page_b = [tile([P, T2], F32, "page_b0")]
         page_a = [tile([P, T2], F32, "page_a0")]
@@ -93,16 +93,9 @@ def tile_list_trap_bench_release_kernel(
             for q in range(4):
                 nc.sync.dma_start(target[t][32 * q : 32 * q + 32, cols], dealt[:, cols])
 
-        def load_gain_once(target, wg, t):
-            nc.sync.dma_start(target[t][:], wg.rearrange("(p t) j -> t p j", t=4)[t].partition_broadcast(4))
-
-        def clear(page):
-            for c in range(CHUNKS):
-                nc.gpsimd.memset(page[:, columns(c)].bitcast(I32), 0)
-
-        def deal_w4(s, spent):
-            a, t0, t1, count = s // 4, s % 4, s % 4 + 1, 1
-            words, plane = spent[:, 0 : 2 * P], spent[:, 2 * P : 3 * P]
+        def deal_w4(s, spent, count=1):
+            a, t0, t1 = s // 4, s % 4, s % 4 + count
+            words, plane = spent[:, 0 : count * 2 * P], spent[:, count * 2 * P : count * 3 * P]
             nc.gpsimd.tensor_copy(
                 words.rearrange("p (t m e) -> p t m e", m=P, e=2),
                 w4_raw_w[:, columns(a, H)].rearrange("p (m t e) -> p t m e", t=4, e=2)[:, t0:t1],
@@ -151,19 +144,19 @@ def tile_list_trap_bench_release_kernel(
 
         def feature_piece(s, piece):
             side, half = 1 - piece // 2, piece % 2
-            values = (a_values(s)[:], h_b[s % 3])[side]
+            values = (a_values(s), h_b[s % 3])[side]
             feature_half(s, side, half, values[:, columns(half)], banks[half])
             if half == 1:
                 nc.gpsimd.tensor_tensor(values, values, (gain_a, gain_b)[side][s % 4][:], MULT)
 
         def scatter_a(s):
-            nc.vector.tensor_copy(page_a[s % 2][:].indirect(list_a[:]), a_values(s)[:])
+            nc.vector.tensor_copy(page_a[s % 2][:].indirect(list_a[:]), a_values(s))
 
         def scatter_b(s):
             nc.vector.tensor_copy(page_b[s % 2][:].indirect(list_b[:]), h_b[s % 3])
 
-        def load_plan(s):
-            nc.sync.dma_start(rows[s % 2][:], plan.rearrange("(a p t) m -> a t p m", a=2, t=4)[s // 4, s % 4])
+        def load_plan(s, cols=slice(0, T2)):
+            nc.sync.dma_start(rows[s % 2][:, cols], plan.rearrange("(a p t) m -> a t p m", a=2, t=4)[s // 4, s % 4][:, cols])
 
         def turn_pages(s, c):
             bank = banks[c % 2]
@@ -219,11 +212,10 @@ def tile_list_trap_bench_release_kernel(
         load_w1(0)
         load_gain(gain_b, wg2, 0, columns(1))
         nc.sync.dma_start(list_a[:], offs2)
-        load_gain(gain_a, wg1, 0, columns(0))
-        load_gain(gain_a, wg1, 0, columns(1))
+        load_gain(gain_a, wg1, 0)
         load_w1(1)
-        load_gain_once(gain_b, wg2, 1)
-        load_gain_once(gain_a, wg1, 1)
+        load_gain(gain_b, wg2, 1)
+        load_gain(gain_a, wg1, 1)
         page_a.append(tile([P, T2], F32, "page_a1"))
         for page in (page_b[0], page_a[0], page_a[1]):
             nc.vector.memset(page[:].bitcast(I32), 0)
@@ -245,12 +237,12 @@ def tile_list_trap_bench_release_kernel(
         nc.vector.tensor_tensor(window(page_b[0], list_b, 1), values, gain_b[0][:, columns(1)], MULT)
         for half in range(2):
             feature_half(0, 0, half, h_a[0][:, columns(half)], banks[4 + half])
-            nc.vector.tensor_tensor(window(page_a[0], list_a, half), h_a[0][:, columns(half)], gain_a[0][:, columns(half)], MULT)
+        nc.vector.tensor_tensor(page_a[0][:].indirect(list_a[:]), h_a[0][:], gain_a[0][:], MULT)
         w1_next = tile([P, 3 * BANK], BF16, "w1_next", tag="page_b1")
         quantise_w1(0, 1, 4, w1_next[:], [(1, 2), (2, 4)])
         page_b.append(tile([P, T2], F32, "page_b1"))
         nc.gpsimd.memset(page_b[1][:].bitcast(I32), 0)
-        quantise_w1(1, 0, 4, h_b[1].bitcast(BF16), [(0, 4)])
+        quantise_w1(1, 0, 4, works[:, S + BANK : 2 * S + BANK].bitcast(BF16), [(0, 4)])
 
         product(1, 1, 0, banks[0])
         nc.vector.tensor_tensor(h_b[1][:, columns(0)], banks[0][:], gain_b[1][:, columns(0)], MULT)
@@ -259,20 +251,20 @@ def tile_list_trap_bench_release_kernel(
         feature_half(1, 1, 1, values, banks[1])
         nc.gpsimd.tensor_tensor(values, values, gain_b[1][:, columns(1)], MULT)
         nc.vector.tensor_copy(window(page_b[1], list_b, 1), values)
+        staged = tile([P, S], F32, "staged")
         for half in range(2):
-            values = h_a[0][:, columns(half)]
-            staged = tile([P, BANK], F32, f"staged{half}")
-            feature_half(1, 0, half, staged[:], banks[half])
-            nc.gpsimd.tensor_tensor(values, staged[:], gain_a[1][:, columns(half)], MULT)
-            nc.vector.tensor_copy(window(page_a[1], list_a, half), values)
-            deal_w4(2 + half, tile([P, 3 * P], U8, f"w4_slice{2 + half}", tag=f"staged{half}")[:])
+            feature_half(1, 0, half, staged[:, columns(half)], banks[4 + half])
+        nc.gpsimd.tensor_tensor(a_values(1), staged[:], gain_a[1][:], MULT)
+        scatter_a(1)
+        deal_w4(2, tile([P, 6 * P], U8, "w4_third", tag="staged")[:], 2)
         rows.extend(tile([P, T2], F32, f"rows{i}") for i in range(2))
-        load_gain_once(gain_b, wg2, 2)
-        load_plan(0)
-        load_gain_once(gain_a, wg1, 2)
-        load_gain_once(gain_b, wg2, 3)
+        load_gain(gain_b, wg2, 2)
+        load_plan(0, columns(0, S))
+        load_gain(gain_a, wg1, 2)
+        load_gain(gain_b, wg2, 3)
+        load_plan(0, columns(1, S))
+        load_gain(gain_a, wg1, 3)
         load_plan(1)
-        load_gain_once(gain_a, wg1, 3)
 
         woven = []
         for s in range(LAST):
@@ -294,9 +286,12 @@ def tile_list_trap_bench_release_kernel(
                     turn_back(s, c - 1)
                     if ahead:
                         feature_piece(s + 2, c - 1)
-                if c in (2, 4):
+                if c == 2 or (c == 4 and ahead):
                     finish(factor(s, c - 2, 2))
                     damp_plan(nc.gpsimd, s, c - 2, 2, factor(s, c - 2, 2))
+                elif c > 2 and not ahead:
+                    finish(factor(s, c - 1))
+                    damp_plan(nc.gpsimd, s, c - 1, 1, factor(s, c - 1))
             if ahead:
                 scatter_b(s + 2)
                 scatter_a(s + 2)

@@ -25,6 +25,7 @@ LAST = SLICES - 1
 CHUNKS = T2 // BANK
 BLOCKS = BANK // P
 LIST_HALF = BANK // 16
+PIECES = (0, 512, 1024, 1536, 2048)
 ON_VECTOR = (11, 13, 15)
 ROOT = 75.0 / 64.0
 
@@ -55,7 +56,7 @@ def tile_list_trap_bench_release_kernel(
         w1_s = tile([P, H], U8, "w1_s")
         w4_raw_w = tile([P, 2 * H], U8, "w4_raw_w")
         w4_raw_s = tile([P, H], U8, "w4_raw_s")
-        w4_dealt = []
+        w4_w, w4_s = [], []
         w8_w = tile([P, 2, N], I32, "w8_w")
         w8_s = tile([P, 2, N], U8, "w8_s")
         gain_a = [tile([P, S], F32, f"gain_a{t}") for t in range(4)]
@@ -81,6 +82,7 @@ def tile_list_trap_bench_release_kernel(
         squares = [tile([P, BANK], F32, f"squares{i}") for i in range(3)]
         pairs = [tile([P, 4 * T2], BF16, f"pairs{a}") for a in range(2)]
         rows = []
+        raw_h = [tile([P, S], F32, f"raw_h{i}") for i in range(2)]
         first_grouped = tile([P, 4 * T2], BF16, "first_grouped")
         second_grouped = [tile([P, 4 * BANK], BF16, f"second_grouped{i}") for i in range(2)]
 
@@ -93,19 +95,23 @@ def tile_list_trap_bench_release_kernel(
             for q in range(4):
                 nc.sync.dma_start(target[t][32 * q : 32 * q + 32, cols], dealt[:, cols])
 
-        def deal_w4(s, spent, count=1):
-            a, t0, t1 = s // 4, s % 4, s % 4 + count
-            words, plane = spent[:, 0 : count * 2 * P], spent[:, count * 2 * P : count * 3 * P]
+        def deal_words(s, count, target):
             nc.gpsimd.tensor_copy(
-                words.rearrange("p (t m e) -> p t m e", m=P, e=2),
-                w4_raw_w[:, columns(a, H)].rearrange("p (m t e) -> p t m e", t=4, e=2)[:, t0:t1],
+                target.rearrange("p (t m e) -> p t m e", m=P, e=2),
+                w4_raw_w[:, columns(s // 4, H)].rearrange("p (m t e) -> p t m e", t=4, e=2)[:, s % 4 : s % 4 + count],
             )
+            w4_w.extend(target[:, columns(t, 2 * P)] for t in range(count))
+
+        def deal_scales(s, count, target):
             nc.gpsimd.tensor_copy(
-                plane.rearrange("p (t m) -> p t m", m=P),
-                w4_raw_s[:, columns(a)].rearrange("p (m t) -> p t m", t=4)[:, t0:t1],
+                target.rearrange("p (t m) -> p t m", m=P),
+                w4_raw_s[:, columns(s // 4)].rearrange("p (m t) -> p t m", t=4)[:, s % 4 : s % 4 + count],
             )
-            for t in range(count):
-                w4_dealt.append((words[:, columns(t, 2 * P)], plane[:, columns(t, P)]))
+            w4_s.extend(target[:, columns(t, P)] for t in range(count))
+
+        def deal_w4(s, target):
+            deal_words(s, 1, target[:, 0 : 2 * P])
+            deal_scales(s, 1, target[:, 2 * P : 3 * P])
 
         def load_w1(a):
             nc.sync.dma_start(w1_raw[a].rearrange("p (j c) -> p j c", j=4), w1[:, columns(a)].rearrange("(p j) c -> p j c", j=4))
@@ -127,7 +133,7 @@ def tile_list_trap_bench_release_kernel(
             if side == 0:
                 weights, plane = w1_w[:, columns(s, P)].bitcast(FP8X4), w1_s[:, columns(s, P)]
             else:
-                weights, plane = w4_dealt[s][0].bitcast(FP4X4), w4_dealt[s][1]
+                weights, plane = w4_w[s].bitcast(FP4X4), w4_s[s]
             nc.tensor.matmul_mx(
                 out=bank[:],
                 lhsT=weights,
@@ -144,10 +150,10 @@ def tile_list_trap_bench_release_kernel(
 
         def feature_piece(s, piece):
             side, half = 1 - piece // 2, piece % 2
-            values = (a_values(s), h_b[s % 3])[side]
-            feature_half(s, side, half, values[:, columns(half)], banks[half])
+            raw = raw_h[(s + side) % 2]
+            feature_half(s, side, half, raw[:, columns(half)], banks[half])
             if half == 1:
-                nc.gpsimd.tensor_tensor(values, values, (gain_a, gain_b)[side][s % 4][:], MULT)
+                nc.gpsimd.tensor_tensor((a_values(s), h_b[s % 3])[side], raw[:], (gain_a, gain_b)[side][s % 4][:], MULT)
 
         def scatter_a(s):
             nc.vector.tensor_copy(page_a[s % 2][:].indirect(list_a[:]), a_values(s))
@@ -216,12 +222,12 @@ def tile_list_trap_bench_release_kernel(
         load_w1(1)
         load_gain(gain_b, wg2, 1)
         load_gain(gain_a, wg1, 1)
-        page_a.append(tile([P, T2], F32, "page_a1"))
-        for page in (page_b[0], page_a[0], page_a[1]):
+        for page in (page_b[0], page_a[0]):
             nc.vector.memset(page[:].bitcast(I32), 0)
         make_identity(nc, ident[:])
         nc.gpsimd.memset(w8_s[:].rearrange("p a n -> p (a n)").bitcast(I32), 0)
-        deal_w4(0, tile([P, 3 * P], U8, "w4_first")[:])
+        deal_words(0, 2, tile([P, 4 * P], U8, "w4_first_words")[:])
+        deal_scales(0, 1, tile([P, P], U8, "w4_first")[:])
         nc.vector.tensor_copy(v_s[:], tab_s[:].indirect(list_tab[:]))
         for half in range(2):
             entries = list_tab[:, columns(half, LIST_HALF)]
@@ -233,15 +239,18 @@ def tile_list_trap_bench_release_kernel(
         quantise_w1(0, 0, 1, w1_first[:], [(0, 1)])
         values = h_b[0][:, columns(1)]
         feature_half(0, 1, 1, values, banks[5])
-        deal_w4(1, tile([P, 3 * P], U8, "w4_second", tag="w4_first")[:])
+        second = tile([P, 4 * P], U8, "w4_second", tag="w4_first")
+        deal_scales(1, 2, second[:, 0 : 2 * P])
+        deal_words(2, 1, second[:, 2 * P : 4 * P])
         nc.vector.tensor_tensor(window(page_b[0], list_b, 1), values, gain_b[0][:, columns(1)], MULT)
         for half in range(2):
             feature_half(0, 0, half, h_a[0][:, columns(half)], banks[4 + half])
         nc.vector.tensor_tensor(page_a[0][:].indirect(list_a[:]), h_a[0][:], gain_a[0][:], MULT)
-        w1_next = tile([P, 3 * BANK], BF16, "w1_next", tag="page_b1")
-        quantise_w1(0, 1, 4, w1_next[:], [(1, 2), (2, 4)])
-        page_b.append(tile([P, T2], F32, "page_b1"))
-        nc.gpsimd.memset(page_b[1][:].bitcast(I32), 0)
+        quantise_w1(0, 1, 2, tile([P, BANK], BF16, "w1_second", tag="page_b1")[:], [(1, 2)])
+        quantise_w1(0, 2, 4, tile([P, 2 * BANK], BF16, "w1_third", tag="page_a1")[:], [(2, 4)])
+        for pages, name in ((page_b, "page_b1"), (page_a, "page_a1")):
+            pages.append(tile([P, T2], F32, name))
+            nc.gpsimd.memset(pages[1][:].bitcast(I32), 0)
         quantise_w1(1, 0, 4, works[:, S + BANK : 2 * S + BANK].bitcast(BF16), [(0, 4)])
 
         product(1, 1, 0, banks[0])
@@ -256,15 +265,13 @@ def tile_list_trap_bench_release_kernel(
             feature_half(1, 0, half, staged[:, columns(half)], banks[4 + half])
         nc.gpsimd.tensor_tensor(a_values(1), staged[:], gain_a[1][:], MULT)
         scatter_a(1)
-        deal_w4(2, tile([P, 6 * P], U8, "w4_third", tag="staged")[:], 2)
+        deal_w4(3, tile([P, 3 * P], U8, "w4_third", tag="staged")[:])
         rows.extend(tile([P, T2], F32, f"rows{i}") for i in range(2))
-        load_gain(gain_b, wg2, 2)
-        load_plan(0, columns(0, S))
-        load_gain(gain_a, wg1, 2)
-        load_gain(gain_b, wg2, 3)
-        load_plan(0, columns(1, S))
-        load_gain(gain_a, wg1, 3)
-        load_plan(1)
+        for s in range(2):
+            load_gain(gain_b, wg2, s + 2)
+            load_plan(s, columns(0, S))
+            load_gain(gain_a, wg1, s + 2)
+            load_plan(s, columns(1, S))
 
         woven = []
         for s in range(LAST):
@@ -278,7 +285,7 @@ def tile_list_trap_bench_release_kernel(
             for c in range(CHUNKS + 1):
                 if c < CHUNKS:
                     turn_pages(s, c)
-                    if s == LAST - 1 or (s >= 4 and c % 2 == 0):
+                    if s in (4, 5):
                         piece = len(woven)
                         woven.append(piece)
                         weave(nc.scalar.copy, 0, piece // 2, first_grouped[:, columns(piece // 2, 4 * BANK)], columns(piece % 2, BANK // 2))
@@ -302,62 +309,76 @@ def tile_list_trap_bench_release_kernel(
         z_w = [tile([P, T2], U32, "z_w0", tag="rows0"), tile([P, T2], U32, "z_w1", tag="page_b0")]
         z_s = [tile([P, T2], U8, "z_s0"), tile([P, T2], U8, "z_s1")]
 
-        def first_codes(c):
+        def span(i):
+            return slice(PIECES[i], PIECES[i + 1])
+
+        def first_codes(i):
+            cols = span(i)
             nc.vector.quantize_mx(
-                out=z_w[0][:, columns(c)].bitcast(FP8X4),
-                scales=z_s[0][:, columns(c)],
-                in_=first_grouped[:, columns(c, 4 * BANK)],
+                out=z_w[0][:, cols].bitcast(FP8X4),
+                scales=z_s[0][:, cols],
+                in_=first_grouped[:, 4 * cols.start : 4 * cols.stop],
             )
 
-        def last_product(c):
-            for n in range(N // P):
-                bank = banks[(BLOCKS * c + n) % 8]
-                for a in range(2):
-                    nc.tensor.matmul_mx(
-                        out=bank[:],
-                        lhsT=w8_w[:, a, columns(n, P)].bitcast(FP8X4),
-                        lhsT_scale=w8_s[:, a, columns(n, P)],
-                        rhs=z_w[a][:, columns(c)].bitcast(FP8X4),
-                        rhs_scale=z_s[a][:, columns(c)],
-                        start=(a == 0),
-                        stop=(a == 1),
-                    )
-                staged = (gain_a + gain_b)[(BLOCKS * c + n) // 2][:, columns(n % 2)]
-                (nc.vector.tensor_copy if BLOCKS * c + n in ON_VECTOR else nc.scalar.copy)(staged, bank[:])
-                nc.sync.dma_start(out[columns(n, P), columns(c)], staged)
+        filled = []
 
-        def last_values(c, count=1):
-            if c < 2:
-                return late[LAST - 1][:, columns(c)]
-            return first_grouped[:, columns(c - 2, 4 * BANK)].bitcast(F32)[:, 0:BANK]
+        def last_product(i):
+            cols = span(i)
+            width = cols.stop - cols.start
+            share = BANK // width
+            for first in range(0, N // P, share):
+                k = len(filled)
+                filled.append(k)
+                bank = banks[k % 8]
+                for j in range(share):
+                    for a in range(2):
+                        nc.tensor.matmul_mx(
+                            out=bank[:, columns(j, width)],
+                            lhsT=w8_w[:, a, columns(first + j, P)].bitcast(FP8X4),
+                            lhsT_scale=w8_s[:, a, columns(first + j, P)],
+                            rhs=z_w[a][:, cols].bitcast(FP8X4),
+                            rhs_scale=z_s[a][:, cols],
+                            start=(a == 0),
+                            stop=(a == 1),
+                        )
+                staged_out = (gain_a + gain_b)[k // 2][:, columns(k % 2)]
+                (nc.vector.tensor_copy if k in ON_VECTOR else nc.scalar.copy)(staged_out, bank[:])
+                nc.sync.dma_start(
+                    out[first * P : (first + share) * P, cols].rearrange("(j p) m -> p j m", p=P),
+                    staged_out.rearrange("p (j m) -> p j m", j=share),
+                )
 
-        def last_factors(c, count=1):
-            x = last_values(c)
-            nc.vector.tensor_tensor(x, page_a[LAST % 2][:, columns(c)], page_b[LAST % 2][:, columns(c)], ADD)
+        def last_values(i):
+            cols = span(i)
+            if cols.stop <= S:
+                return late[LAST - 1][:, cols]
+            return first_grouped[:, columns(cols.start // BANK - 2, 4 * BANK)].bitcast(F32)[:, cols.start % BANK : cols.start % BANK + cols.stop - cols.start]
+
+        def last_factors(i):
+            x = last_values(i)
+            nc.vector.tensor_tensor(x, page_a[LAST % 2][:, span(i)], page_b[LAST % 2][:, span(i)], ADD)
             nc.scalar.activation(x, x, ACT.Square)
             nc.scalar.activation(x, x, ACT.Abs_reciprocal_sqrt, bias=ROOT * ROOT, scale=ROOT * ROOT)
             finish(x)
 
-        def second_codes(c):
-            damp_plan(nc.vector, LAST, c, 1, last_values(c))
-            weave(nc.vector.tensor_copy, 1, c, second_grouped[c % 2][:])
+        def second_codes(i):
+            cols = span(i)
+            c, part = cols.start // BANK, slice(cols.start % BANK, (cols.stop - 1) % BANK + 1)
+            target = pairs[1][:].rearrange("p (c u m e) -> p u e c m", u=2, m=BANK, e=2)
+            nc.vector.tensor_tensor(target[:, 1, 1, c, part], last_values(i), rows[LAST % 2][:, cols], MULT)
+            weave(nc.vector.tensor_copy, 1, c, second_grouped[c % 2][:], part)
             nc.vector.quantize_mx(
-                out=z_w[1][:, columns(c)].bitcast(FP8X4), scales=z_s[1][:, columns(c)], in_=second_grouped[c % 2][:]
+                out=z_w[1][:, cols].bitcast(FP8X4),
+                scales=z_s[1][:, cols],
+                in_=second_grouped[c % 2][:, 4 * part.start : 4 * part.stop],
             )
 
-        last_factors(0)
-        first_codes(0)
-        last_factors(1)
-        first_codes(1)
-        second_codes(0)
-        last_factors(2)
-        second_codes(1)
-        last_factors(3)
-        second_codes(2)
-        first_codes(2)
-        second_codes(3)
-        first_codes(3)
-        last_product(0)
-        last_product(1)
-        last_product(2)
-        last_product(3)
+        count = len(PIECES) - 1
+        for step in range(count + 6):
+            if 1 <= step <= count:
+                second_codes(step - 1)
+            if step < count:
+                last_factors(step)
+                first_codes(step)
+            if step >= 6:
+                last_product(step - 6)

@@ -25,7 +25,6 @@ LAST = SLICES - 1
 CHUNKS = T2 // BANK
 BLOCKS = BANK // P
 LIST_HALF = BANK // 16
-PIECES = (0, 512, 1024, 1536, 2048)
 ON_VECTOR = (11, 13, 15)
 ROOT = 75.0 / 64.0
 
@@ -210,7 +209,7 @@ def tile_list_trap_bench_release_kernel(
         nc.vector.memset(w4_raw_s[:].bitcast(I32), 0)
         nc.sync.dma_start(list_tab[:], offs)
         load_plane(tab_s, tab_scales[0])
-        nc.sync.dma_start(w4_raw_w[:].bitcast(I32), w4_words[0].bitcast(I32))
+        nc.sync.dma_start(w4_raw_w[:, columns(0, H)].bitcast(I32), w4_words[0, :, columns(0, H)].bitcast(I32))
         nc.sync.dma_start(tab_w[:], tab_words[0].rearrange("p n t -> p (n t)").bitcast(I32))
         load_plane(w4_raw_s, w4_scales[0])
         nc.sync.dma_start(list_b[:], offs3)
@@ -220,6 +219,7 @@ def tile_list_trap_bench_release_kernel(
         nc.sync.dma_start(list_a[:], offs2)
         load_gain(gain_a, wg1, 0)
         load_w1(1)
+        nc.sync.dma_start(w4_raw_w[:, columns(1, H)].bitcast(I32), w4_words[0, :, columns(1, H)].bitcast(I32))
         load_gain(gain_b, wg2, 1)
         load_gain(gain_a, wg1, 1)
         for page in (page_b[0], page_a[0]):
@@ -293,10 +293,10 @@ def tile_list_trap_bench_release_kernel(
                     turn_back(s, c - 1)
                     if ahead:
                         feature_piece(s + 2, c - 1)
-                if c == 2 or (c == 4 and ahead):
+                if c in (2, 4) and ahead:
                     finish(factor(s, c - 2, 2))
                     damp_plan(nc.gpsimd, s, c - 2, 2, factor(s, c - 2, 2))
-                elif c > 2 and not ahead:
+                elif c >= 1 and not ahead:
                     finish(factor(s, c - 1))
                     damp_plan(nc.gpsimd, s, c - 1, 1, factor(s, c - 1))
             if ahead:
@@ -309,76 +309,61 @@ def tile_list_trap_bench_release_kernel(
         z_w = [tile([P, T2], U32, "z_w0", tag="rows0"), tile([P, T2], U32, "z_w1", tag="page_b0")]
         z_s = [tile([P, T2], U8, "z_s0"), tile([P, T2], U8, "z_s1")]
 
-        def span(i):
-            return slice(PIECES[i], PIECES[i + 1])
-
-        def first_codes(i):
-            cols = span(i)
+        def first_codes(c):
             nc.vector.quantize_mx(
-                out=z_w[0][:, cols].bitcast(FP8X4),
-                scales=z_s[0][:, cols],
-                in_=first_grouped[:, 4 * cols.start : 4 * cols.stop],
+                out=z_w[0][:, columns(c)].bitcast(FP8X4),
+                scales=z_s[0][:, columns(c)],
+                in_=first_grouped[:, columns(c, 4 * BANK)],
             )
 
-        filled = []
+        def last_values(c):
+            if c < 2:
+                return late[LAST - 1][:, columns(c)]
+            return first_grouped[:, columns(c - 2, 4 * BANK)].bitcast(F32)[:, 0:BANK]
 
-        def last_product(i):
-            cols = span(i)
-            width = cols.stop - cols.start
-            share = BANK // width
-            for first in range(0, N // P, share):
-                k = len(filled)
-                filled.append(k)
-                bank = banks[k % 8]
-                for j in range(share):
-                    for a in range(2):
-                        nc.tensor.matmul_mx(
-                            out=bank[:, columns(j, width)],
-                            lhsT=w8_w[:, a, columns(first + j, P)].bitcast(FP8X4),
-                            lhsT_scale=w8_s[:, a, columns(first + j, P)],
-                            rhs=z_w[a][:, cols].bitcast(FP8X4),
-                            rhs_scale=z_s[a][:, cols],
-                            start=(a == 0),
-                            stop=(a == 1),
-                        )
-                staged_out = (gain_a + gain_b)[k // 2][:, columns(k % 2)]
-                (nc.vector.tensor_copy if k in ON_VECTOR else nc.scalar.copy)(staged_out, bank[:])
-                nc.sync.dma_start(
-                    out[first * P : (first + share) * P, cols].rearrange("(j p) m -> p j m", p=P),
-                    staged_out.rearrange("p (j m) -> p j m", j=share),
-                )
-
-        def last_values(i):
-            cols = span(i)
-            if cols.stop <= S:
-                return late[LAST - 1][:, cols]
-            return first_grouped[:, columns(cols.start // BANK - 2, 4 * BANK)].bitcast(F32)[:, cols.start % BANK : cols.start % BANK + cols.stop - cols.start]
-
-        def last_factors(i):
-            x = last_values(i)
-            nc.vector.tensor_tensor(x, page_a[LAST % 2][:, span(i)], page_b[LAST % 2][:, span(i)], ADD)
+        def last_factors(c):
+            x = last_values(c)
+            nc.vector.tensor_tensor(x, page_a[LAST % 2][:, columns(c)], page_b[LAST % 2][:, columns(c)], ADD)
             nc.scalar.activation(x, x, ACT.Square)
             nc.scalar.activation(x, x, ACT.Abs_reciprocal_sqrt, bias=ROOT * ROOT, scale=ROOT * ROOT)
             finish(x)
 
-        def second_codes(i):
-            cols = span(i)
-            c, part = cols.start // BANK, slice(cols.start % BANK, (cols.stop - 1) % BANK + 1)
-            target = pairs[1][:].rearrange("p (c u m e) -> p u e c m", u=2, m=BANK, e=2)
-            nc.vector.tensor_tensor(target[:, 1, 1, c, part], last_values(i), rows[LAST % 2][:, cols], MULT)
-            weave(nc.vector.tensor_copy, 1, c, second_grouped[c % 2][:], part)
+        def second_codes(c):
+            damp_plan(nc.vector, LAST, c, 1, last_values(c))
+            weave(nc.vector.tensor_copy, 1, c, second_grouped[c % 2][:])
             nc.vector.quantize_mx(
-                out=z_w[1][:, cols].bitcast(FP8X4),
-                scales=z_s[1][:, cols],
-                in_=second_grouped[c % 2][:, 4 * part.start : 4 * part.stop],
+                out=z_w[1][:, columns(c)].bitcast(FP8X4), scales=z_s[1][:, columns(c)], in_=second_grouped[c % 2][:]
             )
 
-        count = len(PIECES) - 1
-        for step in range(count + 6):
-            if 1 <= step <= count:
+        def last_product(c):
+            for n in range(BLOCKS):
+                k = BLOCKS * c + n
+                bank = banks[k % 8]
+                for a in range(2):
+                    nc.tensor.matmul_mx(
+                        out=bank[:],
+                        lhsT=w8_w[:, a, columns(n, P)].bitcast(FP8X4),
+                        lhsT_scale=w8_s[:, a, columns(n, P)],
+                        rhs=z_w[a][:, columns(c)].bitcast(FP8X4),
+                        rhs_scale=z_s[a][:, columns(c)],
+                        start=(a == 0),
+                        stop=(a == 1),
+                    )
+                pair = (gain_a + gain_b)[k // 2]
+                (nc.vector.tensor_copy if k in ON_VECTOR else nc.scalar.copy)(pair[:, columns(k % 2)], bank[:])
+                if k // 2 in (0, 2 * CHUNKS - 1):
+                    nc.sync.dma_start(out[columns(n, P), columns(c)], pair[:, columns(k % 2)])
+                elif k % 2 == 1:
+                    nc.sync.dma_start(
+                        out[columns(n // 2, 2 * P), columns(c)].rearrange("(j p) m -> p j m", p=P),
+                        pair[:].rearrange("p (j m) -> p j m", j=2),
+                    )
+
+        for step in range(CHUNKS + 1):
+            if step >= 1:
                 second_codes(step - 1)
-            if step < count:
+            if step < CHUNKS:
                 last_factors(step)
                 first_codes(step)
-            if step >= 6:
-                last_product(step - 6)
+        for c in range(CHUNKS):
+            last_product(c)

@@ -85,8 +85,8 @@ def tile_list_trap_bench_release_kernel(
         first_grouped = tile([P, 4 * T2], BF16, "first_grouped")
         second_grouped = [tile([P, 4 * BANK], BF16, f"second_grouped{i}") for i in range(2)]
 
-        def load_plane(plane, src_rows):
-            for q in range(4):
+        def load_plane(plane, src_rows, quadrants=range(4)):
+            for q in quadrants:
                 nc.sync.dma_start(plane[32 * q : 32 * q + 4].bitcast(I32), src_rows[4 * q : 4 * q + 4].bitcast(I32))
 
         def load_gain(target, wg, t, cols=slice(0, S)):
@@ -198,22 +198,23 @@ def tile_list_trap_bench_release_kernel(
                 MULT,
             )
 
-        def weave(copy, a, c, target, part=slice(0, BANK)):
-            source = pairs[a][:, columns(c, 4 * BANK)].bitcast(F32).rearrange("p (u m) -> p m u", u=2)
-            copy(target.bitcast(F32).rearrange("p (m u) -> p m u", u=2)[:, part], source[:, part])
+        def weave(copy, a, c, target, part=slice(0, BANK // 4)):
+            source = pairs[a][:, columns(c, 4 * BANK)].bitcast(F32).rearrange("p (u g i) -> p g u i", u=2, i=4)
+            copy(target.bitcast(F32).rearrange("p (g i u) -> p g u i", u=2, i=4)[:, part], source[:, part])
 
         def window(page, entries, half):
             return page[:].indirect(entries[:, columns(half, LIST_HALF)])
 
-        nc.vector.memset(tab_s[:].bitcast(I32), 0)
-        nc.vector.memset(w4_raw_s[:].bitcast(I32), 0)
+        nc.gpsimd.memset(tab_s[:].bitcast(I32), 0)
+        nc.gpsimd.memset(w4_raw_s[:].bitcast(I32), 0)
         nc.sync.dma_start(list_tab[:], offs)
         load_plane(tab_s, tab_scales[0])
         nc.sync.dma_start(w4_raw_w[:, columns(0, H)].bitcast(I32), w4_words[0, :, columns(0, H)].bitcast(I32))
+        load_plane(w4_raw_s, w4_scales[0], range(1))
         nc.sync.dma_start(tab_w[:], tab_words[0].rearrange("p n t -> p (n t)").bitcast(I32))
-        load_plane(w4_raw_s, w4_scales[0])
-        nc.sync.dma_start(list_b[:], offs3)
+        load_plane(w4_raw_s, w4_scales[0], range(1, 4))
         load_gain(gain_b, wg2, 0, columns(0))
+        nc.sync.dma_start(list_b[:], offs3)
         load_w1(0)
         load_gain(gain_b, wg2, 0, columns(1))
         nc.sync.dma_start(list_a[:], offs2)
@@ -288,7 +289,7 @@ def tile_list_trap_bench_release_kernel(
                     if s in (4, 5):
                         piece = len(woven)
                         woven.append(piece)
-                        weave(nc.scalar.copy, 0, piece // 2, first_grouped[:, columns(piece // 2, 4 * BANK)], columns(piece % 2, BANK // 2))
+                        weave(nc.scalar.copy, 0, piece // 2, first_grouped[:, columns(piece // 2, 4 * BANK)], columns(piece % 2, BANK // 8))
                 if c >= 1:
                     turn_back(s, c - 1)
                     if ahead:
@@ -351,13 +352,7 @@ def tile_list_trap_bench_release_kernel(
                     )
                 pair = (gain_a + gain_b)[k // 2]
                 (nc.vector.tensor_copy if k in ON_VECTOR else nc.scalar.copy)(pair[:, columns(k % 2)], bank[:])
-                if k // 2 in (0, 2 * CHUNKS - 1):
-                    nc.sync.dma_start(out[columns(n, P), columns(c)], pair[:, columns(k % 2)])
-                elif k % 2 == 1:
-                    nc.sync.dma_start(
-                        out[columns(n // 2, 2 * P), columns(c)].rearrange("(j p) m -> p j m", p=P),
-                        pair[:].rearrange("p (j m) -> p j m", j=2),
-                    )
+                nc.sync.dma_start(out[columns(n, P), columns(c)], pair[:, columns(k % 2)])
 
         for step in range(CHUNKS + 1):
             if step >= 1:

@@ -20,12 +20,12 @@ ADD = mybir.AluOpType.add
 
 P = 128
 BANK = 512
-SLICES = H // P
-LAST = SLICES - 1
+HALF = BANK // 2
 CHUNKS = T2 // BANK
 BLOCKS = BANK // P
-LIST_HALF = BANK // 16
-ON_VECTOR = (11, 13, 15)
+STEPS = H // P
+LAST = STEPS - 1
+ORDER = (0, 4, 1, 2, 3, 5, 6, 7)
 ROOT = 75.0 / 64.0
 
 
@@ -37,12 +37,16 @@ def tile_list_trap_bench_release_kernel(
         keep = ctx.enter_context(tc.tile_pool(name="keep", bufs=1))
         psum = ctx.enter_context(tc.psum_pool(name="psum", bufs=1))
         banks = [psum.tile([P, BANK], F32, name=f"bank{b}") for b in range(8)]
+        sums, backs, feats = banks[0:4], banks[4:6], banks[6:8]
 
         def columns(i, width=BANK):
             return slice(i * width, (i + 1) * width)
 
         def tile(shape, dtype, name, tag=None):
             return keep.tile(shape, dtype, name=name, tag=tag or name, align_bytes=64)
+
+        def pass_and_slot(step):
+            return divmod(ORDER[step], 4)
 
         list_tab = tile([P, S // 16], U16, "list_tab")
         list_a = tile([P, S // 16], U16, "list_a")
@@ -51,314 +55,402 @@ def tile_list_trap_bench_release_kernel(
         tab_s = tile([P, T], U8, "tab_s")
         v_w = tile([P, S], U32, "v_w")
         v_s = tile([P, S], U8, "v_s")
+        w1_raw = [tile([P, T2], F32, "w1_raw0", tag="rows1"), tile([P, T2], F32, "w1_raw1", tag="factors1")]
         w1_w = tile([P, H], U32, "w1_w")
         w1_s = tile([P, H], U8, "w1_s")
-        w4_raw_w = tile([P, 2 * H], U8, "w4_raw_w")
+        w4_raw_w = [tile([P, H], U8, f"w4_raw_w{a}") for a in range(2)]
         w4_raw_s = tile([P, H], U8, "w4_raw_s")
-        w4_w, w4_s = [], []
+        w4_w = [tile([P, H], U8, "w4_w0")]
+        w4_s_first = tile([P, P], U8, "w4_s_first")
+        w4_s = [tile([P, 3 * P], U8, "w4_s0"), tile([P, 4 * P], U8, "w4_s1")]
         w8_w = tile([P, 2, N], I32, "w8_w")
         w8_s = tile([P, 2, N], U8, "w8_s")
         gain_a = [tile([P, S], F32, f"gain_a{t}") for t in range(4)]
         gain_b = [tile([P, S], F32, f"gain_b{t}") for t in range(4)]
         ident = tile([P, P], F32, "ident")
-        works = tile([P, 5 * S], F32, "works")
-        late = {}
-        h_b = [works[:, columns(i, S)] for i in (0, 1, 3)]
-
-        def factor(s, first, count=1):
-            half = h_b[s % 3] if first < 2 else late[s]
-            return half[:, (first % 2) * BANK : (first % 2 + count) * BANK]
-
-        h_a = [tile([P, S], F32, f"h_a{i}") for i in range(2)]
-
-        def a_values(s):
-            return works[:, columns(2, S)] if s == 1 else h_a[s % 2][:]
-
-        w1_raw = [tile([P, T2], F32, "w1_raw0", tag="rows1")[:], works[:, 3 * S : 5 * S]]
-        w1_first = tile([P, BANK], BF16, "w1_first", tag="page_b1")
+        page_a = tile([P, T2], F32, "page_a")
         page_b = [tile([P, T2], F32, "page_b0")]
-        page_a = [tile([P, T2], F32, "page_a0")]
-        squares = [tile([P, BANK], F32, f"squares{i}") for i in range(3)]
+        early = tile([P, HALF], F32, "early", tag="page_b1")
+        second = tile([P, BANK], F32, "second", tag="w4_w1")
+        staged = tile([P, 2 * S], F32, "staged")
+        weighed = [tile([P, S], F32, "h_a"), tile([P, S], F32, "h_b")]
+        squares = [tile([P, BANK], F32, f"squares{i}") for i in range(CHUNKS)]
         pairs = [tile([P, 4 * T2], BF16, f"pairs{a}") for a in range(2)]
-        rows = []
-        raw_h = [tile([P, S], F32, f"raw_h{i}") for i in range(2)]
         first_grouped = tile([P, 4 * T2], BF16, "first_grouped")
-        second_grouped = [tile([P, 4 * BANK], BF16, f"second_grouped{i}") for i in range(2)]
+        second_grouped = [tile([P, 4 * BANK], BF16, f"second_grouped{i}") for i in range(CHUNKS)]
+        factors, rows = [], []
 
-        def load_plane(plane, src_rows, quadrants=range(4)):
-            for q in quadrants:
+        def load_plane(plane, src_rows):
+            for q in range(4):
                 nc.sync.dma_start(plane[32 * q : 32 * q + 4].bitcast(I32), src_rows[4 * q : 4 * q + 4].bitcast(I32))
 
-        def load_gain(target, wg, t, cols=slice(0, S)):
-            dealt = wg.rearrange("(p t) j -> t p j", t=4)[t]
-            for q in range(4):
-                nc.sync.dma_start(target[t][32 * q : 32 * q + 32, cols], dealt[:, cols])
+        def load_gain(side, t, cols=slice(0, S)):
+            dealt = (wg1, wg2)[side].rearrange("(p t) j -> t p j", t=4)[t]
+            for q in (0, 2, 1, 3):
+                nc.sync.dma_start((gain_a, gain_b)[side][t][32 * q : 32 * q + 32, cols], dealt[:, cols])
 
-        def deal_words(s, count, target):
-            nc.gpsimd.tensor_copy(
-                target.rearrange("p (t m e) -> p t m e", m=P, e=2),
-                w4_raw_w[:, columns(s // 4, H)].rearrange("p (m t e) -> p t m e", t=4, e=2)[:, s % 4 : s % 4 + count],
-            )
-            w4_w.extend(target[:, columns(t, 2 * P)] for t in range(count))
-
-        def deal_scales(s, count, target):
-            nc.gpsimd.tensor_copy(
-                target.rearrange("p (t m) -> p t m", m=P),
-                w4_raw_s[:, columns(s // 4)].rearrange("p (m t) -> p t m", t=4)[:, s % 4 : s % 4 + count],
-            )
-            w4_s.extend(target[:, columns(t, P)] for t in range(count))
-
-        def deal_w4(s, target):
-            deal_words(s, 1, target[:, 0 : 2 * P])
-            deal_scales(s, 1, target[:, 2 * P : 3 * P])
+        def load_w4_words(a):
+            nc.sync.dma_start(w4_raw_w[a][:].bitcast(I32), w4_words[0, :, columns(a, H)].bitcast(I32))
 
         def load_w1(a):
-            nc.sync.dma_start(w1_raw[a].rearrange("p (j c) -> p j c", j=4), w1[:, columns(a)].rearrange("(p j) c -> p j c", j=4))
-
-        def quantise_w1(a, t0, t1, grouped, cuts):
-            nc.scalar.copy(
-                grouped.rearrange("p (t m j) -> p m j t", m=P, j=4),
-                w1_raw[a].rearrange("p (j m t) -> p m j t", j=4, t=4)[:, :, :, t0:t1],
+            nc.sync.dma_start(
+                w1_raw[a][:].rearrange("p (j c) -> p j c", j=4), w1[:, columns(a)].rearrange("(p j) c -> p j c", j=4)
             )
-            for start, stop in cuts:
-                cols = slice((4 * a + start) * P, (4 * a + stop) * P)
-                nc.vector.quantize_mx(
-                    out=w1_w[:, cols].bitcast(FP8X4),
-                    scales=w1_s[:, cols],
-                    in_=grouped[:, (start - t0) * BANK : (stop - t0) * BANK],
-                )
 
-        def product(s, side, half, bank):
+        def load_plan(step):
+            a, t = pass_and_slot(step)
+            nc.sync.dma_start(rows[step % 2][:], plan.rearrange("(a p t) m -> a t p m", a=2, t=4)[a, t])
+
+        def deal_words(a):
+            nc.gpsimd.tensor_copy(
+                w4_w[a][:].rearrange("p (t m e) -> p t m e", m=P, e=2),
+                w4_raw_w[a][:].rearrange("p (m t e) -> p t m e", t=4, e=2),
+            )
+
+        def deal_scales(a, t0, t1, target):
+            nc.gpsimd.tensor_copy(
+                target.rearrange("p (t m) -> p t m", m=P),
+                w4_raw_s[:, columns(a)].rearrange("p (m t) -> p t m", t=4)[:, t0:t1],
+            )
+
+        def round_w1(a, t0, t1, target):
+            nc.scalar.copy(
+                target.rearrange("p (t m j) -> p m j t", m=P, j=4),
+                w1_raw[a][:].rearrange("p (j m t) -> p m j t", j=4, t=4)[:, :, :, t0:t1],
+            )
+
+        def quantise_w1(a, t0, t1, source):
+            cols = slice((4 * a + t0) * P, (4 * a + t1) * P)
+            nc.vector.quantize_mx(out=w1_w[:, cols].bitcast(FP8X4), scales=w1_s[:, cols], in_=source)
+
+        def product(step, side, cols, bank):
+            a, t = pass_and_slot(step)
             if side == 0:
-                weights, plane = w1_w[:, columns(s, P)].bitcast(FP8X4), w1_s[:, columns(s, P)]
+                weights, plane = w1_w[:, columns(4 * a + t, P)].bitcast(FP8X4), w1_s[:, columns(4 * a + t, P)]
             else:
-                weights, plane = w4_w[s].bitcast(FP4X4), w4_s[s]
+                weights = w4_w[a][:, columns(t, 2 * P)].bitcast(FP4X4)
+                plane = w4_s_first[:] if step == 0 else w4_s[a][:, columns(t - 1 + a, P)]
+            target = bank[:, 0 : cols.stop - cols.start]
             nc.tensor.matmul_mx(
-                out=bank[:],
+                out=target,
                 lhsT=weights,
                 lhsT_scale=plane,
-                rhs=v_w[:, columns(half)].bitcast(FP8X4),
-                rhs_scale=v_s[:, columns(half)],
+                rhs=v_w[:, cols].bitcast(FP8X4),
+                rhs_scale=v_s[:, cols],
                 start=True,
                 stop=True,
             )
+            return target
 
-        def feature_half(s, side, half, target, bank):
-            product(s, side, half, bank)
-            nc.scalar.activation(target, bank[:], ACT.Copy, scale=(-1.0, 1.0)[side])
+        def raw(side, cols):
+            return staged[:, side * S + cols.start : side * S + cols.stop]
 
-        def feature_piece(s, piece):
-            side, half = 1 - piece // 2, piece % 2
-            raw = raw_h[(s + side) % 2]
-            feature_half(s, side, half, raw[:, columns(half)], banks[half])
-            if half == 1:
-                nc.gpsimd.tensor_tensor((a_values(s), h_b[s % 3])[side], raw[:], (gain_a, gain_b)[side][s % 4][:], MULT)
+        def features(step, side, cols, bank, target):
+            nc.scalar.activation(target, product(step, side, cols, bank), ACT.Copy, scale=(-1.0, 1.0)[side])
 
-        def scatter_a(s):
-            nc.vector.tensor_copy(page_a[s % 2][:].indirect(list_a[:]), a_values(s))
+        def weigh(step, side, cols, source):
+            gain = (gain_a, gain_b)[side][ORDER[step] % 4]
+            nc.gpsimd.tensor_tensor(weighed[side][:, cols], source, gain[:, cols], MULT)
 
-        def scatter_b(s):
-            nc.vector.tensor_copy(page_b[s % 2][:].indirect(list_b[:]), h_b[s % 3])
+        def page(step, side):
+            return page_b[step % 2] if side else page_a
 
-        def load_plan(s, cols=slice(0, T2)):
-            nc.sync.dma_start(rows[s % 2][:, cols], plan.rearrange("(a p t) m -> a t p m", a=2, t=4)[s // 4, s % 4][:, cols])
+        def scatter(step, side, cols=slice(0, S)):
+            entries = (list_a, list_b)[side][:, cols.start // 16 : cols.stop // 16]
+            nc.vector.tensor_copy(page(step, side)[:].indirect(entries), weighed[side][:, cols])
 
-        def turn_pages(s, c):
-            bank = banks[c % 2]
-            for page in (page_b[s % 2], page_a[s % 2]):
-                for b in range(BLOCKS):
-                    nc.tensor.matmul(
-                        bank[:, columns(b, P)],
-                        lhsT=page[:, columns(BLOCKS * c + b, P)],
-                        rhs=ident[:],
-                        is_transpose=True,
-                        start=(page is page_b[s % 2] and b == 0),
-                        stop=(page is page_a[s % 2] and b == BLOCKS - 1),
-                    )
-            nc.scalar.activation(squares[(CHUNKS * s + c) % 3][:], bank[:], ACT.Square)
-
-        def turn_back(s, c):
-            bank = banks[2 + c % 2]
+        def turn_page(step, side, c, bank, opens):
             for b in range(BLOCKS):
-                nc.tensor.transpose(bank[:, columns(b, P)], squares[(CHUNKS * s + c) % 3][:, columns(b, P)], ident[:])
-            nc.scalar.activation(
-                factor(s, c), bank[:], ACT.Abs_reciprocal_sqrt, bias=ROOT * ROOT, scale=ROOT * ROOT
-            )
+                nc.tensor.matmul(
+                    bank[:, columns(b, P)],
+                    lhsT=page(step, side)[:, columns(BLOCKS * c + b, P)],
+                    rhs=ident[:],
+                    is_transpose=True,
+                    start=(opens and b == 0),
+                    stop=(not opens and b == BLOCKS - 1),
+                )
 
-        def finish(x):
-            nc.scalar.activation(x, x, ACT.Square, scale=ROOT)
+        def square(c, bank):
+            nc.scalar.activation(squares[c][:], bank[:], ACT.Square)
 
-        def damp_plan(engine, s, first, count, x):
-            cols = slice(first * BANK, (first + count) * BANK)
-            target = pairs[s // 4][:].rearrange("p (c u m e) -> p u e c m", u=2, m=BANK, e=2)
+        def turn_back(c, bank, blocks=range(BLOCKS)):
+            for b in blocks:
+                nc.tensor.transpose(bank[:, columns(b, P)], squares[c][:, columns(b, P)], ident[:])
+
+        def root(target, source):
+            nc.scalar.activation(target, source, ACT.Abs_reciprocal_sqrt, bias=ROOT * ROOT, scale=ROOT * ROOT)
+
+        def finish(target, source):
+            nc.scalar.activation(target, source, ACT.Square, scale=ROOT)
+
+        def damp_plan(engine, step, cols):
+            factor = factors[min(step, LAST - 1) % 2][:, cols]
+            a, t = pass_and_slot(step)
+            first, count = cols.start // HALF, (cols.stop - cols.start) // HALF
+            target = pairs[a][:].rearrange("p (c u m e) -> p u e c m", u=2, m=HALF, e=2)
             engine.tensor_tensor(
-                target[:, (s % 4) // 2, s % 2, first : first + count],
-                x.rearrange("p (c m) -> p c m", m=BANK),
-                rows[s % 2][:, cols].rearrange("p (c m) -> p c m", m=BANK),
+                target[:, t // 2, t % 2, first : first + count],
+                factor.rearrange("p (c m) -> p c m", m=HALF),
+                rows[step % 2][:, cols].rearrange("p (c m) -> p c m", m=HALF),
                 MULT,
             )
 
-        def weave(copy, a, c, target, part=slice(0, BANK // 4)):
-            source = pairs[a][:, columns(c, 4 * BANK)].bitcast(F32).rearrange("p (u g i) -> p g u i", u=2, i=4)
-            copy(target.bitcast(F32).rearrange("p (g i u) -> p g u i", u=2, i=4)[:, part], source[:, part])
+        def weave(copy, a, cols, target):
+            source = pairs[a][:, 4 * cols.start : 4 * cols.stop].bitcast(F32)
+            copy(
+                target.bitcast(F32).rearrange("p (c g i u) -> p c g u i", g=HALF // 4, u=2, i=4),
+                source.rearrange("p (c u g i) -> p c g u i", g=HALF // 4, u=2, i=4),
+            )
 
-        def window(page, entries, half):
-            return page[:].indirect(entries[:, columns(half, LIST_HALF)])
+        def first_weave(c):
+            weave(nc.scalar.copy, 0, columns(c), first_grouped[:, columns(c, 4 * BANK)])
 
+        quarters = [columns(i, HALF) for i in range(4)]
+        whole = slice(0, S)
         nc.gpsimd.memset(tab_s[:].bitcast(I32), 0)
-        nc.gpsimd.memset(w4_raw_s[:].bitcast(I32), 0)
+        nc.vector.memset(w4_raw_s[:].bitcast(I32), 0)
         nc.sync.dma_start(list_tab[:], offs)
+        load_w4_words(0)
         load_plane(tab_s, tab_scales[0])
-        nc.sync.dma_start(w4_raw_w[:, columns(0, H)].bitcast(I32), w4_words[0, :, columns(0, H)].bitcast(I32))
-        load_plane(w4_raw_s, w4_scales[0], range(1))
         nc.sync.dma_start(tab_w[:], tab_words[0].rearrange("p n t -> p (n t)").bitcast(I32))
-        load_plane(w4_raw_s, w4_scales[0], range(1, 4))
-        load_gain(gain_b, wg2, 0, columns(0))
+        load_plane(w4_raw_s, w4_scales[0])
         nc.sync.dma_start(list_b[:], offs3)
+        load_w4_words(1)
+        load_gain(1, 0, columns(0))
         load_w1(0)
-        load_gain(gain_b, wg2, 0, columns(1))
+        load_gain(1, 0, columns(1))
         nc.sync.dma_start(list_a[:], offs2)
-        load_gain(gain_a, wg1, 0)
+        load_gain(0, 0, columns(0))
+        load_gain(0, 0, columns(1))
         load_w1(1)
-        nc.sync.dma_start(w4_raw_w[:, columns(1, H)].bitcast(I32), w4_words[0, :, columns(1, H)].bitcast(I32))
-        load_gain(gain_b, wg2, 1)
-        load_gain(gain_a, wg1, 1)
-        for page in (page_b[0], page_a[0]):
-            nc.vector.memset(page[:].bitcast(I32), 0)
+        for side in (1, 0):
+            nc.vector.memset(page(0, side)[:].bitcast(I32), 0)
+        deal_words(0)
+        deal_scales(0, 0, 1, w4_s_first[:])
+        nc.vector.tensor_copy(v_s[:], tab_s[:].indirect(list_tab[:]))
+        for cols in (quarters[0], quarters[1], columns(1)):
+            entries = list_tab[:, cols.start // 16 : cols.stop // 16]
+            nc.vector.tensor_copy(v_w[:, cols], tab_w[:].bitcast(U32).indirect(entries))
+
+        first = product(0, 1, quarters[0], feats[0])
+        nc.vector.tensor_tensor(weighed[1][:, quarters[0]], first, gain_b[0][:, quarters[0]], MULT)
+        scatter(0, 1, quarters[0])
+        features(0, 1, quarters[1], feats[1], early[:])
+        weigh(0, 1, quarters[1], early[:])
+        scatter(0, 1, quarters[1])
+        features(0, 1, columns(1), backs[0], second[:])
+        deal_scales(1, 0, 4, w4_s[1][:])
+        deal_scales(0, 1, 4, w4_s[0][:])
+        page_b.append(tile([P, T2], F32, "page_b1"))
+        nc.gpsimd.memset(page_b[1][:].bitcast(I32), 0)
         make_identity(nc, ident[:])
         nc.gpsimd.memset(w8_s[:].rearrange("p a n -> p (a n)").bitcast(I32), 0)
-        deal_words(0, 2, tile([P, 4 * P], U8, "w4_first_words")[:])
-        deal_scales(0, 1, tile([P, P], U8, "w4_first")[:])
-        nc.vector.tensor_copy(v_s[:], tab_s[:].indirect(list_tab[:]))
+        w1_rounded = [tile([P, 4 * BANK], BF16, f"w1_rounded{a}") for a in range(2)]
+        round_w1(0, 0, 4, w1_rounded[0][:])
+        quantise_w1(0, 0, 4, w1_rounded[0][:])
+        weigh(0, 1, columns(1), second[:])
+        scatter(0, 1, columns(1))
+        w4_w.append(tile([P, H], U8, "w4_w1"))
+        deal_words(1)
         for half in range(2):
-            entries = list_tab[:, columns(half, LIST_HALF)]
-            nc.vector.tensor_copy(v_w[:, columns(half)], tab_w[:].bitcast(U32).indirect(entries))
-
-        product(0, 1, 0, banks[4])
-        nc.vector.tensor_tensor(h_b[0][:, columns(0)], banks[4][:], gain_b[0][:, columns(0)], MULT)
-        nc.vector.tensor_copy(window(page_b[0], list_b, 0), h_b[0][:, columns(0)])
-        quantise_w1(0, 0, 1, w1_first[:], [(0, 1)])
-        values = h_b[0][:, columns(1)]
-        feature_half(0, 1, 1, values, banks[5])
-        second = tile([P, 4 * P], U8, "w4_second", tag="w4_first")
-        deal_scales(1, 2, second[:, 0 : 2 * P])
-        deal_words(2, 1, second[:, 2 * P : 4 * P])
-        nc.vector.tensor_tensor(window(page_b[0], list_b, 1), values, gain_b[0][:, columns(1)], MULT)
+            features(0, 0, columns(half), feats[1 - half], raw(0, columns(half)))
+            weigh(0, 0, columns(half), raw(0, columns(half)))
+            scatter(0, 0, columns(half))
+        round_w1(1, 0, 4, w1_rounded[1][:])
+        quantise_w1(1, 0, 4, w1_rounded[1][:])
         for half in range(2):
-            feature_half(0, 0, half, h_a[0][:, columns(half)], banks[4 + half])
-        nc.vector.tensor_tensor(page_a[0][:].indirect(list_a[:]), h_a[0][:], gain_a[0][:], MULT)
-        quantise_w1(0, 1, 2, tile([P, BANK], BF16, "w1_second", tag="page_b1")[:], [(1, 2)])
-        quantise_w1(0, 2, 4, tile([P, 2 * BANK], BF16, "w1_third", tag="page_a1")[:], [(2, 4)])
-        for pages, name in ((page_b, "page_b1"), (page_a, "page_a1")):
-            pages.append(tile([P, T2], F32, name))
-            nc.gpsimd.memset(pages[1][:].bitcast(I32), 0)
-        quantise_w1(1, 0, 4, works[:, S + BANK : 2 * S + BANK].bitcast(BF16), [(0, 4)])
-
-        product(1, 1, 0, banks[0])
-        nc.vector.tensor_tensor(h_b[1][:, columns(0)], banks[0][:], gain_b[1][:, columns(0)], MULT)
-        nc.vector.tensor_copy(window(page_b[1], list_b, 0), h_b[1][:, columns(0)])
-        values = h_b[1][:, columns(1)]
-        feature_half(1, 1, 1, values, banks[1])
-        nc.gpsimd.tensor_tensor(values, values, gain_b[1][:, columns(1)], MULT)
-        nc.vector.tensor_copy(window(page_b[1], list_b, 1), values)
-        staged = tile([P, S], F32, "staged")
+            features(1, 1, columns(half), sums[half], w1_raw[1][:, columns(half)])
+        weigh(1, 1, whole, w1_raw[1][:, whole])
         for half in range(2):
-            feature_half(1, 0, half, staged[:, columns(half)], banks[4 + half])
-        nc.gpsimd.tensor_tensor(a_values(1), staged[:], gain_a[1][:], MULT)
-        scatter_a(1)
-        deal_w4(3, tile([P, 3 * P], U8, "w4_third", tag="staged")[:])
+            features(1, 0, columns(half), sums[2 + half], raw(0, columns(half)))
         rows.extend(tile([P, T2], F32, f"rows{i}") for i in range(2))
-        for s in range(2):
-            load_gain(gain_b, wg2, s + 2)
-            load_plan(s, columns(0, S))
-            load_gain(gain_a, wg1, s + 2)
-            load_plan(s, columns(1, S))
+        factors.extend(tile([P, T2], F32, f"factors{i}") for i in range(2))
+        for t in range(1, 4):
+            if t < 3:
+                load_plan(t - 1)
+            load_gain(1, t)
+            load_gain(0, t)
+        nc.sync.dma_start(w8_w[:], w8_words.rearrange("a p n t -> p a (n t)").bitcast(I32))
+        load_plane(w8_s, w8_scales.rearrange("a r n -> r a n"))
 
-        woven = []
-        for s in range(LAST):
-            if s > 0:
-                load_plan(s + 1)
-            if s == 1:
-                nc.sync.dma_start(w8_w[:], w8_words.rearrange("a p n t -> p a (n t)").bitcast(I32))
-                load_plane(w8_s, w8_scales.rearrange("a r n -> r a n"))
-            ahead = s + 2 <= LAST
-            late[s] = tile([P, S], F32, f"late_factors{s}", tag=f"late{s % 2}")
-            for c in range(CHUNKS + 1):
-                if c < CHUNKS:
-                    turn_pages(s, c)
-                    if s in (4, 5):
-                        piece = len(woven)
-                        woven.append(piece)
-                        weave(nc.scalar.copy, 0, piece // 2, first_grouped[:, columns(piece // 2, 4 * BANK)], columns(piece % 2, BANK // 8))
-                if c >= 1:
-                    turn_back(s, c - 1)
-                    if ahead:
-                        feature_piece(s + 2, c - 1)
-                if c in (2, 4) and ahead:
-                    finish(factor(s, c - 2, 2))
-                    damp_plan(nc.gpsimd, s, c - 2, 2, factor(s, c - 2, 2))
-                elif c >= 1 and not ahead:
-                    finish(factor(s, c - 1))
-                    damp_plan(nc.gpsimd, s, c - 1, 1, factor(s, c - 1))
+        def unfold(c, roots, targets):
+            share = BLOCKS // len(targets)
+            for i, bank in enumerate(targets):
+                turn_back(c, bank, range(share * i, share * (i + 1)))
+            for i, bank in enumerate(targets):
+                cols = columns(i, share * P)
+                root(roots[:, cols], bank[:, cols])
+
+        shared = tile([P, S + P], F32, "shared")
+        late_roots = [shared[:, HALF : HALF + BANK], tile([P, BANK], F32, "late_roots", tag="first_words0")[:]]
+        for step in range(LAST):
+            ahead = step + 2 <= LAST
+            if step > 0:
+                load_plan(step + 1)
+            scatter(step + 1, 1)
+            weigh(step + 1, 0, whole, raw(0, whole))
+            factor = factors[step % 2]
+            turns = (backs, feats)[step % 2]
+            if step >= LAST - 2:
+                first_weave(step - LAST + 2)
+            for c in range(2):
+                turn_page(step, 0, c, sums[c], True)
+                turn_page(step, 1, c, sums[c], False)
+                square(c, sums[c])
+            turn_page(step, 0, 2, sums[2], True)
+            unfold(0, factor[:, columns(0)], [turns[0]])
+            turn_page(step, 0, 3, sums[3], True)
+            for c in (2, 3):
+                turn_page(step, 1, c, sums[c], False)
+                square(c, sums[c])
+                if not ahead:
+                    finish(factor[:, columns(c - 2)], factor[:, columns(c - 2)])
+                    damp_plan(nc.gpsimd, step, columns(c - 2))
+                if c == 2:
+                    unfold(1, factor[:, columns(1)], [turns[1]])
+            for half in range(2 if ahead else 0):
+                features(step + 2, 1, columns(half), turns[half], raw(1, columns(half)))
             if ahead:
-                scatter_b(s + 2)
-                scatter_a(s + 2)
-            if s < 4:
-                deal_w4(4 + s, tile([P, 3 * P], U8, f"w4_slice{4 + s}", tag=f"late{s % 2}")[:])
+                finish(factor[:, columns(0, S)], factor[:, columns(0, S)])
+                weigh(step + 2, 1, whole, raw(1, whole))
+                damp_plan(nc.gpsimd, step, columns(0, S))
+            for half in range(2 if ahead else 0):
+                features(step + 2, 0, columns(half), turns[half], raw(0, columns(half)))
+            if ahead:
+                unfold(2, factor[:, columns(2)], sums[0:2])
+                unfold(3, factor[:, columns(3)], sums[2:4])
+                finish(factor[:, columns(1, S)], factor[:, columns(1, S)])
+            else:
+                for i in range(2):
+                    unfold(2 + i, late_roots[i], [feats[i]])
+                for i in range(2):
+                    finish(factor[:, columns(2 + i)], late_roots[i])
+            if ahead:
+                damp_plan(nc.gpsimd, step, columns(1, S))
+            else:
+                for c in (2, 3):
+                    damp_plan(nc.gpsimd, step, columns(c))
+                    first_weave(c)
+            scatter(step + 1, 0)
 
+        second_words = tile([P, T2], U32, "second_words")
+        first_words = {}
+        z_s = [tile([P, T2], U8, f"z_s{a}") for a in range(2)]
+        last = factors[(LAST - 1) % 2]
+        staging = [pair[:, columns(i)] for pair in gain_a + gain_b for i in range(2)]
+        free_banks = sums + backs + feats
+        emptied = []
 
-        z_w = [tile([P, T2], U32, "z_w0", tag="rows0"), tile([P, T2], U32, "z_w1", tag="page_b0")]
-        z_s = [tile([P, T2], U8, "z_s0"), tile([P, T2], U8, "z_s1")]
+        def words(a, cols):
+            if a == 1:
+                return second_words[:, cols].bitcast(FP8X4)
+            start = cols.start % BANK
+            return first_words[cols.start // BANK][:, start : start + cols.stop - cols.start].bitcast(FP8X4)
 
-        def first_codes(c):
-            nc.vector.quantize_mx(
-                out=z_w[0][:, columns(c)].bitcast(FP8X4),
-                scales=z_s[0][:, columns(c)],
-                in_=first_grouped[:, columns(c, 4 * BANK)],
-            )
+        def codes(a, cols):
+            c = cols.start // BANK
+            if a == 0 and c == 0:
+                both = tile([P, S], U32, "first_words0")
+                first_words.update({0: both[:, columns(0)], 1: both[:, columns(1)]})
+            if a == 0 and c >= 2:
+                first_words[c] = tile([P, BANK], U32, f"first_words{c}", tag=f"second_grouped{c - 2}")[:]
+            nc.vector.quantize_mx(out=words(a, cols), scales=z_s[a][:, cols], in_=z_values(a, cols))
 
-        def last_values(c):
-            if c < 2:
-                return late[LAST - 1][:, columns(c)]
-            return first_grouped[:, columns(c - 2, 4 * BANK)].bitcast(F32)[:, 0:BANK]
+        def z_values(a, cols):
+            if a == 0:
+                return first_grouped[:, 4 * cols.start : 4 * cols.stop]
+            start = cols.start % BANK
+            return second_grouped[cols.start // BANK][:, 4 * start : 4 * (start + cols.stop - cols.start)]
 
-        def last_factors(c):
-            x = last_values(c)
-            nc.vector.tensor_tensor(x, page_a[LAST % 2][:, columns(c)], page_b[LAST % 2][:, columns(c)], ADD)
-            nc.scalar.activation(x, x, ACT.Square)
-            nc.scalar.activation(x, x, ACT.Abs_reciprocal_sqrt, bias=ROOT * ROOT, scale=ROOT * ROOT)
-            finish(x)
+        def last_weave(cols):
+            weave(nc.vector.tensor_copy, 1, cols, z_values(1, cols))
 
-        def second_codes(c):
-            damp_plan(nc.vector, LAST, c, 1, last_values(c))
-            weave(nc.vector.tensor_copy, 1, c, second_grouped[c % 2][:])
-            nc.vector.quantize_mx(
-                out=z_w[1][:, columns(c)].bitcast(FP8X4), scales=z_s[1][:, columns(c)], in_=second_grouped[c % 2][:]
-            )
-
-        def last_product(c):
-            for n in range(BLOCKS):
-                k = BLOCKS * c + n
-                bank = banks[k % 8]
+        def last_product(cols, first_bank, engines, groups=None):
+            width = cols.stop - cols.start
+            share = BANK // width
+            groups = groups or range(BLOCKS // share)
+            for g in groups:
+                bank = free_banks[(first_bank + g - groups[0]) % 8]
                 for a in range(2):
-                    nc.tensor.matmul_mx(
-                        out=bank[:],
-                        lhsT=w8_w[:, a, columns(n, P)].bitcast(FP8X4),
-                        lhsT_scale=w8_s[:, a, columns(n, P)],
-                        rhs=z_w[a][:, columns(c)].bitcast(FP8X4),
-                        rhs_scale=z_s[a][:, columns(c)],
-                        start=(a == 0),
-                        stop=(a == 1),
-                    )
-                pair = (gain_a + gain_b)[k // 2]
-                (nc.vector.tensor_copy if k in ON_VECTOR else nc.scalar.copy)(pair[:, columns(k % 2)], bank[:])
-                nc.sync.dma_start(out[columns(n, P), columns(c)], pair[:, columns(k % 2)])
+                    for i in range(share):
+                        n = share * g + i
+                        nc.tensor.matmul_mx(
+                            out=bank[:, columns(i, width)],
+                            lhsT=w8_w[:, a, columns(n, P)].bitcast(FP8X4),
+                            lhsT_scale=w8_s[:, a, columns(n, P)],
+                            rhs=words(a, cols),
+                            rhs_scale=z_s[a][:, cols],
+                            start=(a == 0 and i == 0),
+                            stop=(a == 1 and i == share - 1),
+                        )
+                result = staging[len(emptied)]
+                emptied.append(g)
+                engines[g](result, bank[:])
+                target = out[columns(g, share * P), cols].rearrange("(i p) m -> p i m", p=P)
+                nc.sync.dma_start(target, result.rearrange("p (i m) -> p i m", i=share))
 
-        for step in range(CHUNKS + 1):
-            if step >= 1:
-                second_codes(step - 1)
-            if step < CHUNKS:
-                last_factors(step)
-                first_codes(step)
-        for c in range(CHUNKS):
-            last_product(c)
+        def values(cols):
+            start = P + cols.start % S
+            return shared[:, start : start + cols.stop - cols.start]
+
+        def add_pages(cols):
+            nc.vector.tensor_tensor(values(cols), page_a[:, cols], page(LAST, 1)[:, cols], ADD)
+
+        def last_square(cols):
+            nc.scalar.activation(values(cols), values(cols), ACT.Square)
+
+        def last_root(cols):
+            root(values(cols), values(cols))
+
+        def last_finish(cols):
+            finish(last[:, cols], values(cols))
+
+        on_vector, on_scalar = nc.vector.tensor_copy, nc.scalar.copy
+        eighths = [columns(i, HALF) for i in range(2 * CHUNKS)]
+        for h in range(2):
+            add_pages(eighths[h])
+        codes(0, columns(0))
+        add_pages(columns(1))
+        for stage in (last_square, last_root, last_finish):
+            for h in range(2):
+                stage(eighths[h])
+        codes(0, columns(1))
+        last_square(columns(1))
+        for h in range(2):
+            damp_plan(nc.vector, LAST, eighths[h])
+        add_pages(columns(2))
+        last_root(columns(1))
+        last_square(columns(2))
+        last_finish(columns(1))
+        for h in range(2):
+            last_weave(eighths[h])
+        for h in range(2):
+            codes(1, eighths[h])
+        last_root(columns(2))
+        last_product(eighths[0], 0, [on_scalar, on_scalar])
+        damp_plan(nc.vector, LAST, columns(1))
+        add_pages(columns(3))
+        last_finish(columns(2))
+        last_product(eighths[1], 2, [on_scalar, on_scalar])
+        last_weave(columns(1))
+        codes(0, columns(2))
+        codes(1, columns(1))
+        last_square(columns(3))
+        damp_plan(nc.vector, LAST, columns(2))
+        last_product(columns(1), 4, [on_scalar, on_scalar, on_scalar, on_scalar], (0,))
+        last_root(columns(3))
+        last_product(columns(1), 5, [on_scalar, on_scalar, on_scalar, on_scalar], (1,))
+        last_finish(columns(3))
+        last_product(columns(1), 6, [on_scalar, on_scalar, on_scalar, on_scalar], (2, 3))
+        codes(0, columns(3))
+        last_weave(columns(2))
+        damp_plan(nc.vector, LAST, eighths[6])
+        codes(1, columns(2))
+        damp_plan(nc.vector, LAST, eighths[7])
+        last_product(columns(2), 0, [on_scalar, on_scalar, on_scalar, on_scalar])
+        for h in range(2):
+            last_weave(eighths[6 + h])
+        for h in range(2):
+            codes(1, eighths[6 + h])
+        for h in range(2):
+            last_product(eighths[6 + h], 4 + 2 * h, [on_vector, on_vector])

@@ -68,9 +68,10 @@ def tile_list_trap_bench_release_kernel(
         gain_a = [tile([P, S], F32, f"gain_a{t}") for t in range(4)]
         gain_b = [tile([P, S], F32, f"gain_b{t}") for t in range(4)]
         ident = tile([P, P], F32, "ident")
-        page_a = tile([P, T2], F32, "page_a")
+        page_a = []
         page_b = [tile([P, T2], F32, "page_b0")]
-        early = tile([P, HALF], F32, "early", tag="page_b1")
+        early = tile([P, HALF], F32, "early", tag="page_a")
+        middle = tile([P, BANK], F32, "middle", tag="page_b1")
         second = tile([P, BANK], F32, "second", tag="w4_w1")
         staged = tile([P, 2 * S], F32, "staged")
         weighed = [tile([P, S], F32, "h_a"), tile([P, S], F32, "h_b")]
@@ -153,7 +154,7 @@ def tile_list_trap_bench_release_kernel(
             nc.gpsimd.tensor_tensor(weighed[side][:, cols], source, gain[:, cols], MULT)
 
         def page(step, side):
-            return page_b[step % 2] if side else page_a
+            return page_b[step % 2] if side else page_a[0]
 
         def scatter(step, side, cols=slice(0, S)):
             entries = (list_a, list_b)[side][:, cols.start // 16 : cols.stop // 16]
@@ -223,8 +224,7 @@ def tile_list_trap_bench_release_kernel(
         load_gain(0, 0, columns(0))
         load_gain(0, 0, columns(1))
         load_w1(1)
-        for side in (1, 0):
-            nc.vector.memset(page(0, side)[:].bitcast(I32), 0)
+        nc.vector.memset(page_b[0][:].bitcast(I32), 0)
         deal_words(0)
         deal_scales(0, 0, 1, w4_s_first[:])
         nc.vector.tensor_copy(v_s[:], tab_s[:].indirect(list_tab[:]))
@@ -241,8 +241,8 @@ def tile_list_trap_bench_release_kernel(
         features(0, 1, columns(1), backs[0], second[:])
         deal_scales(1, 0, 4, w4_s[1][:])
         deal_scales(0, 1, 4, w4_s[0][:])
-        page_b.append(tile([P, T2], F32, "page_b1"))
-        nc.gpsimd.memset(page_b[1][:].bitcast(I32), 0)
+        page_a.append(tile([P, T2], F32, "page_a"))
+        nc.gpsimd.memset(page_a[0][:].bitcast(I32), 0)
         make_identity(nc, ident[:])
         nc.gpsimd.memset(w8_s[:].rearrange("p a n -> p (a n)").bitcast(I32), 0)
         w1_rounded = [tile([P, 4 * BANK], BF16, f"w1_rounded{a}") for a in range(2)]
@@ -253,9 +253,12 @@ def tile_list_trap_bench_release_kernel(
         w4_w.append(tile([P, H], U8, "w4_w1"))
         deal_words(1)
         for half in range(2):
-            features(0, 0, columns(half), feats[1 - half], raw(0, columns(half)))
-            weigh(0, 0, columns(half), raw(0, columns(half)))
+            target = (raw(0, columns(0)), middle[:])[half]
+            features(0, 0, columns(half), feats[1 - half], target)
+            weigh(0, 0, columns(half), target)
             scatter(0, 0, columns(half))
+        page_b.append(tile([P, T2], F32, "page_b1"))
+        nc.gpsimd.memset(page_b[1][:].bitcast(I32), 0)
         round_w1(1, 0, 4, w1_rounded[1][:])
         quantise_w1(1, 0, 4, w1_rounded[1][:])
         for half in range(2):
@@ -321,8 +324,8 @@ def tile_list_trap_bench_release_kernel(
                 unfold(3, factor[:, columns(3)], sums[2:4])
                 finish(factor[:, columns(1, S)], factor[:, columns(1, S)])
             else:
-                for i in range(2):
-                    unfold(2 + i, late_roots[i], [feats[i]])
+                unfold(2, late_roots[0], [feats[0]])
+                unfold(3, late_roots[1], sums[2:4])
                 for i in range(2):
                     finish(factor[:, columns(2 + i)], late_roots[i])
             if ahead:
@@ -331,6 +334,8 @@ def tile_list_trap_bench_release_kernel(
                 for c in (2, 3):
                     damp_plan(nc.gpsimd, step, columns(c))
                     first_weave(c)
+                for c in (2, 3):
+                    turn_page(LAST, 1, c, sums[c], True)
             scatter(step + 1, 0)
 
         second_words = tile([P, T2], U32, "second_words")
@@ -338,7 +343,7 @@ def tile_list_trap_bench_release_kernel(
         z_s = [tile([P, T2], U8, f"z_s{a}") for a in range(2)]
         last = factors[(LAST - 1) % 2]
         staging = [pair[:, columns(i)] for pair in gain_a + gain_b for i in range(2)]
-        free_banks = sums + backs + feats
+        free_banks = sums[0:2] + backs + feats + sums[2:4]
         emptied = []
 
         def words(a, cols):
@@ -350,10 +355,8 @@ def tile_list_trap_bench_release_kernel(
         def codes(a, cols):
             c = cols.start // BANK
             if a == 0 and c == 0:
-                both = tile([P, S], U32, "first_words0")
-                first_words.update({0: both[:, columns(0)], 1: both[:, columns(1)]})
-            if a == 0 and c >= 2:
-                first_words[c] = tile([P, BANK], U32, f"first_words{c}", tag=f"second_grouped{c - 2}")[:]
+                every = tile([P, T2], U32, "first_words0")
+                first_words.update({i: every[:, columns(i)] for i in range(CHUNKS)})
             nc.vector.quantize_mx(out=words(a, cols), scales=z_s[a][:, cols], in_=z_values(a, cols))
 
         def z_values(a, cols):
@@ -365,12 +368,12 @@ def tile_list_trap_bench_release_kernel(
         def last_weave(cols):
             weave(nc.vector.tensor_copy, 1, cols, z_values(1, cols))
 
-        def last_product(cols, first_bank, engines, groups=None):
+        def last_product(cols, engines, groups=None):
             width = cols.stop - cols.start
             share = BANK // width
             groups = groups or range(BLOCKS // share)
             for g in groups:
-                bank = free_banks[(first_bank + g - groups[0]) % 8]
+                bank = free_banks[len(emptied) % 8]
                 for a in range(2):
                     for i in range(share):
                         n = share * g + i
@@ -390,11 +393,12 @@ def tile_list_trap_bench_release_kernel(
                 nc.sync.dma_start(target, result.rearrange("p (i m) -> p i m", i=share))
 
         def values(cols):
-            start = P + cols.start % S
-            return shared[:, start : start + cols.stop - cols.start]
+            if cols.start >= S:
+                return first_grouped[:, 4 * (cols.start - S) : 4 * (cols.stop - S)].bitcast(F32)[:, 0:BANK]
+            return shared[:, P + cols.start : P + cols.stop]
 
         def add_pages(cols):
-            nc.vector.tensor_tensor(values(cols), page_a[:, cols], page(LAST, 1)[:, cols], ADD)
+            nc.vector.tensor_tensor(values(cols), page(LAST, 0)[:, cols], page(LAST, 1)[:, cols], ADD)
 
         def last_square(cols):
             nc.scalar.activation(values(cols), values(cols), ACT.Square)
@@ -406,51 +410,24 @@ def tile_list_trap_bench_release_kernel(
             finish(last[:, cols], values(cols))
 
         on_vector, on_scalar = nc.vector.tensor_copy, nc.scalar.copy
-        eighths = [columns(i, HALF) for i in range(2 * CHUNKS)]
-        for h in range(2):
-            add_pages(eighths[h])
-        codes(0, columns(0))
-        add_pages(columns(1))
-        for stage in (last_square, last_root, last_finish):
-            for h in range(2):
-                stage(eighths[h])
-        codes(0, columns(1))
-        last_square(columns(1))
-        for h in range(2):
-            damp_plan(nc.vector, LAST, eighths[h])
-        add_pages(columns(2))
-        last_root(columns(1))
-        last_square(columns(2))
-        last_finish(columns(1))
-        for h in range(2):
-            last_weave(eighths[h])
-        for h in range(2):
-            codes(1, eighths[h])
-        last_root(columns(2))
-        last_product(eighths[0], 0, [on_scalar, on_scalar])
-        damp_plan(nc.vector, LAST, columns(1))
-        add_pages(columns(3))
-        last_finish(columns(2))
-        last_product(eighths[1], 2, [on_scalar, on_scalar])
-        last_weave(columns(1))
-        codes(0, columns(2))
-        codes(1, columns(1))
-        last_square(columns(3))
-        damp_plan(nc.vector, LAST, columns(2))
-        last_product(columns(1), 4, [on_scalar, on_scalar, on_scalar, on_scalar], (0,))
-        last_root(columns(3))
-        last_product(columns(1), 5, [on_scalar, on_scalar, on_scalar, on_scalar], (1,))
-        last_finish(columns(3))
-        last_product(columns(1), 6, [on_scalar, on_scalar, on_scalar, on_scalar], (2, 3))
-        codes(0, columns(3))
-        last_weave(columns(2))
-        damp_plan(nc.vector, LAST, eighths[6])
-        codes(1, columns(2))
-        damp_plan(nc.vector, LAST, eighths[7])
-        last_product(columns(2), 0, [on_scalar, on_scalar, on_scalar, on_scalar])
-        for h in range(2):
-            last_weave(eighths[6 + h])
-        for h in range(2):
-            codes(1, eighths[6 + h])
-        for h in range(2):
-            last_product(eighths[6 + h], 4 + 2 * h, [on_vector, on_vector])
+        for c in range(CHUNKS + 1):
+            if c >= 1:
+                damp_plan(nc.vector, LAST, columns(c - 1))
+                last_weave(columns(c - 1))
+                codes(1, columns(c - 1))
+            if c < 2:
+                add_pages(columns(c))
+                last_square(columns(c))
+                last_root(columns(c))
+                last_finish(columns(c))
+            elif c < CHUNKS:
+                turn_page(LAST, 0, c, sums[c], False)
+                squares[c] = values(columns(c))
+                square(c, sums[c])
+                turn_back(c, sums[c])
+                root(last[:, columns(c)], sums[c][:])
+                finish(last[:, columns(c)], last[:, columns(c)])
+            if c < CHUNKS:
+                codes(0, columns(c))
+        for c in range(CHUNKS):
+            last_product(columns(c), [on_vector if BLOCKS * c + n in (9, 11, 13, 15) else on_scalar for n in range(BLOCKS)])

@@ -23,10 +23,11 @@ BANK = 512
 HALF = BANK // 2
 CHUNKS = T2 // BANK
 BLOCKS = BANK // P
-STEPS = H // P
-LAST = STEPS - 1
-ORDER = (0, 4, 1, 2, 3, 5, 6, 7)
+SLICES = H // P
+LAST = SLICES - 1
+ORDER = ((0, 0), (1, 0), (0, 1), (1, 1), (0, 2), (0, 3), (1, 2), (1, 3))
 ROOT = 75.0 / 64.0
+A, B = 0, 1
 
 
 def tile_list_trap_bench_release_kernel(
@@ -37,7 +38,7 @@ def tile_list_trap_bench_release_kernel(
         keep = ctx.enter_context(tc.tile_pool(name="keep", bufs=1))
         psum = ctx.enter_context(tc.psum_pool(name="psum", bufs=1))
         banks = [psum.tile([P, BANK], F32, name=f"bank{b}") for b in range(8)]
-        sums, backs, feats = banks[0:4], banks[4:6], banks[6:8]
+        sums, backs, spare = banks[0:4], banks[4:6], banks[6:8]
 
         def columns(i, width=BANK):
             return slice(i * width, (i + 1) * width)
@@ -45,41 +46,37 @@ def tile_list_trap_bench_release_kernel(
         def tile(shape, dtype, name, tag=None):
             return keep.tile(shape, dtype, name=name, tag=tag or name, align_bytes=64)
 
-        def pass_and_slot(step):
-            return divmod(ORDER[step], 4)
-
         list_tab = tile([P, S // 16], U16, "list_tab")
-        list_a = tile([P, S // 16], U16, "list_a")
-        list_b = tile([P, S // 16], U16, "list_b")
+        lists = [tile([P, S // 16], U16, "list_a"), tile([P, S // 16], U16, "list_b")]
         tab_w = tile([P, T], I32, "tab_w", tag="rows0")
         tab_s = tile([P, T], U8, "tab_s")
         v_w = tile([P, S], U32, "v_w")
         v_s = tile([P, S], U8, "v_s")
-        w1_raw = [tile([P, T2], F32, "w1_raw0", tag="rows1"), tile([P, T2], F32, "w1_raw1", tag="factors1")]
+        w1_raw = [tile([P, T2], F32, "w1_raw0", tag="rows1"), tile([P, T2], F32, "w1_raw1")]
+        w1_rounded = tile([P, 4 * H], BF16, "w1_rounded")
         w1_w = tile([P, H], U32, "w1_w")
         w1_s = tile([P, H], U8, "w1_s")
-        w4_raw_w = [tile([P, H], U8, f"w4_raw_w{a}") for a in range(2)]
-        w4_raw_s = tile([P, H], U8, "w4_raw_s")
-        w4_w = [tile([P, H], U8, "w4_w0")]
-        w4_s_first = tile([P, P], U8, "w4_s_first")
-        w4_s = [tile([P, 3 * P], U8, "w4_s0"), tile([P, 4 * P], U8, "w4_s1")]
+        w4_raw_w = tile([P, 2 * H], U8, "w4_raw_w")
+        w4_raw_s = tile([P, H], U8, "w4_raw_s", tag="w4_rest_w")
+        w4_first_w = tile([P, 4 * P], U8, "w4_first_w")
+        w4_first_s = tile([P, 2 * P], U8, "w4_first_s")
+        w4_rest_s = tile([P, 6 * P], U8, "w4_rest_s")
+        w4_rest_w = []
         w8_w = tile([P, 2, N], I32, "w8_w")
         w8_s = tile([P, 2, N], U8, "w8_s")
-        gain_a = [tile([P, S], F32, f"gain_a{t}") for t in range(4)]
-        gain_b = [tile([P, S], F32, f"gain_b{t}") for t in range(4)]
+        gains = [[tile([P, S], F32, f"gain{side}{t}") for t in range(4)] for side in (A, B)]
         ident = tile([P, P], F32, "ident")
-        page_a = []
-        page_b = [tile([P, T2], F32, "page_b0")]
-        early = tile([P, HALF], F32, "early", tag="page_a")
-        middle = tile([P, BANK], F32, "middle", tag="page_b1")
-        second = tile([P, BANK], F32, "second", tag="w4_w1")
-        staged = tile([P, 2 * S], F32, "staged")
-        weighed = [tile([P, S], F32, "h_a"), tile([P, S], F32, "h_b")]
-        squares = [tile([P, BANK], F32, f"squares{i}") for i in range(CHUNKS)]
-        pairs = [tile([P, 4 * T2], BF16, f"pairs{a}") for a in range(2)]
-        first_grouped = tile([P, 4 * T2], BF16, "first_grouped")
-        second_grouped = [tile([P, 4 * BANK], BF16, f"second_grouped{i}") for i in range(CHUNKS)]
-        factors, rows = [], []
+        pages = [[], [tile([P, T2], F32, f"page_b{i}") for i in range(2)]]
+        ahead_of_page = [tile([P, BANK], F32, f"ahead_of_page{i}", tag=f"page_a{i}") for i in range(2)]
+        weighed = [[tile([P, S], F32, f"weighed{side}{i}") for i in range(2)] for side in (A, B)]
+        all_squares = tile([P, T2], F32, "all_squares")
+        squares = [all_squares[:, columns(c)] for c in range(CHUNKS)]
+        roots = [tile([P, BANK], F32, f"roots{c}")[:] for c in range(CHUNKS - 1)]
+        roots.append(all_squares[:].rearrange("p (c m) -> p c m", c=CHUNKS)[:, :, 0:P])
+        factors = [[tile([P, BANK], F32, f"factors{i}{c}") for c in range(CHUNKS)] for i in range(2)]
+        pairs = [[tile([P, 4 * BANK], BF16, f"pairs{a}{c}") for c in range(CHUNKS)] for a in range(2)]
+        grouped = [[], []]
+        rows = []
 
         def load_plane(plane, src_rows):
             for q in range(4):
@@ -87,96 +84,70 @@ def tile_list_trap_bench_release_kernel(
 
         def load_gain(side, t, cols=slice(0, S)):
             dealt = (wg1, wg2)[side].rearrange("(p t) j -> t p j", t=4)[t]
+            if t > 0:
+                nc.sync.dma_start(gains[side][t][:], dealt.unsqueeze(0).to_broadcast([4, 32, S]))
+                return
             for q in (0, 2, 1, 3):
-                nc.sync.dma_start((gain_a, gain_b)[side][t][32 * q : 32 * q + 32, cols], dealt[:, cols])
-
-        def load_w4_words(a):
-            nc.sync.dma_start(w4_raw_w[a][:].bitcast(I32), w4_words[0, :, columns(a, H)].bitcast(I32))
+                nc.sync.dma_start(gains[side][t][32 * q : 32 * q + 32, cols], dealt[:, cols])
 
         def load_w1(a):
             nc.sync.dma_start(
                 w1_raw[a][:].rearrange("p (j c) -> p j c", j=4), w1[:, columns(a)].rearrange("(p j) c -> p j c", j=4)
             )
 
-        def load_plan(step):
-            a, t = pass_and_slot(step)
-            nc.sync.dma_start(rows[step % 2][:], plan.rearrange("(a p t) m -> a t p m", a=2, t=4)[a, t])
+        def load_plan(s):
+            nc.sync.dma_start(rows[s % 3][:], plan.rearrange("(a p t) m -> a t p m", a=2, t=4)[ORDER[s]])
 
-        def deal_words(a):
-            nc.gpsimd.tensor_copy(
-                w4_w[a][:].rearrange("p (t m e) -> p t m e", m=P, e=2),
-                w4_raw_w[a][:].rearrange("p (m t e) -> p t m e", t=4, e=2),
-            )
-
-        def deal_scales(a, t0, t1, target):
-            nc.gpsimd.tensor_copy(
-                target.rearrange("p (t m) -> p t m", m=P),
-                w4_raw_s[:, columns(a)].rearrange("p (m t) -> p t m", t=4)[:, t0:t1],
-            )
-
-        def round_w1(a, t0, t1, target):
+        def round_w1(a):
             nc.scalar.copy(
-                target.rearrange("p (t m j) -> p m j t", m=P, j=4),
-                w1_raw[a][:].rearrange("p (j m t) -> p m j t", j=4, t=4)[:, :, :, t0:t1],
+                w1_rounded[:, columns(a, 4 * BANK)].rearrange("p (t m j) -> p m j t", m=P, j=4),
+                w1_raw[a][:].rearrange("p (j m t) -> p m j t", j=4, t=4),
             )
 
-        def quantise_w1(a, t0, t1, source):
-            cols = slice((4 * a + t0) * P, (4 * a + t1) * P)
-            nc.vector.quantize_mx(out=w1_w[:, cols].bitcast(FP8X4), scales=w1_s[:, cols], in_=source)
-
-        def product(step, side, cols, bank):
-            a, t = pass_and_slot(step)
-            if side == 0:
+        def product(s, side, half, bank):
+            a, t = ORDER[s]
+            if side == A:
                 weights, plane = w1_w[:, columns(4 * a + t, P)].bitcast(FP8X4), w1_s[:, columns(4 * a + t, P)]
+            elif t == 0:
+                weights, plane = w4_first_w[:, columns(a, 2 * P)].bitcast(FP4X4), w4_first_s[:, columns(a, P)]
             else:
-                weights = w4_w[a][:, columns(t, 2 * P)].bitcast(FP4X4)
-                plane = w4_s_first[:] if step == 0 else w4_s[a][:, columns(t - 1 + a, P)]
-            target = bank[:, 0 : cols.stop - cols.start]
+                weights, plane = w4_rest_w[0][:, columns(2 * t - 2 + a, 2 * P)].bitcast(FP4X4), w4_rest_s[:, columns(2 * t - 2 + a, P)]
             nc.tensor.matmul_mx(
-                out=target,
+                out=bank[:],
                 lhsT=weights,
                 lhsT_scale=plane,
-                rhs=v_w[:, cols].bitcast(FP8X4),
-                rhs_scale=v_s[:, cols],
+                rhs=v_w[:, columns(half)].bitcast(FP8X4),
+                rhs_scale=v_s[:, columns(half)],
                 start=True,
                 stop=True,
             )
-            return target
 
-        def raw(side, cols):
-            return staged[:, side * S + cols.start : side * S + cols.stop]
+        def features(s, side, half, bank, target=None):
+            product(s, side, half, bank)
+            target = weighed[side][s % 2][:, columns(half)] if target is None else target
+            nc.scalar.activation(target, bank[:], ACT.Copy, scale=(-1.0, 1.0)[side])
 
-        def features(step, side, cols, bank, target):
-            nc.scalar.activation(target, product(step, side, cols, bank), ACT.Copy, scale=(-1.0, 1.0)[side])
+        def weigh(s, side, cols=slice(0, S), source=None):
+            target = weighed[side][s % 2][:, cols]
+            nc.gpsimd.tensor_tensor(target, target if source is None else source, gains[side][ORDER[s][1]][:, cols], MULT)
 
-        def weigh(step, side, cols, source):
-            gain = (gain_a, gain_b)[side][ORDER[step] % 4]
-            nc.gpsimd.tensor_tensor(weighed[side][:, cols], source, gain[:, cols], MULT)
+        def scatter(s, side, cols=slice(0, S)):
+            entries = lists[side][:, cols.start // 16 : cols.stop // 16]
+            nc.vector.tensor_copy(pages[side][s % 2][:].indirect(entries), weighed[side][s % 2][:, cols])
 
-        def page(step, side):
-            return page_b[step % 2] if side else page_a[0]
-
-        def scatter(step, side, cols=slice(0, S)):
-            entries = (list_a, list_b)[side][:, cols.start // 16 : cols.stop // 16]
-            nc.vector.tensor_copy(page(step, side)[:].indirect(entries), weighed[side][:, cols])
-
-        def turn_page(step, side, c, bank, opens):
+        def turn_page(s, side, c):
             for b in range(BLOCKS):
                 nc.tensor.matmul(
-                    bank[:, columns(b, P)],
-                    lhsT=page(step, side)[:, columns(BLOCKS * c + b, P)],
+                    sums[c][:, columns(b, P)],
+                    lhsT=pages[side][s % 2][:, columns(BLOCKS * c + b, P)],
                     rhs=ident[:],
                     is_transpose=True,
-                    start=(opens and b == 0),
-                    stop=(not opens and b == BLOCKS - 1),
+                    start=(side == B and b == 0),
+                    stop=(side == A and b == BLOCKS - 1),
                 )
 
-        def square(c, bank):
-            nc.scalar.activation(squares[c][:], bank[:], ACT.Square)
-
-        def turn_back(c, bank, blocks=range(BLOCKS)):
-            for b in blocks:
-                nc.tensor.transpose(bank[:, columns(b, P)], squares[c][:, columns(b, P)], ident[:])
+        def square(target, source):
+            nc.scalar.activation(target, source, ACT.Square)
 
         def root(target, source):
             nc.scalar.activation(target, source, ACT.Abs_reciprocal_sqrt, bias=ROOT * ROOT, scale=ROOT * ROOT)
@@ -184,250 +155,252 @@ def tile_list_trap_bench_release_kernel(
         def finish(target, source):
             nc.scalar.activation(target, source, ACT.Square, scale=ROOT)
 
-        def damp_plan(engine, step, cols):
-            factor = factors[min(step, LAST - 1) % 2][:, cols]
-            a, t = pass_and_slot(step)
-            first, count = cols.start // HALF, (cols.stop - cols.start) // HALF
-            target = pairs[a][:].rearrange("p (c u m e) -> p u e c m", u=2, m=HALF, e=2)
-            engine.tensor_tensor(
-                target[:, t // 2, t % 2, first : first + count],
-                factor.rearrange("p (c m) -> p c m", m=HALF),
-                rows[step % 2][:, cols].rearrange("p (c m) -> p c m", m=HALF),
-                MULT,
-            )
+        def by_blocks(values):
+            return values if len(values.shape) == 3 else values.rearrange("p (b m) -> p b m", m=P)
 
-        def weave(copy, a, cols, target):
-            source = pairs[a][:, 4 * cols.start : 4 * cols.stop].bitcast(F32)
+        def unfold(c, squared, targets):
+            share = BLOCKS // len(targets)
+            for b in range(BLOCKS):
+                nc.tensor.transpose(targets[b // share][:, columns(b, P)], squared[:, columns(b, P)], ident[:])
+            for i, bank in enumerate(targets):
+                blocks = columns(i, share)
+                root(by_blocks(roots[c])[:, blocks], by_blocks(bank[:])[:, blocks])
+
+        def factor(s, c):
+            finish(by_blocks(factors[s % 2][c][:]), by_blocks(roots[c]))
+
+        def damp_plan(engine, s, c, cols=slice(0, BANK)):
+            a, t = ORDER[s]
+            target = pairs[a][c][:].rearrange("p (u m e) -> p u e m", u=2, e=2)[:, t // 2, t % 2]
+            engine.tensor_tensor(target[:, cols], factors[s % 2][c][:, cols], rows[s % 3][:, columns(c)][:, cols], MULT)
+
+        def weave(copy, a, c, word, cols=slice(0, BANK)):
+            fours = slice(cols.start // 4, cols.stop // 4)
             copy(
-                target.bitcast(F32).rearrange("p (c g i u) -> p c g u i", g=HALF // 4, u=2, i=4),
-                source.rearrange("p (c u g i) -> p c g u i", g=HALF // 4, u=2, i=4),
+                grouped[a][c].bitcast(word).rearrange("p (g i u) -> p g u i", u=2, i=4)[:, fours],
+                pairs[a][c][:].bitcast(word).rearrange("p (u g i) -> p g u i", u=2, i=4)[:, fours],
             )
 
-        def first_weave(c):
-            weave(nc.scalar.copy, 0, columns(c), first_grouped[:, columns(c, 4 * BANK)])
-
-        quarters = [columns(i, HALF) for i in range(4)]
-        whole = slice(0, S)
+        first, second = columns(0), columns(1)
         nc.gpsimd.memset(tab_s[:].bitcast(I32), 0)
         nc.vector.memset(w4_raw_s[:].bitcast(I32), 0)
         nc.sync.dma_start(list_tab[:], offs)
-        load_w4_words(0)
+        nc.sync.dma_start(lists[B][:], offs3)
         load_plane(tab_s, tab_scales[0])
         nc.sync.dma_start(tab_w[:], tab_words[0].rearrange("p n t -> p (n t)").bitcast(I32))
+        nc.sync.dma_start(w4_raw_w[:].bitcast(I32), w4_words[0].bitcast(I32))
         load_plane(w4_raw_s, w4_scales[0])
-        nc.sync.dma_start(list_b[:], offs3)
-        load_w4_words(1)
-        load_gain(1, 0, columns(0))
+        load_gain(B, 0, first)
+        load_gain(B, 0, second)
         load_w1(0)
-        load_gain(1, 0, columns(1))
-        nc.sync.dma_start(list_a[:], offs2)
-        load_gain(0, 0, columns(0))
-        load_gain(0, 0, columns(1))
         load_w1(1)
-        nc.vector.memset(page_b[0][:].bitcast(I32), 0)
-        deal_words(0)
-        deal_scales(0, 0, 1, w4_s_first[:])
-        nc.vector.tensor_copy(v_s[:], tab_s[:].indirect(list_tab[:]))
-        for cols in (quarters[0], quarters[1], columns(1)):
-            entries = list_tab[:, cols.start // 16 : cols.stop // 16]
-            nc.vector.tensor_copy(v_w[:, cols], tab_w[:].bitcast(U32).indirect(entries))
-
-        first = product(0, 1, quarters[0], feats[0])
-        nc.vector.tensor_tensor(weighed[1][:, quarters[0]], first, gain_b[0][:, quarters[0]], MULT)
-        scatter(0, 1, quarters[0])
-        features(0, 1, quarters[1], feats[1], early[:])
-        weigh(0, 1, quarters[1], early[:])
-        scatter(0, 1, quarters[1])
-        features(0, 1, columns(1), backs[0], second[:])
-        deal_scales(1, 0, 4, w4_s[1][:])
-        deal_scales(0, 1, 4, w4_s[0][:])
-        page_a.append(tile([P, T2], F32, "page_a"))
-        nc.gpsimd.memset(page_a[0][:].bitcast(I32), 0)
+        nc.sync.dma_start(lists[A][:], offs2)
+        load_gain(A, 0)
+        load_gain(B, 1)
+        nc.vector.memset(pages[B][0][:].bitcast(I32), 0)
+        raw_words = w4_raw_w[:].rearrange("p (a m t e) -> p t a m e", a=2, t=4, e=2)
+        raw_scales = w4_raw_s[:].rearrange("p (a m t) -> p t a m", a=2, t=4)
+        nc.gpsimd.tensor_copy(w4_first_w[:].rearrange("p (a m e) -> p a m e", a=2, e=2), raw_words[:, 0])
+        nc.gpsimd.tensor_copy(w4_first_s[:].rearrange("p (a m) -> p a m", a=2), raw_scales[:, 0])
+        nc.gpsimd.memset(pages[B][1][:].bitcast(I32), 0)
         make_identity(nc, ident[:])
         nc.gpsimd.memset(w8_s[:].rearrange("p a n -> p (a n)").bitcast(I32), 0)
-        w1_rounded = [tile([P, 4 * BANK], BF16, f"w1_rounded{a}") for a in range(2)]
-        round_w1(0, 0, 4, w1_rounded[0][:])
-        quantise_w1(0, 0, 4, w1_rounded[0][:])
-        weigh(0, 1, columns(1), second[:])
-        scatter(0, 1, columns(1))
-        w4_w.append(tile([P, H], U8, "w4_w1"))
-        deal_words(1)
+        nc.vector.tensor_copy(v_s[:], tab_s[:].indirect(list_tab[:]))
         for half in range(2):
-            target = (raw(0, columns(0)), middle[:])[half]
-            features(0, 0, columns(half), feats[1 - half], target)
-            weigh(0, 0, columns(half), target)
-            scatter(0, 0, columns(half))
-        page_b.append(tile([P, T2], F32, "page_b1"))
-        nc.gpsimd.memset(page_b[1][:].bitcast(I32), 0)
-        round_w1(1, 0, 4, w1_rounded[1][:])
-        quantise_w1(1, 0, 4, w1_rounded[1][:])
-        for half in range(2):
-            features(1, 1, columns(half), sums[half], w1_raw[1][:, columns(half)])
-        weigh(1, 1, whole, w1_raw[1][:, whole])
-        for half in range(2):
-            features(1, 0, columns(half), sums[2 + half], raw(0, columns(half)))
-        rows.extend(tile([P, T2], F32, f"rows{i}") for i in range(2))
-        factors.extend(tile([P, T2], F32, f"factors{i}") for i in range(2))
-        for t in range(1, 4):
-            if t < 3:
-                load_plan(t - 1)
-            load_gain(1, t)
-            load_gain(0, t)
-        nc.sync.dma_start(w8_w[:], w8_words.rearrange("a p n t -> p a (n t)").bitcast(I32))
-        load_plane(w8_s, w8_scales.rearrange("a r n -> r a n"))
+            entries = list_tab[:, columns(half, BANK // 16)]
+            nc.vector.tensor_copy(v_w[:, columns(half)], tab_w[:].bitcast(U32).indirect(entries))
 
-        def unfold(c, roots, targets):
-            share = BLOCKS // len(targets)
-            for i, bank in enumerate(targets):
-                turn_back(c, bank, range(share * i, share * (i + 1)))
-            for i, bank in enumerate(targets):
-                cols = columns(i, share * P)
-                root(roots[:, cols], bank[:, cols])
+        product(0, B, 0, spare[0])
+        nc.vector.tensor_tensor(weighed[B][0][:, first], spare[0][:], gains[B][0][:, first], MULT)
+        scatter(0, B, first)
+        features(1, B, 0, spare[1])
+        weigh(1, B, first)
+        scatter(1, B, first)
+        features(0, B, 1, backs[0], ahead_of_page[0][:])
+        weigh(0, B, second, ahead_of_page[0][:])
+        scatter(0, B, second)
+        nc.gpsimd.tensor_copy(w4_rest_s[:].rearrange("p (t a m) -> p t a m", a=2, m=P), raw_scales[:, 1:4])
+        w4_rest_w.append(tile([P, 12 * P], U8, "w4_rest_w"))
+        nc.gpsimd.tensor_copy(w4_rest_w[0][:].rearrange("p (t a m e) -> p t a m e", a=2, m=P, e=2), raw_words[:, 1:4])
+        pages[A].append(tile([P, T2], F32, "page_a0"))
+        nc.gpsimd.memset(pages[A][0][:].bitcast(I32), 0)
+        round_w1(0)
+        round_w1(1)
+        nc.vector.quantize_mx(out=w1_w[:].bitcast(FP8X4), scales=w1_s[:], in_=w1_rounded[:])
+        features(1, B, 1, backs[1], w1_raw[1][:, second])
+        weigh(1, B, second, w1_raw[1][:, second])
+        scatter(1, B, second)
+        features(0, A, 0, sums[0])
+        weigh(0, A, first)
+        scatter(0, A, first)
+        features(0, A, 1, sums[1], ahead_of_page[1][:])
+        weigh(0, A, second, ahead_of_page[1][:])
+        scatter(0, A, second)
+        pages[A].append(tile([P, T2], F32, "page_a1"))
+        nc.gpsimd.memset(pages[A][1][:].bitcast(I32), 0)
+        for half in range(2):
+            features(1, A, half, sums[2 + half])
+        weigh(1, A)
+        scatter(1, A)
+        for half in range(2):
+            features(2, B, half, sums[half])
+        weigh(2, B)
+        unweighed = [tile([P, S], F32, f"unweighed{i}") for i in range(2)]
+        third = unweighed[0]
+        for half in range(2):
+            features(2, A, half, sums[2 + half], third[:, columns(half)])
+        rows.extend(tile([P, T2], F32, f"rows{i}") for i in range(3))
+        load_gain(A, 1)
+        weigh(2, A, source=third[:])
+        load_plan(0)
+        load_plan(1)
+        load_gain(B, 2)
+        load_plan(2)
+        load_gain(A, 2)
+        load_gain(B, 3)
+        load_gain(A, 3)
+        for c in range(CHUNKS):
+            turn_page(0, B, c)
 
-        shared = tile([P, S + P], F32, "shared")
-        late_roots = [shared[:, HALF : HALF + BANK], tile([P, BANK], F32, "late_roots", tag="first_words0")[:]]
-        for step in range(LAST):
-            ahead = step + 2 <= LAST
-            if step > 0:
-                load_plan(step + 1)
-            scatter(step + 1, 1)
-            weigh(step + 1, 0, whole, raw(0, whole))
-            factor = factors[step % 2]
-            turns = (backs, feats)[step % 2]
-            if step >= LAST - 2:
-                first_weave(step - LAST + 2)
-            for c in range(2):
-                turn_page(step, 0, c, sums[c], True)
-                turn_page(step, 1, c, sums[c], False)
-                square(c, sums[c])
-            turn_page(step, 0, 2, sums[2], True)
-            unfold(0, factor[:, columns(0)], [turns[0]])
-            turn_page(step, 0, 3, sums[3], True)
-            for c in (2, 3):
-                turn_page(step, 1, c, sums[c], False)
-                square(c, sums[c])
-                if not ahead:
-                    finish(factor[:, columns(c - 2)], factor[:, columns(c - 2)])
-                    damp_plan(nc.gpsimd, step, columns(c - 2))
-                if c == 2:
-                    unfold(1, factor[:, columns(1)], [turns[1]])
-            for half in range(2 if ahead else 0):
-                features(step + 2, 1, columns(half), turns[half], raw(1, columns(half)))
-            if ahead:
-                finish(factor[:, columns(0, S)], factor[:, columns(0, S)])
-                weigh(step + 2, 1, whole, raw(1, whole))
-                damp_plan(nc.gpsimd, step, columns(0, S))
-            for half in range(2 if ahead else 0):
-                features(step + 2, 0, columns(half), turns[half], raw(0, columns(half)))
-            if ahead:
-                unfold(2, factor[:, columns(2)], sums[0:2])
-                unfold(3, factor[:, columns(3)], sums[2:4])
-                finish(factor[:, columns(1, S)], factor[:, columns(1, S)])
-            else:
-                unfold(2, late_roots[0], [feats[0]])
-                unfold(3, late_roots[1], sums[2:4])
-                for i in range(2):
-                    finish(factor[:, columns(2 + i)], late_roots[i])
-            if ahead:
-                damp_plan(nc.gpsimd, step, columns(1, S))
-            else:
-                for c in (2, 3):
-                    damp_plan(nc.gpsimd, step, columns(c))
-                    first_weave(c)
-                for c in (2, 3):
-                    turn_page(LAST, 1, c, sums[c], True)
-            scatter(step + 1, 0)
+        for s in range(LAST):
+            if s + 2 <= LAST:
+                scatter(s + 2, B)
+            for c in range(CHUNKS):
+                turn_page(s, A, c)
+                square(squares[c], sums[c][:])
+            for c in range(CHUNKS):
+                unfold(c, squares[c], [backs[c], spare[c]] if c < 2 else sums[2 * c - 4 : 2 * c - 2])
+            for c in range(CHUNKS):
+                factor(s, c)
+            for c in range(CHUNKS):
+                damp_plan(nc.gpsimd, s, c)
+            if 0 < s <= LAST - 2:
+                held = weighed[B][(s + 1) % 2]
+                for half in range(2):
+                    features(s + 2, A, half, backs[half], held[:, columns(half)])
+                weigh(s + 2, A, source=held[:])
+            if s + 2 <= LAST:
+                scatter(s + 2, A)
+            if s + 3 <= LAST:
+                for half in range(2):
+                    features(s + 3, B, half, spare[half], unweighed[(s + 1) % 2][:, columns(half)])
+                weigh(s + 3, B, source=unweighed[(s + 1) % 2][:])
+            if s + 3 <= LAST:
+                load_plan(s + 3)
+            if s == 3:
+                nc.sync.dma_start(w8_w[:], w8_words.rearrange("a p n t -> p a (n t)").bitcast(I32))
+                load_plane(w8_s, w8_scales.rearrange("a r n -> r a n"))
+            for c in range(CHUNKS):
+                if s + 1 < LAST or c >= 1:
+                    turn_page(s + 1, B, c)
+            if s == LAST - 2:
+                for tag in ("w1_raw1", "w1_rounded"):
+                    two = tile([P, 8 * BANK], BF16, f"grouped_on_{tag}", tag=tag)
+                    grouped[0].extend(two[:, columns(i, 4 * BANK)] for i in range(2))
+                for c in range(2):
+                    weave(nc.gpsimd.tensor_copy, 0, c, I32)
+            if s == LAST - 1:
+                for c in range(2, CHUNKS):
+                    weave(nc.scalar.copy, 0, c, F32)
 
         second_words = tile([P, T2], U32, "second_words")
-        first_words = {}
-        z_s = [tile([P, T2], U8, f"z_s{a}") for a in range(2)]
-        last = factors[(LAST - 1) % 2]
-        staging = [pair[:, columns(i)] for pair in gain_a + gain_b for i in range(2)]
-        free_banks = sums[0:2] + backs + feats + sums[2:4]
-        emptied = []
+        words = [{}, [second_words[:, columns(c)] for c in range(CHUNKS)]]
+        planes = [tile([P, T2], U8, f"z_s{a}") for a in range(2)]
+        staging = [gain[:, columns(i)] for gain in gains[A] + gains[B] for i in range(2)]
+        late = tile([P, T2], F32, "late", tag="rows0")
+        last = factors[LAST % 2]
+        results = [backs + spare, sums]
+        pieces = [columns(i, 256) for i in range(BANK // 256)]
+        whole = columns(0)
 
-        def words(a, cols):
-            if a == 1:
-                return second_words[:, cols].bitcast(FP8X4)
-            start = cols.start % BANK
-            return first_words[cols.start // BANK][:, start : start + cols.stop - cols.start].bitcast(FP8X4)
+        def within(c, cols):
+            return slice(c * BANK + cols.start, c * BANK + cols.stop)
 
-        def codes(a, cols):
-            c = cols.start // BANK
-            if a == 0 and c == 0:
-                every = tile([P, T2], U32, "first_words0")
-                first_words.update({i: every[:, columns(i)] for i in range(CHUNKS)})
-            nc.vector.quantize_mx(out=words(a, cols), scales=z_s[a][:, cols], in_=z_values(a, cols))
+        def factor_on_vector(cols):
+            nc.vector.tensor_tensor(late[:, cols], pages[A][1][:, cols], pages[B][1][:, cols], ADD)
+            square(roots[0][:, cols], late[:, cols])
+            root(roots[0][:, cols], roots[0][:, cols])
+            finish(last[0][:, cols], roots[0][:, cols])
 
-        def z_values(a, cols):
-            if a == 0:
-                return first_grouped[:, 4 * cols.start : 4 * cols.stop]
-            start = cols.start % BANK
-            return second_grouped[cols.start // BANK][:, 4 * start : 4 * (start + cols.stop - cols.start)]
+        def squares_on_tensor(c):
+            turn_page(LAST, A, c)
+            squared = late[:].rearrange("p (b c m) -> p c b m", b=BLOCKS, m=P)[:, c]
+            square(squared, by_blocks(sums[c][:]))
+            for b in range(BLOCKS):
+                nc.tensor.transpose(sums[c][:, columns(b, P)], squared[:, b], ident[:])
 
-        def last_weave(cols):
-            weave(nc.vector.tensor_copy, 1, cols, z_values(1, cols))
+        def factor_from_tensor(c):
+            target = roots[1] if c == 1 else squares[c]
+            root(target, sums[c][:])
+            finish(last[c][:], target)
 
-        def last_product(cols, engines, groups=None):
-            width = cols.stop - cols.start
-            share = BANK // width
-            groups = groups or range(BLOCKS // share)
-            for g in groups:
-                bank = free_banks[len(emptied) % 8]
-                for a in range(2):
-                    for i in range(share):
-                        n = share * g + i
-                        nc.tensor.matmul_mx(
-                            out=bank[:, columns(i, width)],
-                            lhsT=w8_w[:, a, columns(n, P)].bitcast(FP8X4),
-                            lhsT_scale=w8_s[:, a, columns(n, P)],
-                            rhs=words(a, cols),
-                            rhs_scale=z_s[a][:, cols],
-                            start=(a == 0 and i == 0),
-                            stop=(a == 1 and i == share - 1),
-                        )
-                result = staging[len(emptied)]
-                emptied.append(g)
-                engines[g](result, bank[:])
-                target = out[columns(g, share * P), cols].rearrange("(i p) m -> p i m", p=P)
-                nc.sync.dma_start(target, result.rearrange("p (i m) -> p i m", i=share))
+        def codes(a, c, cols):
+            nc.vector.quantize_mx(
+                out=words[a][c][:, cols].bitcast(FP8X4),
+                scales=planes[a][:, within(c, cols)],
+                in_=grouped[a][c][:, 4 * cols.start : 4 * cols.stop],
+            )
 
-        def values(cols):
-            if cols.start >= S:
-                return first_grouped[:, 4 * (cols.start - S) : 4 * (cols.stop - S)].bitcast(F32)[:, 0:BANK]
-            return shared[:, P + cols.start : P + cols.stop]
+        def products(a, c, cols):
+            for n in range(BLOCKS):
+                nc.tensor.matmul_mx(
+                    out=results[c % 2][n][:, cols],
+                    lhsT=w8_w[:, a, columns(n, P)].bitcast(FP8X4),
+                    lhsT_scale=w8_s[:, a, columns(n, P)],
+                    rhs=words[a][c][:, cols].bitcast(FP8X4),
+                    rhs_scale=planes[a][:, within(c, cols)],
+                    start=(a == 0),
+                    stop=(a == 1 and cols.stop == BANK),
+                )
 
-        def add_pages(cols):
-            nc.vector.tensor_tensor(values(cols), page(LAST, 0)[:, cols], page(LAST, 1)[:, cols], ADD)
+        def first_pass(c):
+            codes(0, c, whole)
+            products(0, c, whole)
 
-        def last_square(cols):
-            nc.scalar.activation(values(cols), values(cols), ACT.Square)
+        def second_pass(c, parts):
+            for cols in parts:
+                damp_plan(nc.vector, LAST, c, cols)
+                weave(nc.vector.tensor_copy, 1, c, F32, cols)
+                codes(1, c, cols)
+                products(1, c, cols)
 
-        def last_root(cols):
-            root(values(cols), values(cols))
+        def first_words(chunks, tag):
+            held = tile([P, len(chunks) * BANK], U32, f"first_words_on_{tag}", tag=tag)
+            words[0].update({c: held[:, columns(i)] for i, c in enumerate(chunks)})
 
-        def last_finish(cols):
-            finish(last[:, cols], values(cols))
+        def hand_out(c):
+            for n in range(BLOCKS):
+                place = BLOCKS * c + n
+                copy = nc.vector.tensor_copy if place in (0, 11, 13, 15) else nc.scalar.copy
+                copy(staging[place], results[c % 2][n][:])
+                nc.sync.dma_start(out[columns(n, P), columns(c)], staging[place])
 
-        on_vector, on_scalar = nc.vector.tensor_copy, nc.scalar.copy
-        for c in range(CHUNKS + 1):
-            if c >= 1:
-                damp_plan(nc.vector, LAST, columns(c - 1))
-                last_weave(columns(c - 1))
-                codes(1, columns(c - 1))
-            if c < 2:
-                add_pages(columns(c))
-                last_square(columns(c))
-                last_root(columns(c))
-                last_finish(columns(c))
-            elif c < CHUNKS:
-                turn_page(LAST, 0, c, sums[c], False)
-                squares[c] = values(columns(c))
-                square(c, sums[c])
-                turn_back(c, sums[c])
-                root(last[:, columns(c)], sums[c][:])
-                finish(last[:, columns(c)], last[:, columns(c)])
-            if c < CHUNKS:
-                codes(0, columns(c))
-        for c in range(CHUNKS):
-            last_product(columns(c), [on_vector if BLOCKS * c + n in (9, 11, 13, 15) else on_scalar for n in range(BLOCKS)])
+        halves = [columns(i, HALF) for i in range(2)]
+        for cols in pieces:
+            factor_on_vector(cols)
+        first_words((0, 2), "page_b1")
+        grouped[1].extend(
+            tile([P, 4 * BANK], BF16, f"grouped1{c}", tag=f"weighed{c // 2}{c % 2}")[:] for c in range(CHUNKS)
+        )
+        first_pass(0)
+        second_pass(0, pieces)
+        squares_on_tensor(1)
+        factor_from_tensor(1)
+        squares_on_tensor(2)
+        squares_on_tensor(3)
+        codes(0, 2, whole)
+        first_words((1,), "roots0")
+        codes(0, 1, whole)
+        factor_from_tensor(2)
+        hand_out(0)
+        factor_from_tensor(3)
+        products(0, 1, whole)
+        second_pass(1, halves)
+        hand_out(1)
+        products(0, 2, whole)
+        second_pass(2, halves)
+        first_words((3,), "roots1")
+        first_pass(3)
+        hand_out(2)
+        second_pass(3, halves)
+        hand_out(3)

@@ -84,9 +84,6 @@ def tile_list_trap_bench_release_kernel(
 
         def load_gain(side, t, cols=slice(0, S)):
             dealt = (wg1, wg2)[side].rearrange("(p t) j -> t p j", t=4)[t]
-            if t > 0:
-                nc.sync.dma_start(gains[side][t][:], dealt.unsqueeze(0).to_broadcast([4, 32, S]))
-                return
             for q in (0, 2, 1, 3):
                 nc.sync.dma_start(gains[side][t][32 * q : 32 * q + 32, cols], dealt[:, cols])
 

@@ -57,15 +57,12 @@ def tile_list_trap_bench_release_kernel(
         w1_w = tile([P, H], U32, "w1_w")
         w1_s = tile([P, H], U8, "w1_s")
         w4_raw_w = tile([P, 2 * H], U8, "w4_raw_w")
-        w4_raw_s = tile([P, H], U8, "w4_raw_s", tag="w4_rest_w")
-        w4_first_w = tile([P, 4 * P], U8, "w4_first_w")
+        w4_raw_s = tile([P, H], U8, "w4_raw_s")
+        w4_w = tile([P, 2 * H], U8, "w4_w")
         w4_first_s = tile([P, 2 * P], U8, "w4_first_s")
         w4_rest_s = tile([P, 6 * P], U8, "w4_rest_s")
-        w4_rest_w = []
         w8_w = tile([P, 2, N], I32, "w8_w")
-        w8_s = tile([P, 2, N], U8, "w8_s")
         gains = [[tile([P, S], F32, f"gain{side}{t}") for t in range(4)] for side in (A, B)]
-        ident = tile([P, P], F32, "ident")
         pages = [[], [tile([P, T2], F32, f"page_b{i}") for i in range(2)]]
         ahead_of_page = [tile([P, BANK], F32, f"ahead_of_page{i}", tag=f"page_a{i}") for i in range(2)]
         weighed = [[tile([P, S], F32, f"weighed{side}{i}") for i in range(2)] for side in (A, B)]
@@ -95,32 +92,31 @@ def tile_list_trap_bench_release_kernel(
         def load_plan(s):
             nc.sync.dma_start(rows[s % 3][:], plan.rearrange("(a p t) m -> a t p m", a=2, t=4)[ORDER[s]])
 
-        def round_w1(a):
+        def round_w1(a, part=slice(0, P)):
             nc.scalar.copy(
-                w1_rounded[:, columns(a, 4 * BANK)].rearrange("p (t m j) -> p m j t", m=P, j=4),
-                w1_raw[a][:].rearrange("p (j m t) -> p m j t", j=4, t=4),
+                w1_rounded[:, columns(a, 4 * BANK)].rearrange("p (t m j) -> p m j t", m=P, j=4)[:, part],
+                w1_raw[a][:].rearrange("p (j m t) -> p m j t", j=4, t=4)[:, part],
             )
 
-        def product(s, side, half, bank):
+        def product(s, side, cols, bank):
             a, t = ORDER[s]
             if side == A:
                 weights, plane = w1_w[:, columns(4 * a + t, P)].bitcast(FP8X4), w1_s[:, columns(4 * a + t, P)]
-            elif t == 0:
-                weights, plane = w4_first_w[:, columns(a, 2 * P)].bitcast(FP4X4), w4_first_s[:, columns(a, P)]
             else:
-                weights, plane = w4_rest_w[0][:, columns(2 * t - 2 + a, 2 * P)].bitcast(FP4X4), w4_rest_s[:, columns(2 * t - 2 + a, P)]
+                weights = w4_w[:, columns(2 * t + a, 2 * P)].bitcast(FP4X4)
+                plane = w4_first_s[:, columns(a, P)] if t == 0 else w4_rest_s[:, columns(2 * t - 2 + a, P)]
             nc.tensor.matmul_mx(
-                out=bank[:],
+                out=bank[:, 0 : cols.stop - cols.start],
                 lhsT=weights,
                 lhsT_scale=plane,
-                rhs=v_w[:, columns(half)].bitcast(FP8X4),
-                rhs_scale=v_s[:, columns(half)],
+                rhs=v_w[:, cols].bitcast(FP8X4),
+                rhs_scale=v_s[:, cols],
                 start=True,
                 stop=True,
             )
 
         def features(s, side, half, bank, target=None):
-            product(s, side, half, bank)
+            product(s, side, columns(half), bank)
             target = weighed[side][s % 2][:, columns(half)] if target is None else target
             nc.scalar.activation(target, bank[:], ACT.Copy, scale=(-1.0, 1.0)[side])
 
@@ -182,34 +178,37 @@ def tile_list_trap_bench_release_kernel(
         nc.gpsimd.memset(tab_s[:].bitcast(I32), 0)
         nc.vector.memset(w4_raw_s[:].bitcast(I32), 0)
         nc.sync.dma_start(list_tab[:], offs)
-        nc.sync.dma_start(lists[B][:], offs3)
+        nc.sync.dma_start(w4_raw_w[:].bitcast(I32), w4_words[0].bitcast(I32))
         load_plane(tab_s, tab_scales[0])
         nc.sync.dma_start(tab_w[:], tab_words[0].rearrange("p n t -> p (n t)").bitcast(I32))
-        nc.sync.dma_start(w4_raw_w[:].bitcast(I32), w4_words[0].bitcast(I32))
         load_plane(w4_raw_s, w4_scales[0])
+        nc.sync.dma_start(lists[B][:], offs3)
         load_gain(B, 0, first)
-        load_gain(B, 0, second)
         load_w1(0)
+        load_gain(B, 0, second)
         load_w1(1)
         nc.sync.dma_start(lists[A][:], offs2)
         load_gain(A, 0)
         load_gain(B, 1)
-        nc.vector.memset(pages[B][0][:].bitcast(I32), 0)
+        for i in range(2):
+            nc.vector.memset(pages[B][i][:].bitcast(I32), 0)
         raw_words = w4_raw_w[:].rearrange("p (a m t e) -> p t a m e", a=2, t=4, e=2)
         raw_scales = w4_raw_s[:].rearrange("p (a m t) -> p t a m", a=2, t=4)
-        nc.gpsimd.tensor_copy(w4_first_w[:].rearrange("p (a m e) -> p a m e", a=2, e=2), raw_words[:, 0])
+        nc.gpsimd.tensor_copy(w4_w[:].rearrange("p (t a m e) -> p t a m e", a=2, m=P, e=2), raw_words)
         nc.gpsimd.tensor_copy(w4_first_s[:].rearrange("p (a m) -> p a m", a=2), raw_scales[:, 0])
-        nc.gpsimd.memset(pages[B][1][:].bitcast(I32), 0)
-        make_identity(nc, ident[:])
-        nc.gpsimd.memset(w8_s[:].rearrange("p a n -> p (a n)").bitcast(I32), 0)
         nc.vector.tensor_copy(v_s[:], tab_s[:].indirect(list_tab[:]))
-        for half in range(2):
-            entries = list_tab[:, columns(half, BANK // 16)]
-            nc.vector.tensor_copy(v_w[:, columns(half)], tab_w[:].bitcast(U32).indirect(entries))
+        quarters = [columns(i, HALF) for i in range(2)]
+        for cols in quarters + [second]:
+            entries = list_tab[:, cols.start // 16 : cols.stop // 16]
+            nc.vector.tensor_copy(v_w[:, cols], tab_w[:].bitcast(U32).indirect(entries))
 
-        product(0, B, 0, spare[0])
-        nc.vector.tensor_tensor(weighed[B][0][:, first], spare[0][:], gains[B][0][:, first], MULT)
-        scatter(0, B, first)
+        product(0, B, quarters[0], spare[0])
+        nc.vector.tensor_tensor(weighed[B][0][:, quarters[0]], spare[0][:, 0:HALF], gains[B][0][:, quarters[0]], MULT)
+        scatter(0, B, quarters[0])
+        product(0, B, quarters[1], sums[0])
+        nc.scalar.copy(weighed[B][0][:, quarters[1]], sums[0][:, 0:HALF])
+        weigh(0, B, quarters[1])
+        scatter(0, B, quarters[1])
         features(1, B, 0, spare[1])
         weigh(1, B, first)
         scatter(1, B, first)
@@ -217,15 +216,25 @@ def tile_list_trap_bench_release_kernel(
         weigh(0, B, second, ahead_of_page[0][:])
         scatter(0, B, second)
         nc.gpsimd.tensor_copy(w4_rest_s[:].rearrange("p (t a m) -> p t a m", a=2, m=P), raw_scales[:, 1:4])
-        w4_rest_w.append(tile([P, 12 * P], U8, "w4_rest_w"))
-        nc.gpsimd.tensor_copy(w4_rest_w[0][:].rearrange("p (t a m e) -> p t a m e", a=2, m=P, e=2), raw_words[:, 1:4])
+        ident = tile([P, P], F32, "ident", tag="w4_raw_w")
+        make_identity(nc, ident[:])
+        w8_s = tile([P, 2, N], U8, "w8_s", tag="w4_raw_s")
+        nc.gpsimd.memset(w8_s[:].rearrange("p a n -> p (a n)").bitcast(I32), 0)
         pages[A].append(tile([P, T2], F32, "page_a0"))
         nc.gpsimd.memset(pages[A][0][:].bitcast(I32), 0)
         round_w1(0)
-        round_w1(1)
+        round_w1(1, slice(0, 3 * P // 4))
+        spent = w1_raw[1][:].rearrange("p (j c) -> p j c", j=4)[:, 0:2, 0:HALF]
+        product(1, B, second, backs[1])
+        nc.scalar.copy(spent, backs[1][:].rearrange("p (j c) -> p j c", j=2))
+        round_w1(1, slice(3 * P // 4, P))
         nc.vector.quantize_mx(out=w1_w[:].bitcast(FP8X4), scales=w1_s[:], in_=w1_rounded[:])
-        features(1, B, 1, backs[1], w1_raw[1][:, second])
-        weigh(1, B, second, w1_raw[1][:, second])
+        nc.gpsimd.tensor_tensor(
+            weighed[B][1][:, second].rearrange("p (j c) -> p j c", j=2),
+            spent,
+            gains[B][0][:, second].rearrange("p (j c) -> p j c", j=2),
+            MULT,
+        )
         scatter(1, B, second)
         features(0, A, 0, sums[0])
         weigh(0, A, first)

@@ -167,11 +167,11 @@ def tile_list_trap_bench_release_kernel(
             target = pairs[a][c][:].rearrange("p (u m e) -> p u e m", u=2, e=2)[:, t // 2, t % 2]
             engine.tensor_tensor(target[:, cols], factors[s % 2][c][:, cols], rows[s % 3][:, columns(c)][:, cols], MULT)
 
-        def weave(copy, a, c, word, cols=slice(0, BANK)):
+        def weave(copy, a, c, cols=slice(0, BANK)):
             fours = slice(cols.start // 4, cols.stop // 4)
             copy(
-                grouped[a][c].bitcast(word).rearrange("p (g i u) -> p g u i", u=2, i=4)[:, fours],
-                pairs[a][c][:].bitcast(word).rearrange("p (u g i) -> p g u i", u=2, i=4)[:, fours],
+                grouped[a][c].bitcast(F32).rearrange("p (g i u) -> p g u i", u=2, i=4)[:, fours],
+                pairs[a][c][:].bitcast(F32).rearrange("p (u g i) -> p g u i", u=2, i=4)[:, fours],
             )
 
         first, second = columns(0), columns(1)
@@ -271,13 +271,29 @@ def tile_list_trap_bench_release_kernel(
         for s in range(LAST):
             if s + 2 <= LAST:
                 scatter(s + 2, B)
-            for c in range(CHUNKS):
-                turn_page(s, A, c)
-                square(squares[c], sums[c][:])
-            for c in range(CHUNKS):
-                unfold(c, squares[c], [backs[c], spare[c]] if c < 2 else sums[2 * c - 4 : 2 * c - 2])
-            for c in range(CHUNKS):
-                factor(s, c)
+            if s < LAST - 1:
+                for c in range(CHUNKS):
+                    turn_page(s, A, c)
+                    square(squares[c], sums[c][:])
+                for c in range(CHUNKS):
+                    unfold(c, squares[c], [backs[c], spare[c]] if c < 2 else sums[2 * c - 4 : 2 * c - 2])
+                    if c == 0:
+                        factor(s, c)
+                for c in range(1, CHUNKS):
+                    factor(s, c)
+            else:
+                for c in range(2):
+                    turn_page(s, A, c)
+                    square(squares[c], sums[c][:])
+                for c in range(2):
+                    unfold(c, squares[c], [sums[2 + c]])
+                for c in range(2):
+                    factor(s, c)
+                for c in range(2, CHUNKS):
+                    nc.gpsimd.tensor_tensor(squares[c], pages[A][0][:, columns(c)], pages[B][0][:, columns(c)], ADD)
+                    square(squares[c], squares[c])
+                    root(squares[c], squares[c])
+                    finish(factors[s % 2][c][:], squares[c])
             for c in range(CHUNKS):
                 damp_plan(nc.gpsimd, s, c)
             if 0 < s <= LAST - 2:
@@ -297,17 +313,17 @@ def tile_list_trap_bench_release_kernel(
                 nc.sync.dma_start(w8_w[:], w8_words.rearrange("a p n t -> p a (n t)").bitcast(I32))
                 load_plane(w8_s, w8_scales.rearrange("a r n -> r a n"))
             for c in range(CHUNKS):
-                if s + 1 < LAST or c >= 1:
+                if s + 1 < LAST - 1 or (c < 2) == (s + 1 < LAST):
                     turn_page(s + 1, B, c)
             if s == LAST - 2:
                 for tag in ("w1_raw1", "w1_rounded"):
                     two = tile([P, 8 * BANK], BF16, f"grouped_on_{tag}", tag=tag)
                     grouped[0].extend(two[:, columns(i, 4 * BANK)] for i in range(2))
                 for c in range(2):
-                    weave(nc.gpsimd.tensor_copy, 0, c, I32)
+                    weave(nc.scalar.copy, 0, c)
             if s == LAST - 1:
                 for c in range(2, CHUNKS):
-                    weave(nc.scalar.copy, 0, c, F32)
+                    weave(nc.scalar.copy, 0, c)
 
         second_words = tile([P, T2], U32, "second_words")
         words = [{}, [second_words[:, columns(c)] for c in range(CHUNKS)]]
@@ -322,21 +338,21 @@ def tile_list_trap_bench_release_kernel(
         def within(c, cols):
             return slice(c * BANK + cols.start, c * BANK + cols.stop)
 
-        def factor_on_vector(cols):
-            nc.vector.tensor_tensor(late[:, cols], pages[A][1][:, cols], pages[B][1][:, cols], ADD)
-            square(roots[0][:, cols], late[:, cols])
-            root(roots[0][:, cols], roots[0][:, cols])
-            finish(last[0][:, cols], roots[0][:, cols])
+        def factor_on_vector(c, cols, gap):
+            nc.vector.tensor_tensor(gap, pages[A][1][:, within(c, cols)], pages[B][1][:, within(c, cols)], ADD)
+            square(roots[c][:, cols], gap)
+            root(roots[c][:, cols], roots[c][:, cols])
+            finish(last[c][:, cols], roots[c][:, cols])
 
         def squares_on_tensor(c):
             turn_page(LAST, A, c)
-            squared = late[:].rearrange("p (b c m) -> p c b m", b=BLOCKS, m=P)[:, c]
+            squared = by_blocks(late[:, columns(c - 2)])
             square(squared, by_blocks(sums[c][:]))
             for b in range(BLOCKS):
                 nc.tensor.transpose(sums[c][:, columns(b, P)], squared[:, b], ident[:])
 
         def factor_from_tensor(c):
-            target = roots[1] if c == 1 else squares[c]
+            target = squares[c]
             root(target, sums[c][:])
             finish(last[c][:], target)
 
@@ -366,7 +382,7 @@ def tile_list_trap_bench_release_kernel(
         def second_pass(c, parts):
             for cols in parts:
                 damp_plan(nc.vector, LAST, c, cols)
-                weave(nc.vector.tensor_copy, 1, c, F32, cols)
+                weave(nc.vector.tensor_copy, 1, c, cols)
                 codes(1, c, cols)
                 products(1, c, cols)
 
@@ -377,24 +393,26 @@ def tile_list_trap_bench_release_kernel(
         def hand_out(c):
             for n in range(BLOCKS):
                 place = BLOCKS * c + n
-                copy = nc.vector.tensor_copy if place in (0, 11, 13, 15) else nc.scalar.copy
+                copy = nc.vector.tensor_copy if place in (1, 11, 13, 15) else nc.scalar.copy
                 copy(staging[place], results[c % 2][n][:])
                 nc.sync.dma_start(out[columns(n, P), columns(c)], staging[place])
 
         halves = [columns(i, HALF) for i in range(2)]
-        for cols in pieces:
-            factor_on_vector(cols)
-        first_words((0, 2), "page_b1")
+        first_gap = tile([P, HALF], F32, "first_gap", tag=f"factors0{CHUNKS - 1}")
+        factor_on_vector(0, halves[0], first_gap[:])
+        factor_on_vector(0, halves[1], late[:, halves[1]])
         grouped[1].extend(
             tile([P, 4 * BANK], BF16, f"grouped1{c}", tag=f"weighed{c // 2}{c % 2}")[:] for c in range(CHUNKS)
         )
+        first_words((0,), "factors03")
         first_pass(0)
-        second_pass(0, pieces)
-        squares_on_tensor(1)
-        factor_from_tensor(1)
+        factor_on_vector(1, halves[0], late[:, columns(2, HALF)])
+        factor_on_vector(1, halves[1], late[:, columns(3, HALF)])
         squares_on_tensor(2)
         squares_on_tensor(3)
+        first_words((2,), "page_b1")
         codes(0, 2, whole)
+        second_pass(0, halves)
         first_words((1,), "roots0")
         codes(0, 1, whole)
         factor_from_tensor(2)
@@ -402,8 +420,8 @@ def tile_list_trap_bench_release_kernel(
         factor_from_tensor(3)
         products(0, 1, whole)
         second_pass(1, halves)
-        hand_out(1)
         products(0, 2, whole)
+        hand_out(1)
         second_pass(2, halves)
         first_words((3,), "roots1")
         first_pass(3)

@@ -175,7 +175,7 @@ def tile_list_trap_bench_release_kernel(
             )
 
         first, second = columns(0), columns(1)
-        nc.gpsimd.memset(tab_s[:].bitcast(I32), 0)
+        nc.vector.memset(tab_s[:].bitcast(I32), 0)
         nc.vector.memset(w4_raw_s[:].bitcast(I32), 0)
         nc.sync.dma_start(list_tab[:], offs)
         nc.sync.dma_start(w4_raw_w[:].bitcast(I32), w4_words[0].bitcast(I32))
@@ -205,20 +205,18 @@ def tile_list_trap_bench_release_kernel(
         product(0, B, quarters[0], spare[0])
         nc.vector.tensor_tensor(weighed[B][0][:, quarters[0]], spare[0][:, 0:HALF], gains[B][0][:, quarters[0]], MULT)
         scatter(0, B, quarters[0])
-        product(0, B, quarters[1], sums[0])
-        nc.scalar.copy(weighed[B][0][:, quarters[1]], sums[0][:, 0:HALF])
-        weigh(0, B, quarters[1])
-        scatter(0, B, quarters[1])
-        features(1, B, 0, spare[1])
-        weigh(1, B, first)
-        scatter(1, B, first)
+        for i, (s, cols) in enumerate(((1, quarters[0]), (0, quarters[1]), (1, quarters[1]))):
+            product(s, B, cols, sums[i])
+            nc.scalar.copy(weighed[B][s][:, cols], sums[i][:, 0:HALF])
+            weigh(s, B, cols)
+            scatter(s, B, cols)
         features(0, B, 1, backs[0], ahead_of_page[0][:])
         weigh(0, B, second, ahead_of_page[0][:])
         scatter(0, B, second)
         nc.gpsimd.tensor_copy(w4_rest_s[:].rearrange("p (t a m) -> p t a m", a=2, m=P), raw_scales[:, 1:4])
-        ident = tile([P, P], F32, "ident", tag="w4_raw_w")
+        ident = tile([P, P], F32, "ident", tag="w4_raw_s")
         make_identity(nc, ident[:])
-        w8_s = tile([P, 2, N], U8, "w8_s", tag="w4_raw_s")
+        w8_s = tile([P, 2, N], U8, "w8_s", tag="w4_raw_w")
         nc.gpsimd.memset(w8_s[:].rearrange("p a n -> p (a n)").bitcast(I32), 0)
         pages[A].append(tile([P, T2], F32, "page_a0"))
         nc.gpsimd.memset(pages[A][0][:].bitcast(I32), 0)

@@ -294,7 +294,7 @@ def tile_list_trap_bench_release_kernel(
                     finish(factors[s % 2][c][:], squares[c])
             for c in range(CHUNKS):
                 damp_plan(nc.gpsimd, s, c)
-            if 0 < s <= LAST - 2:
+            if 1 < s <= LAST - 2:
                 held = weighed[B][(s + 1) % 2]
                 for half in range(2):
                     features(s + 2, A, half, backs[half], held[:, columns(half)])
@@ -305,6 +305,10 @@ def tile_list_trap_bench_release_kernel(
                 for half in range(2):
                     features(s + 3, B, half, spare[half], unweighed[(s + 1) % 2][:, columns(half)])
                 weigh(s + 3, B, source=unweighed[(s + 1) % 2][:])
+            if s == 0:
+                for half in range(2):
+                    features(3, A, half, backs[half], third[:, columns(half)])
+                weigh(3, A, source=third[:])
             if s + 3 <= LAST:
                 load_plan(s + 3)
             if s == 3:

@@ -386,7 +386,7 @@ def tile_list_trap_bench_release_kernel(
                 damp_plan(nc.vector, LAST, c, cols)
                 weave(nc.vector.tensor_copy, 1, c, cols)
                 codes(1, c, cols)
-                products(1, c, cols)
+            products(1, c, whole)
 
         def first_words(chunks, tag):
             held = tile([P, len(chunks) * BANK], U32, f"first_words_on_{tag}", tag=tag)

@@ -92,10 +92,10 @@ def tile_list_trap_bench_release_kernel(
         def load_plan(s):
             nc.sync.dma_start(rows[s % 3][:], plan.rearrange("(a p t) m -> a t p m", a=2, t=4)[ORDER[s]])
 
-        def round_w1(a, part=slice(0, P)):
+        def round_w1(a):
             nc.scalar.copy(
-                w1_rounded[:, columns(a, 4 * BANK)].rearrange("p (t m j) -> p m j t", m=P, j=4)[:, part],
-                w1_raw[a][:].rearrange("p (j m t) -> p m j t", j=4, t=4)[:, part],
+                w1_rounded[:, columns(a, 4 * BANK)].rearrange("p (t m j) -> p m j t", m=P, j=4),
+                w1_raw[a][:].rearrange("p (j m t) -> p m j t", j=4, t=4),
             )
 
         def product(s, side, cols, bank):
@@ -221,19 +221,11 @@ def tile_list_trap_bench_release_kernel(
         pages[A].append(tile([P, T2], F32, "page_a0"))
         nc.gpsimd.memset(pages[A][0][:].bitcast(I32), 0)
         round_w1(0)
-        round_w1(1, slice(0, 3 * P // 4))
-        spent = w1_raw[1][:].rearrange("p (j c) -> p j c", j=4)[:, 0:2, 0:HALF]
+        round_w1(1)
         product(1, B, second, backs[1])
-        nc.scalar.copy(spent, backs[1][:].rearrange("p (j c) -> p j c", j=2))
-        round_w1(1, slice(3 * P // 4, P))
+        nc.vector.tensor_tensor(w1_raw[1][:, second], backs[1][:], gains[B][0][:, second], MULT)
         nc.vector.quantize_mx(out=w1_w[:].bitcast(FP8X4), scales=w1_s[:], in_=w1_rounded[:])
-        nc.gpsimd.tensor_tensor(
-            weighed[B][1][:, second].rearrange("p (j c) -> p j c", j=2),
-            spent,
-            gains[B][0][:, second].rearrange("p (j c) -> p j c", j=2),
-            MULT,
-        )
-        scatter(1, B, second)
+        nc.vector.tensor_copy(pages[B][1][:].indirect(lists[B][:, BANK // 16 : S // 16]), w1_raw[1][:, second])
         features(0, A, 0, sums[0])
         weigh(0, A, first)
         scatter(0, A, first)

from contextlib import ExitStack

import concourse.mybir as mybir
from concourse.masks import make_identity

K, H, N, T, S, T2 = 512, 1024, 512, 2048, 1024, 2048
FLOPS = 2 * (2 * K * H * S + H * N * T2)

F32 = mybir.dt.float32
BF16 = mybir.dt.bfloat16
I32 = mybir.dt.int32
U32 = mybir.dt.uint32
U16 = mybir.dt.uint16
U8 = mybir.dt.uint8
FP8X4 = mybir.dt.float8_e4m3fn_x4
FP4X4 = mybir.dt.float4_e2m1fn_x4
ACT = mybir.ActivationFunctionType
MULT = mybir.AluOpType.mult
ADD = mybir.AluOpType.add

P = 128
BANK = 512
HALF = BANK // 2
CHUNKS = T2 // BANK
BLOCKS = BANK // P
SLICES = H // P
LAST = SLICES - 1
ORDER = ((0, 0), (1, 0), (0, 1), (1, 1), (0, 2), (0, 3), (1, 2), (1, 3))
ROOT = 75.0 / 64.0
A, B = 0, 1


def tile_list_trap_bench_release_kernel(
    tc, tab_words, tab_scales, offs, offs2, offs3, w1, w4_words, w4_scales, wg1, wg2, plan, w8_words, w8_scales, out
):
    nc = tc.nc
    with ExitStack() as ctx:
        keep = ctx.enter_context(tc.tile_pool(name="keep", bufs=1))
        psum = ctx.enter_context(tc.psum_pool(name="psum", bufs=1))
        banks = [psum.tile([P, BANK], F32, name=f"bank{b}") for b in range(8)]
        sums, backs, spare = banks[0:4], banks[4:6], banks[6:8]

        def columns(i, width=BANK):
            return slice(i * width, (i + 1) * width)

        def tile(shape, dtype, name, tag=None):
            return keep.tile(shape, dtype, name=name, tag=tag or name, align_bytes=64)

        list_tab = tile([P, S // 16], U16, "list_tab")
        lists = [tile([P, S // 16], U16, "list_a"), tile([P, S // 16], U16, "list_b")]
        tab_w = tile([P, T], I32, "tab_w", tag="rows0")
        tab_s = tile([P, T], U8, "tab_s")
        v_w = tile([P, S], U32, "v_w")
        v_s = tile([P, S], U8, "v_s")
        w1_raw = [tile([P, T2], F32, "w1_raw0", tag="rows1"), tile([P, T2], F32, "w1_raw1")]
        w1_rounded = tile([P, 4 * H], BF16, "w1_rounded")
        w1_w = tile([P, H], U32, "w1_w")
        w1_s = tile([P, H], U8, "w1_s")
        w4_raw_w = tile([P, 2 * H], U8, "w4_raw_w")
        w4_raw_s = tile([P, H], U8, "w4_raw_s")
        w4_w = tile([P, 2 * H], U8, "w4_w")
        w4_first_s = tile([P, 2 * P], U8, "w4_first_s")
        w4_rest_s = tile([P, 6 * P], U8, "w4_rest_s")
        w8_w = tile([P, 2, N], I32, "w8_w")
        gains = [[tile([P, S], F32, f"gain{side}{t}") for t in range(4)] for side in (A, B)]
        pages = [[], [tile([P, T2], F32, f"page_b{i}") for i in range(2)]]
        ahead_of_page = [tile([P, BANK], F32, f"ahead_of_page{i}", tag=f"page_a{i}") for i in range(2)]
        weighed = [[tile([P, S], F32, f"weighed{side}{i}") for i in range(2)] for side in (A, B)]
        all_squares = tile([P, T2], F32, "all_squares")
        squares = [all_squares[:, columns(c)] for c in range(CHUNKS)]
        roots = [tile([P, BANK], F32, f"roots{c}")[:] for c in range(CHUNKS - 1)]
        roots.append(all_squares[:].rearrange("p (c m) -> p c m", c=CHUNKS)[:, :, 0:P])
        factors = [[tile([P, BANK], F32, f"factors{i}{c}") for c in range(CHUNKS)] for i in range(2)]
        pairs = [[tile([P, 4 * BANK], BF16, f"pairs{a}{c}") for c in range(CHUNKS)] for a in range(2)]
        grouped = [[], []]
        rows = []

        def load_plane(plane, src_rows):
            for q in range(4):
                nc.sync.dma_start(plane[32 * q : 32 * q + 4].bitcast(I32), src_rows[4 * q : 4 * q + 4].bitcast(I32))

        def load_gain(side, t, cols=slice(0, S)):
            dealt = (wg1, wg2)[side].rearrange("(p t) j -> t p j", t=4)[t]
            for q in (0, 2, 1, 3):
                nc.sync.dma_start(gains[side][t][32 * q : 32 * q + 32, cols], dealt[:, cols])

        def load_w1(a):
            nc.sync.dma_start(
                w1_raw[a][:].rearrange("p (j c) -> p j c", j=4), w1[:, columns(a)].rearrange("(p j) c -> p j c", j=4)
            )

        def load_plan(s):
            nc.sync.dma_start(rows[s % 3][:], plan.rearrange("(a p t) m -> a t p m", a=2, t=4)[ORDER[s]])

        def round_w1(a):
            nc.scalar.copy(
                w1_rounded[:, columns(a, 4 * BANK)].rearrange("p (t m j) -> p m j t", m=P, j=4),
                w1_raw[a][:].rearrange("p (j m t) -> p m j t", j=4, t=4),
            )

        def product(s, side, cols, bank):
            a, t = ORDER[s]
            if side == A:
                weights, plane = w1_w[:, columns(4 * a + t, P)].bitcast(FP8X4), w1_s[:, columns(4 * a + t, P)]
            else:
                weights = w4_w[:, columns(2 * t + a, 2 * P)].bitcast(FP4X4)
                plane = w4_first_s[:, columns(a, P)] if t == 0 else w4_rest_s[:, columns(2 * t - 2 + a, P)]
            nc.tensor.matmul_mx(
                out=bank[:, 0 : cols.stop - cols.start],
                lhsT=weights,
                lhsT_scale=plane,
                rhs=v_w[:, cols].bitcast(FP8X4),
                rhs_scale=v_s[:, cols],
                start=True,
                stop=True,
            )

        def features(s, side, half, bank, target=None):
            product(s, side, columns(half), bank)
            target = weighed[side][s % 2][:, columns(half)] if target is None else target
            nc.scalar.activation(target, bank[:], ACT.Copy, scale=(-1.0, 1.0)[side])

        def weigh(s, side, cols=slice(0, S), source=None):
            target = weighed[side][s % 2][:, cols]
            nc.gpsimd.tensor_tensor(target, target if source is None else source, gains[side][ORDER[s][1]][:, cols], MULT)

        def scatter(s, side, cols=slice(0, S)):
            entries = lists[side][:, cols.start // 16 : cols.stop // 16]
            nc.vector.tensor_copy(pages[side][s % 2][:].indirect(entries), weighed[side][s % 2][:, cols])

        def turn_page(s, side, c):
            for b in range(BLOCKS):
                nc.tensor.matmul(
                    sums[c][:, columns(b, P)],
                    lhsT=pages[side][s % 2][:, columns(BLOCKS * c + b, P)],
                    rhs=ident[:],
                    is_transpose=True,
                    start=(side == B and b == 0),
                    stop=(side == A and b == BLOCKS - 1),
                )

        def square(target, source):
            nc.scalar.activation(target, source, ACT.Square)

        def root(target, source):
            nc.scalar.activation(target, source, ACT.Abs_reciprocal_sqrt, bias=ROOT * ROOT, scale=ROOT * ROOT)

        def finish(target, source):
            nc.scalar.activation(target, source, ACT.Square, scale=ROOT)

        def by_blocks(values):
            return values if len(values.shape) == 3 else values.rearrange("p (b m) -> p b m", m=P)

        def unfold(c, squared, targets):
            share = BLOCKS // len(targets)
            for b in range(BLOCKS):
                nc.tensor.transpose(targets[b // share][:, columns(b, P)], squared[:, columns(b, P)], ident[:])
            for i, bank in enumerate(targets):
                blocks = columns(i, share)
                root(by_blocks(roots[c])[:, blocks], by_blocks(bank[:])[:, blocks])

        def factor(s, c):
            finish(by_blocks(factors[s % 2][c][:]), by_blocks(roots[c]))

        def damp_plan(engine, s, c, cols=slice(0, BANK)):
            a, t = ORDER[s]
            target = pairs[a][c][:].rearrange("p (u m e) -> p u e m", u=2, e=2)[:, t // 2, t % 2]
            engine.tensor_tensor(target[:, cols], factors[s % 2][c][:, cols], rows[s % 3][:, columns(c)][:, cols], MULT)

        def weave(copy, a, c, cols=slice(0, BANK)):
            fours = slice(cols.start // 4, cols.stop // 4)
            copy(
                grouped[a][c].bitcast(F32).rearrange("p (g i u) -> p g u i", u=2, i=4)[:, fours],
                pairs[a][c][:].bitcast(F32).rearrange("p (u g i) -> p g u i", u=2, i=4)[:, fours],
            )

        first, second = columns(0), columns(1)
        nc.vector.memset(tab_s[:].bitcast(I32), 0)
        nc.vector.memset(w4_raw_s[:].bitcast(I32), 0)
        nc.sync.dma_start(list_tab[:], offs)
        nc.sync.dma_start(w4_raw_w[:].bitcast(I32), w4_words[0].bitcast(I32))
        load_plane(tab_s, tab_scales[0])
        nc.sync.dma_start(tab_w[:], tab_words[0].rearrange("p n t -> p (n t)").bitcast(I32))
        load_plane(w4_raw_s, w4_scales[0])
        nc.sync.dma_start(lists[B][:], offs3)
        load_gain(B, 0, first)
        load_w1(0)
        load_gain(B, 0, second)
        load_w1(1)
        nc.sync.dma_start(lists[A][:], offs2)
        load_gain(A, 0)
        load_gain(B, 1)
        for i in range(2):
            nc.vector.memset(pages[B][i][:].bitcast(I32), 0)
        raw_words = w4_raw_w[:].rearrange("p (a m t e) -> p t a m e", a=2, t=4, e=2)
        raw_scales = w4_raw_s[:].rearrange("p (a m t) -> p t a m", a=2, t=4)
        nc.gpsimd.tensor_copy(w4_w[:].rearrange("p (t a m e) -> p t a m e", a=2, m=P, e=2), raw_words)
        nc.gpsimd.tensor_copy(w4_first_s[:].rearrange("p (a m) -> p a m", a=2), raw_scales[:, 0])
        nc.vector.tensor_copy(v_s[:], tab_s[:].indirect(list_tab[:]))
        quarters = [columns(i, HALF) for i in range(2)]
        for cols in quarters + [second]:
            entries = list_tab[:, cols.start // 16 : cols.stop // 16]
            nc.vector.tensor_copy(v_w[:, cols], tab_w[:].bitcast(U32).indirect(entries))

        product(0, B, quarters[0], spare[0])
        nc.vector.tensor_tensor(weighed[B][0][:, quarters[0]], spare[0][:, 0:HALF], gains[B][0][:, quarters[0]], MULT)
        scatter(0, B, quarters[0])
        for i, (s, cols) in enumerate(((1, quarters[0]), (0, quarters[1]), (1, quarters[1]))):
            product(s, B, cols, sums[i])
            nc.scalar.copy(weighed[B][s][:, cols], sums[i][:, 0:HALF])
            weigh(s, B, cols)
            scatter(s, B, cols)
        features(0, B, 1, backs[0], ahead_of_page[0][:])
        weigh(0, B, second, ahead_of_page[0][:])
        scatter(0, B, second)
        nc.gpsimd.tensor_copy(w4_rest_s[:].rearrange("p (t a m) -> p t a m", a=2, m=P), raw_scales[:, 1:4])
        ident = tile([P, P], F32, "ident", tag="w4_raw_s")
        make_identity(nc, ident[:])
        w8_s = tile([P, 2, N], U8, "w8_s", tag="w4_raw_w")
        nc.gpsimd.memset(w8_s[:].rearrange("p a n -> p (a n)").bitcast(I32), 0)
        pages[A].append(tile([P, T2], F32, "page_a0"))
        nc.gpsimd.memset(pages[A][0][:].bitcast(I32), 0)
        round_w1(0)
        round_w1(1)
        product(1, B, second, backs[1])
        nc.vector.tensor_tensor(w1_raw[1][:, second], backs[1][:], gains[B][0][:, second], MULT)
        nc.vector.quantize_mx(out=w1_w[:].bitcast(FP8X4), scales=w1_s[:], in_=w1_rounded[:])
        nc.vector.tensor_copy(pages[B][1][:].indirect(lists[B][:, BANK // 16 : S // 16]), w1_raw[1][:, second])
        features(0, A, 0, sums[0])
        weigh(0, A, first)
        scatter(0, A, first)
        features(0, A, 1, sums[1], ahead_of_page[1][:])
        weigh(0, A, second, ahead_of_page[1][:])
        scatter(0, A, second)
        pages[A].append(tile([P, T2], F32, "page_a1"))
        nc.gpsimd.memset(pages[A][1][:].bitcast(I32), 0)
        for half in range(2):
            features(1, A, half, sums[2 + half])
        weigh(1, A)
        scatter(1, A)
        for half in range(2):
            features(2, B, half, sums[half])
        weigh(2, B)
        unweighed = [tile([P, S], F32, f"unweighed{i}") for i in range(2)]
        third = unweighed[0]
        for half in range(2):
            features(2, A, half, sums[2 + half], third[:, columns(half)])
        rows.extend(tile([P, T2], F32, f"rows{i}") for i in range(3))
        load_gain(A, 1)
        weigh(2, A, source=third[:])
        load_plan(0)
        load_plan(1)
        load_gain(B, 2)
        load_plan(2)
        load_gain(A, 2)
        load_gain(B, 3)
        load_gain(A, 3)
        for c in range(CHUNKS):
            turn_page(0, B, c)

        for s in range(LAST):
            if s + 2 <= LAST:
                scatter(s + 2, B)
            if s < LAST - 1:
                for c in range(CHUNKS):
                    turn_page(s, A, c)
                    square(squares[c], sums[c][:])
                for c in range(CHUNKS):
                    unfold(c, squares[c], [backs[c], spare[c]] if c < 2 else sums[2 * c - 4 : 2 * c - 2])
                    if c == 0:
                        factor(s, c)
                for c in range(1, CHUNKS):
                    factor(s, c)
            else:
                for c in range(2):
                    turn_page(s, A, c)
                    square(squares[c], sums[c][:])
                for c in range(2):
                    unfold(c, squares[c], [sums[2 + c]])
                for c in range(2):
                    factor(s, c)
                for c in range(2, CHUNKS):
                    nc.gpsimd.tensor_tensor(squares[c], pages[A][0][:, columns(c)], pages[B][0][:, columns(c)], ADD)
                    square(squares[c], squares[c])
                    root(squares[c], squares[c])
                    finish(factors[s % 2][c][:], squares[c])
            for c in range(CHUNKS):
                damp_plan(nc.gpsimd, s, c)
            if 1 < s <= LAST - 2:
                held = weighed[B][(s + 1) % 2]
                for half in range(2):
                    features(s + 2, A, half, backs[half], held[:, columns(half)])
                weigh(s + 2, A, source=held[:])
            if s + 2 <= LAST:
                scatter(s + 2, A)
            if s + 3 <= LAST:
                for half in range(2):
                    features(s + 3, B, half, spare[half], unweighed[(s + 1) % 2][:, columns(half)])
                weigh(s + 3, B, source=unweighed[(s + 1) % 2][:])
            if s == 0:
                for half in range(2):
                    features(3, A, half, backs[half], third[:, columns(half)])
                weigh(3, A, source=third[:])
            if s + 3 <= LAST:
                load_plan(s + 3)
            if s == 3:
                nc.sync.dma_start(w8_w[:], w8_words.rearrange("a p n t -> p a (n t)").bitcast(I32))
                load_plane(w8_s, w8_scales.rearrange("a r n -> r a n"))
            for c in range(CHUNKS):
                if s + 1 < LAST - 1 or (c < 2) == (s + 1 < LAST):
                    turn_page(s + 1, B, c)
            if s == LAST - 2:
                for tag in ("w1_raw1", "w1_rounded"):
                    two = tile([P, 8 * BANK], BF16, f"grouped_on_{tag}", tag=tag)
                    grouped[0].extend(two[:, columns(i, 4 * BANK)] for i in range(2))
                for c in range(2):
                    weave(nc.scalar.copy, 0, c)
            if s == LAST - 1:
                for c in range(2, CHUNKS):
                    weave(nc.scalar.copy, 0, c)

        second_words = tile([P, T2], U32, "second_words")
        words = [{}, [second_words[:, columns(c)] for c in range(CHUNKS)]]
        planes = [tile([P, T2], U8, f"z_s{a}") for a in range(2)]
        staging = [gain[:, columns(i)] for gain in gains[A] + gains[B] for i in range(2)]
        late = tile([P, T2], F32, "late", tag="rows0")
        last = factors[LAST % 2]
        results = [backs + spare, sums]
        pieces = [columns(i, 256) for i in range(BANK // 256)]
        whole = columns(0)

        def within(c, cols):
            return slice(c * BANK + cols.start, c * BANK + cols.stop)

        def factor_on_vector(c, cols, gap):
            nc.vector.tensor_tensor(gap, pages[A][1][:, within(c, cols)], pages[B][1][:, within(c, cols)], ADD)
            square(roots[c][:, cols], gap)
            root(roots[c][:, cols], roots[c][:, cols])
            finish(last[c][:, cols], roots[c][:, cols])

        def squares_on_tensor(c):
            turn_page(LAST, A, c)
            squared = by_blocks(late[:, columns(c - 2)])
            square(squared, by_blocks(sums[c][:]))
            for b in range(BLOCKS):
                nc.tensor.transpose(sums[c][:, columns(b, P)], squared[:, b], ident[:])

        def factor_from_tensor(c):
            target = squares[c]
            root(target, sums[c][:])
            finish(last[c][:], target)

        def codes(a, c, cols):
            nc.vector.quantize_mx(
                out=words[a][c][:, cols].bitcast(FP8X4),
                scales=planes[a][:, within(c, cols)],
                in_=grouped[a][c][:, 4 * cols.start : 4 * cols.stop],
            )

        def products(a, c, cols):
            for n in range(BLOCKS):
                nc.tensor.matmul_mx(
                    out=results[c % 2][n][:, cols],
                    lhsT=w8_w[:, a, columns(n, P)].bitcast(FP8X4),
                    lhsT_scale=w8_s[:, a, columns(n, P)],
                    rhs=words[a][c][:, cols].bitcast(FP8X4),
                    rhs_scale=planes[a][:, within(c, cols)],
                    start=(a == 0),
                    stop=(a == 1 and cols.stop == BANK),
                )

        def first_pass(c):
            codes(0, c, whole)
            products(0, c, whole)

        def second_pass(c, parts):
            for cols in parts:
                damp_plan(nc.vector, LAST, c, cols)
                weave(nc.vector.tensor_copy, 1, c, cols)
                codes(1, c, cols)
            products(1, c, whole)

        def first_words(chunks, tag):
            held = tile([P, len(chunks) * BANK], U32, f"first_words_on_{tag}", tag=tag)
            words[0].update({c: held[:, columns(i)] for i, c in enumerate(chunks)})

        def hand_out(c):
            for n in range(BLOCKS):
                place = BLOCKS * c + n
                copy = nc.vector.tensor_copy if place in (1, 11, 13, 15) else nc.scalar.copy
                copy(staging[place], results[c % 2][n][:])
                nc.sync.dma_start(out[columns(n, P), columns(c)], staging[place])

        halves = [columns(i, HALF) for i in range(2)]
        first_gap = tile([P, HALF], F32, "first_gap", tag=f"factors0{CHUNKS - 1}")
        factor_on_vector(0, halves[0], first_gap[:])
        factor_on_vector(0, halves[1], late[:, halves[1]])
        grouped[1].extend(
            tile([P, 4 * BANK], BF16, f"grouped1{c}", tag=f"weighed{c // 2}{c % 2}")[:] for c in range(CHUNKS)
        )
        first_words((0,), "factors03")
        first_pass(0)
        factor_on_vector(1, halves[0], late[:, columns(2, HALF)])
        factor_on_vector(1, halves[1], late[:, columns(3, HALF)])
        squares_on_tensor(2)
        squares_on_tensor(3)
        first_words((2,), "page_b1")
        codes(0, 2, whole)
        second_pass(0, halves)
        first_words((1,), "roots0")
        codes(0, 1, whole)
        factor_from_tensor(2)
        hand_out(0)
        factor_from_tensor(3)
        products(0, 1, whole)
        second_pass(1, halves)
        products(0, 2, whole)
        hand_out(1)
        second_pass(2, halves)
        first_words((3,), "roots1")
        first_pass(3)
        hand_out(2)
        second_pass(3, halves)
        hand_out(3)
